import numpy as np, ml_dtypes
CORES = [2,3,42,43,82,83,122,123]
N = 8
import mx_ref
BF = ml_dtypes.bfloat16
def gentries(a):
    return np.ascontiguousarray(a.reshape(8, 16, -1).transpose(0, 2, 1)).reshape(8, -1)
def gtable(e):
    e = np.asarray(e); return np.ascontiguousarray(e.reshape(8, -1, 16).transpose(0, 2, 1)).reshape(128, -1).astype(np.int32)
def gcols(t, e):
    v = np.concatenate([t.reshape(8, 16, -1, 4), np.zeros((8, 16, 1, 4), BF)], axis=2)
    return np.ascontiguousarray(np.stack([v[g][:, e[g]] for g in range(8)])).reshape(128, -1)
def tile(rs):
    return np.stack(rs, axis=2).reshape(128, -1).astype(BF)
def pick(q, e):
    c = np.concatenate([q[0].reshape(128, -1, 4), np.zeros((128, 1, 4), np.uint8)], axis=1); s = np.concatenate([q[1], np.ones((16, 1), np.uint8)], axis=1)
    return (np.ascontiguousarray(c[:, e].reshape(128, -1)), np.ascontiguousarray(s[:, e]))
def join(*qs):
    return (np.concatenate([q[0] for q in qs], axis=1), np.concatenate([q[1] for q in qs], axis=1))
def put(q, e, v):
    c, s = q[0].reshape(128, -1, 4).copy(), q[1].copy(); c[:, e] = v[0].reshape(128, -1, 4); s[:, e] = v[1]
    return (c.reshape(128, -1), s)
def pk(c, s):
    return (np.ascontiguousarray(c), mx_ref.live(s))
def emit(q):
    return q[0], q[1]
def packed(v, rng):
    q = [mx_ref.quantize(np.ascontiguousarray(v[r])) for r in range(N)]
    return np.stack([a for a, b in q]), np.stack([mx_ref.plane(b, rng) for a, b in q])
def values_of_codes():
    e, c = np.zeros((128, 128, 4), np.float32), np.zeros((128, 2, 4), np.uint8)
    e[np.arange(128), np.arange(128), 0] = 1
    c[:127, :, 0] = np.arange(256).reshape(2, 128).T[:127]
    return mx_ref.matmul(mx_ref.quantize(e.reshape(128, 512).astype(BF)), (c.reshape(128, 8), np.full((16, 2), 127, np.uint8))).T.reshape(-1).astype(np.float64)
CODE_VALUE, SCALE_VALUE = values_of_codes(), 2.0 ** (np.arange(256) - 127.0)
def decode(q):
    return (CODE_VALUE[q[0]].reshape(16, 8, -1, 4) * SCALE_VALUE[q[1]][:, None, :, None] + 0.0).reshape(128, -1).astype(np.float32)
def f(rng, *shape):
    return mx_ref.flush((rng.standard_normal(shape, dtype=np.float32) * np.exp2(rng.integers(-2, 3, shape[:-1] + (1,)))).astype(BF))
def wide(rng, *shape, cols=0):
    v = rng.standard_normal(shape, dtype=np.float32) * np.exp2(rng.integers(-12, 13, shape)).astype(np.float32)
    if cols: v *= np.repeat(np.exp2(rng.integers(-cols, cols + 1, shape[:-2] + (1, shape[-1] // 4))) * (rng.random(shape[:-2] + (1, shape[-1] // 4)) > 0.0625), 4, axis=-1).astype(np.float32)
    return mx_ref.flush(v.astype(BF))
L, R = 256, 3
STEP = [1, 2, 4]
def contract(a, b, turn):
    turn = turn & (b >= 0)
    a, b = np.where(turn, b, a), np.where(turn, a, b)
    go, o = [int(a[L - 1])], []
    while go:
        n = go.pop()
        if n < L: o.append(n)
        else: go += [int(b[n - L]), int(a[n - L])]
    leaf = np.array(o)[1::2]
    up = np.zeros(2 * L, np.int64)
    up[b] = L + np.arange(L)
    up[a] = L + np.arange(L)
    parent = up[leaf]
    left = a[parent - L] == leaf
    add = np.full((2, 2 * L), -1)
    for i, now in enumerate((left, ~left)):
        l, p = leaf[now], parent[now]
        s = a[p - L] + b[p - L] - l
        add[i, s] = np.flatnonzero(now)
        top = up[p]
        w = a[top - L] == p
        a[top[w] - L] = s[w]
        b[top[~w] - L] = s[~w]
        up[s] = top
        a[p - L] = -1
        b[p - L] = -1
    return a, b, leaf, parent, add
def numbers_of(rng):
    return {"x": np.array(f(rng, N, 128, 8 * L)), "u": np.array(f(rng, N, 128, 512)), "v": np.array(f(rng, N, 128, 512))}
def weights(rng, w):
    c, p = packed(w, rng)
    return {"wc": c, "ws": p}
def trees(rng, kind, q=None):
    e = np.full((2, N, 8, L), -1)
    for r in range(N):
        for g in range(8):
            pool, k = rng.permutation(L).tolist(), int(kind[r, g])
            w, c = rng.random(L), rng.integers(0, 2, L)
            for i, n in enumerate(rng.permutation(L - 1).tolist()):
                j = int(w[i] * (len(pool) - 1)) if k == 0 or k == 5 and i >= L // 2 else i // 2 * 2 + 1 if k == 5 else 0
                two = pool[j:j + 2]
                if k == 4 or k == 1 and c[i] or k == 5 and q[r, g, L + n] > 0: two = two[::-1]
                pool[j:j + 2] = []
                pool.insert(len(pool) if k == 2 else j, L + n)
                e[:, r, g, n] = two
            e[0, r, g, L - 1] = pool[0]
    return {"ka": np.stack([gtable(a) for a in e[0]]), "kb": np.stack([gtable(a) for a in e[1]])}
def planted(rng, kind, q, size, unit):
    d = numbers_of(rng)
    x = d["x"].astype(np.float32).reshape(N, 8, 16, 2 * L, 4)
    x[:, :, :8] = 0
    x[:, :, 0, :, 0] = (10 - q) * 0.125 * size
    x[:, :, 1, :, 0] = (9 - q) * 0.125 * size
    u = d["u"].reshape(N, 128, 128, 4)
    u[:, :, ::16] = 0
    for h in range(0, 128, 16):
        u[:, h, h, 0] = (1.125 * unit).astype(np.float32).astype(BF)
        u[:, h + 1, h, 0] = (-1.25 * unit).astype(np.float32).astype(BF)
    w = np.array(f(rng, N, 128, 2048)).reshape(N, 128, 4, 8, 16, 4)
    w[:, :, :, :, :8] = 0
    return {"x": x.reshape(N, 128, 8 * L).astype(BF), "u": u.reshape(N, 128, 512), "v": d["v"], **trees(rng, kind, q), **weights(rng, w.reshape(N, 128, 2048))}
def setup_inputs(rng):
    return {**numbers_of(rng), **trees(rng, rng.integers(0, 3, (N, 8))), **weights(rng, f(rng, N, 128, 2048))}
def setup_inputs_near(rng):
    q = rng.integers(-1, 2, (N, 8, 2 * L))
    size = np.exp2(-1.0 * rng.integers(0, 21, (N, 8, 2 * L)))
    small = rng.permutation(N) % 2 == 0
    size[small] = 2.0 ** -30
    kind = rng.integers(0, 3, (N, 8))
    g = np.stack([rng.permutation(8) for r in range(N)])
    kind[np.arange(N), g[:, 0]] = 5
    d = planted(rng, kind, q, size, np.where(small, 2.0 ** -30, 1.0))
    x = d["x"].reshape(N, 8, 16, 2 * L, 4)
    for r in range(N):
        e = int(g[r, 1])
        x[r, e, :8] = 0
        x[r, e, 0, :, 0] = np.exp2(-12.0 - np.arange(2 * L) % 8).astype(np.float32).astype(BF)
        x[r, e, 2, :, 0] = 1.9921875
    return {**d, "x": x.reshape(N, 128, 8 * L)}
def setup_inputs_deep(rng):
    k = np.stack([rng.permutation(8) for r in range(N)])
    m = (k // 2)[:, :, None]
    q = np.where(m < 3, m - 1, rng.integers(0, 2, (N, 8, 2 * L)) * 2 - 1)
    return planted(rng, 3 + k % 2, q, np.ones((N, 8, 2 * L)), np.ones(N))
def setup_inputs_huge(rng):
    d = numbers_of(rng)
    o = rng.permutation(N)
    c = np.stack([rng.permutation(2 * L) % 2 * 2.0 - 1.0 for r in range(N)])
    c[o == 0] = 1
    c[o == 1] = -1
    x = 2.0 ** 28 * (1 + rng.random((N, 128, 2 * L, 4))) * c[:, None, :, None]
    g = np.stack([rng.permutation(8) % 2 * 2.0 - 1.0 for r in range(N)])
    u = d["u"].reshape(N, 128, 128, 4)
    u[:, :, ::16] = (2.0 ** 30 * (0.75 + 0.25 * rng.random((N, 128, 8, 4))) * g[:, None, :, None]).astype(np.float32).astype(BF)
    w = np.zeros((N, 128, 4, 128, 4), np.float32)
    i = np.arange(128)
    for b in range(4): w[:, i, b, i, b] = 2
    return {"x": x.astype(np.float32).reshape(N, 128, 8 * L).astype(BF), "u": u.reshape(N, 128, 512), "v": d["v"], **trees(rng, rng.integers(0, 3, (N, 8))), **weights(rng, w.reshape(N, 128, 2048).astype(BF))}
def setup_inputs_spread(rng):
    d = setup_inputs(rng)
    d["x"] = wide(rng, N, 128, 8 * L, cols=6)
    return d
def check_inputs(d):
    bad = []
    for k in ("x", "u", "v"):
        a = np.abs(d[k].astype(np.float32))
        if not (np.isfinite(a).all() and ((a == 0) | (a >= 2.0 ** -30) & (a <= 2.0 ** 30)).all()): bad.append("a value of " + k)
    top = 2 * L - 1
    for r in range(N):
        a, b = gentries(d["ka"][r]).astype(np.int64), gentries(d["kb"][r]).astype(np.int64)
        if (b[:, L - 1] != -1).any(): bad.append("kb: the last entry of a group isn't -1")
        k = np.concatenate([a, b[:, :L - 1]], axis=1)
        if (np.sort(k, axis=1) != np.arange(top)).any():
            bad.append("ka, kb: a node isn't a child exactly once")
            continue
        up = np.full((8, 2 * L), top)
        np.put_along_axis(up, k, np.tile(np.concatenate([L + np.arange(L), L + np.arange(L - 1)]), (8, 1)), axis=1)
        for i in range(10): up = np.take_along_axis(up, up, axis=1)
        if (up != top).any(): bad.append("ka, kb: a node isn't under the head")
    return bad
def reference(x, u, v, ka, kb, wc, ws):
    qu = [mx_ref.quantize(u[r]) for r in range(N)]
    lay = [pk(wc[r], ws[r]) for r in range(N)]
    state = [x[r] for r in range(N)]
    own = [[(gentries(ka[r])[g], gentries(kb[r])[g]) for g in range(8)] for r in range(N)]
    for t in range(R):
        sent, add = [], []
        for r in range(N):
            q = mx_ref.quantize(state[r])
            state[r] = decode(q).astype(BF)
            p = mx_ref.matmul(qu[r], q)[::16, L:]
            done = [contract(own[r][g][0], own[r][g][1], p[g] > 0) for g in range(8)]
            own[r] = [e[:2] for e in done]
            one = gcols(state[r], np.stack([e[2] for e in done])).astype(np.float32)
            two = gcols(state[r], np.stack([e[3] for e in done])).astype(np.float32)
            sent.append(mx_ref.quantize(((one + two) * np.float32(0.5)).astype(BF)))
            add.append(np.stack([e[4] for e in done]))
        for r in range(N):
            q = sent[r ^ STEP[t]]
            h = tile([np.maximum(mx_ref.matmul(pick(lay[r], np.arange(128 * b, 128 * b + 128)), q), np.float32(0.0)) * np.float32(0.03125) for b in range(4)])
            for i in range(2):
                state[r] = (state[r].astype(np.float32) + gcols(h, add[r][:, i]).astype(np.float32)).astype(BF)
    y, kid = np.zeros((N, 128, 2 * L), np.float32), np.zeros((N, 8, 2 * L), np.float32)
    oc, osc = np.zeros((N, 128, 8 * L), np.uint8), np.zeros((N, 16, 2 * L), np.uint8)
    for r in range(N):
        q = mx_ref.quantize(state[r])
        y[r] = mx_ref.matmul(mx_ref.quantize(v[r]), q)
        for g in range(8): kid[r, g] = np.concatenate(own[r][g])
        oc[r], osc[r] = emit(q)
    return {"y": y, "kid": kid, "oc": oc, "osc": osc}

@@ -1,0 +1,626 @@
+from concourse.mybir import dt, AluOpType, ActivationFunctionType
+
+A = AluOpType
+AF = ActivationFunctionType
+BIG, HUGE, MAGIC, EPS = 4096.0, 8192.0, 12582912.0, 1.0 / 2048
+WAKE, PASSES, ORDER = 0.15, 12, {}
+HS = [128, 64, 32]
+LOFF = [0, 128, 192]
+STEP = [1, 2, 4]
+CHUNK = [16, 16, 16, 16, 16, 32, 64, 128]
+BASE = [512]
+for _k in range(8):
+    BASE.append(BASE[-1] + 512 + (CHUNK[_k - 1] if _k else 0))
+VCOLS = [14, 14, 14, 14, 14, 16, 16, 18]
+
+ARENA = {"f32": [], "b16": [], "u16": [], "i32": [], "h16": []}
+PLACE = {}
+
+
+def _al(kind, **kw):
+    for n, w in kw.items():
+        lo = sum(ARENA[kind])
+        ARENA[kind].append((w + 15) // 16 * 16)
+        PLACE[n] = (kind, lo, w)
+
+
+_al("f32", IO=1024, IOC=256, COL=32, PF=16, C48=48, C48a=48, C48b=48, CONST0=512, KFR=128, MM=32, KP=32, EW=32, DW=16, XW=16, YW=16, UPD=16,
+    WD=112, WBS=112, WP=112, WS=112, TWW=16, XT=512, CH=768, SG=512, FLD0=256, FLDE=256, D0=512, SX=512, SO1=512,
+    TGX=16, BN0=256, BN1=128, BN2=64, BI=128, SO2=128, SO3=256, R3=16, F3=16, SR=512, KO=768, SV=256, SO4=256,
+    GL=256, LF=128, RF=128, KX=128, SEL=128, SELC=128, T3=384, TA=128, SO5=384, R5=32, F5=32, SO6=128,
+    SXR=512, SXP=512, SXW=48, XY=32, HL=16, MW=16, DL=32, TB1=1024, TB2=1024, ZT=512, ZZ=512, SO8=512, SOA=256, SOB=256,
+    LP1=384, LP2=192, SO9=384, PW=8, Q9=16, CSR=128, SOC=128, LC=128, FLD1=128, FLD2=64, NUM=128, NU2=128, SON=128, ALV=128, CNT=144,
+    MR=256, FW2=16, DM=16, KL=32, KK=32, KID=512)
+_al("b16", CP16=512, CP4=384, CP2=128, CPH=576, TWB=2304, WB=BASE[8] + 640, O256=256, BV1=640, BV2=576, PROD=640, SS=512,
+    SG0=512, VV=512, HIW=512, MG=256)
+_al("h16", SOH=576, SOG=512)
+_al("u16", QL=48, UL=8, KL16=32, UN=112, S0L=32, LS0=48, LS1=48, LS2=48, LS3=48, LS4=48, LS5=48, LS6=48, LS7=48, LS8=16,
+    ORDW=32, TGL=32, FL=64, OE=16, IE=8, LPP=8, L2=16, L5=96, L6=8, TL=48, BL=48, POS1=8, POS2=8, LID=8, CSL=8, NL=8, LM=48,
+    HIL=16, DLL=32, KLL=32)
+_al("i32", PI=16, J48=48, J48c=48, UI=16, KA2=32, SWI=16, SWJ=16, ZI=32, ZJ=32, EI=16, EJ=16, HI=48, SI=8, SJ=8)
+
+C4, U8 = "float8_e4m3fn_x4", "uint8"
+SCRATCH = {"f32": ("sbuf", [128, sum(ARENA["f32"])], "float32"), "b16": ("sbuf", [128, sum(ARENA["b16"])], "bfloat16"),
+           "h16": ("sbuf", [128, sum(ARENA["h16"])], "float16"), "u16": ("sbuf", [128, sum(ARENA["u16"])], "uint16"),
+           "i32": ("sbuf", [128, sum(ARENA["i32"])], "int32"), "ki": ("sbuf", [128, 32], "int32"), "yb": ("sbuf", [128, 512], "float32"),
+           "pd": ("psum", [128, 2048], "float32"), "pp": ("psum", [128, 1024], "float32")}
+for _n, _w in dict(xt=7168, ut=512, vt=512, one=528, zt=528, hz=528, vv=512, uu=512, fg=1024, ft=512).items():
+    SCRATCH[_n] = ("sbuf", [128, _w], "bfloat16")
+for _c, _s, _w in [("qx", "sx", 512), ("qe", "se", 512), ("qw", "sw", 512), ("qu", "su", 128), ("qup", "sup", 128), ("qv", "sv", 128),
+                   ("qf", "sf", 384), ("lq", "ls", 224)]:
+    SCRATCH[_c] = ("sbuf", [128, _w], C4)
+    SCRATCH[_s] = ("sbuf", [128, _w], U8)
+SEMAPHORES = ["v", "s", "p", "g", "dka", "dkb", "dx1", "dx0", "du", "dwc", "dws", "dv", "arr0", "arr1", "arr2", "snt", "outa", "outb"]
+
+
+def meets(a, b):
+    return b[0] < a[1] and a[0] < b[1] and (a[2] or b[2]) and not (a[3] == b[3] and (a[0] - b[0]) % a[3])
+
+
+def note(log, acc, tag):
+    for buf, lo, hi, w, st in acc:
+        old = log.get(buf, [])
+        if w and st == 1:
+            old = [x for x in old if not (lo <= x[0] and x[1] <= hi)]
+        log[buf] = old + [(lo, hi, w, st, tag)]
+
+
+def schedule(prog):
+    n = len(prog)
+    if (n, WAKE) in ORDER:
+        return ORDER[(n, WAKE)]
+    pred, seen = [], {}
+    for i, p in enumerate(prog):
+        pred.append({x[4] for r in p[2] for x in seen.get(r[0], []) if meets(r[1:], x)})
+        note(seen, p[2], i)
+    succ = [[] for _ in prog]
+    for i, d in enumerate(pred):
+        for j in sorted(d):
+            succ[j].append(i)
+    cost, lat = [q[6] for q in prog], [q[7] for q in prog]
+
+    def place(prio, back):
+        before, after = (succ, pred) if back else (pred, succ)
+        left = [len(d) for d in before]
+        ready = [i for i in range(n) if not left[i]]
+        at, busy, start, end = [lat[i] if back else 0.0 for i in range(n)], {}, [0.0] * n, 0.0
+        while ready:
+            i = max(ready, key=lambda i: (prio[i], -i))
+            ready.remove(i)
+            t, c, slots = at[i], cost[i], busy.setdefault(prog[i][0], [])
+            k = 0
+            while k < len(slots) and slots[k][0] < t + c:
+                t = max(t, slots[k][1])
+                k += 1
+            slots.append((t, t + c))
+            slots.sort()
+            start[i] = t
+            end = max(end, t + c + (0.0 if back else lat[i]))
+            for j in after[i]:
+                at[j] = max(at[j], t + c + lat[j if back else i] + WAKE)
+                left[j] -= 1
+                if not left[j]:
+                    ready.append(j)
+        return start, end
+    prio = [0.0] * n
+    for i in range(n - 1, -1, -1):
+        prio[i] = cost[i] + lat[i] + max([prio[j] + WAKE for j in succ[i]] + [0.0])
+    best = None
+    for _ in range(PASSES):
+        start, end = place(prio, False)
+        if best is None or end < best[0]:
+            best = (end, start)
+        rev = place([start[i] + cost[i] + lat[i] for i in range(n)], True)[0]
+        prio = [rev[i] + cost[i] for i in range(n)]
+    ORDER[(n, WAKE)] = sorted(range(n), key=lambda i: (best[1][i], i))
+    return ORDER[(n, WAKE)]
+
+
+def rank_program(g, core, T, topo):
+    rank = T.rank_of(core)
+    if rank is None:
+        return
+    Q = {"v": g.vector, "s": g.scalar, "p": g.tensor, "g": g, "y": g.sync}
+    cnt, clock, log, prog = {}, {}, {}, []
+    known = {e: {} for e in Q}
+
+    def V(name, a=None, b=None, st=1):
+        buf, lo, w = PLACE[name] if name in PLACE else (name, 0, SCRATCH[name][1][1])
+        a = 0 if a is None else a
+        b = w if b is None else b
+        assert 0 <= a < b <= w, (name, a, b, w)
+        ap = T[buf][:, lo + a:lo + b] if st == 1 else T[buf][:, lo + a:lo + b:st]
+        if buf in ("pd", "pp"):
+            return (ap, [(buf, a // 512 * 512, (b + 511) // 512 * 512, True, 1)])
+        return (ap, [(buf, lo + a, lo + b, False, st)])
+
+    def ind(w, o):
+        return (w[0].indirect(o[0]), w[1] + o[1])
+
+    def need(e, sem, c):
+        if known[e].get(sem, 0) < c:
+            Q[e].wait_ge(T.sem[sem], c)
+            known[e][sem] = c
+            for k2, v2 in clock.get((sem, c), {}).items():
+                if known[e].get(k2, 0) < v2:
+                    known[e][k2] = v2
+
+    def op(e, fn, reads, writes, sem=None, inc=1, mark=True, cost=0.1, lat=0.0):
+        acc = [r for x in reads for r in x] + [(r[0], r[1], r[2], True, r[4]) for x in writes for r in x]
+        prog.append((e, fn, acc, sem or e, inc, mark, cost, lat))
+
+    def issue(e, fn, acc, sem, inc, mark):
+        if fn is None:
+            note(log, [r for r in acc if r[3]], (sem, inc))
+            return
+        deps = {}
+        for r in acc:
+            for x in log.get(r[0], []):
+                if meets(r[1:], x):
+                    deps[x[4][0]] = max(deps.get(x[4][0], 0), x[4][1])
+        for s2 in sorted(deps, key=lambda s: s == sem):
+            need(e, s2, deps[s2])
+        ins = fn()
+        cnt[sem] = cnt.get(sem, 0) + inc
+        if mark:
+            ins.then_inc(T.sem[sem], inc)
+        clock[(sem, cnt[sem])] = dict(known[e])
+        note(log, acc, (sem, cnt[sem]))
+
+    def est(out, ins, two=False, half=True):
+        def n(x):
+            r = x[1][-1]
+            return (r[2] - r[1] + r[4] - 1) // r[4] * (16 if len(x[1]) > 1 else 1)
+        if len(out[1]) > 1:
+            return 0.05 + n(out) * 0.004
+        if any(len(x[1]) > 1 for x in ins):
+            return 0.05 + n(out) * 0.0016
+        k = 2.0 if two else 0.5 if half and all(x[1][0][0] not in ("f32", "i32", "pd", "pp", "yb", "ki") for x in ins + [out]) else 1.0
+        return 0.03 + max(64, min(n(x) for x in ins + [out]) * k) * 0.00104
+
+    def sc(x):
+        return (x[0], [x[1]]) if isinstance(x, tuple) else (x, [])
+
+    def wr(out):
+        return [out[1][:1]]
+
+    def ts(out, a, s1, o0, s2=None, o1=None):
+        (a1, r1), (a2, r2) = sc(s1), sc(s2)
+        args = (a1, None, o0) if o1 is None else (a1, a2, o0, o1)
+        op("v", lambda: g.vector.tensor_scalar(out[0], a[0], *args), [a[1]] + r1 + r2, wr(out), cost=est(out, [a]))
+
+    def tt(out, a, b, o):
+        op("v", lambda: g.vector.tensor_tensor(out[0], a[0], b[0], o), [a[1], b[1]], wr(out), cost=est(out, [a, b], True))
+
+    def cp(out, a):
+        op("v", lambda: g.vector.tensor_copy(out[0], a[0]), [a[1], out[1][1:]], wr(out), cost=est(out, [a]))
+
+    def ms(out, c):
+        op("v", lambda: g.vector.memset(out[0], c), [], wr(out), cost=est(out, []))
+
+    def scan(out, d0, d1, init, o0, o1):
+        op("v", lambda: g.vector.tensor_tensor_scan(out[0], d0[0], d1[0], init, o0, o1), [d0[1], d1[1]], wr(out), cost=est(out, [d0, d1]))
+
+    def act(out, a, scale=1.0, bias=0.0, f=AF.Identity):
+        (a1, r1), (a2, r2) = sc(scale), sc(bias)
+        kw = {} if f == AF.Copy else {"bias": a2, "scale": a1}
+        op("s", lambda: g.scalar.activation(out[0], a[0], f, **kw), [a[1]] + r1 + r2, wr(out), cost=0.03 + est(out, [a], False, False))
+
+    def iota(out, pat, base, cm, flt=False):
+        kw = {"allow_small_or_imprecise_dtypes": True} if flt else {}
+        op("g", lambda: g.iota(out[0], pat, base, cm, **kw), [], wr(out), cost=0.1 + 2 * est(out, [], False, False) if flt else 0.16)
+
+    def quant(q, s, a, b, src):
+        o1, o2 = V(q, a, b), V(s, a, b)
+        op("v", lambda: g.vector.quantize_mx(o1[0], o2[0], src[0]), [src[1]], [o1[1], o2[1]], cost=0.012 + 0.0011 * (b - a))
+
+    def mm(out, lq, ls, la, rq, rs, ra, rb):
+        x = [V(lq, la, la + 128), V(ls, la, la + 128), V(rq, ra, rb), V(rs, ra, rb)]
+        op("p", lambda: g.tensor.matmul_mx(out[0], x[0][0], x[1][0], x[2][0], x[3][0], True, True), [y[1] for y in x], wr(out), cost=0.0006 * (rb - ra + 16))
+
+    def dma(e, out, src, sem, reads, writes, lat=2.2):
+        op(e, lambda: Q[e].dma_start(out, src), reads, writes, sem=sem, inc=16, cost=0.06, lat=lat)
+
+    def wrap(out, at, data, pat, n):
+        scan(V(out, at, at + n), data, V(pat, 0, n), -(HUGE / 8 if pat == "CPH" else HUGE), A.max, A.add)
+
+    def col(j):
+        return V("COL", j, j + 1)
+
+    def pf(j):
+        return V("PF", j, j + 1)
+
+    def tw(a, n=256):
+        return V("TWB", a, a + n)
+    cP, c16, c4t, c2c, cH, cF1, cN16, cSA, cBA, cBB, cTG, cB0, cW1, c4r = 0, 3, 4, 5, 6, 7, 8, 9, 10, 11, 12, 13, 14, 17
+    NF0, F0, TW0, NF1, TW1, TW2, T2S, NF2, F2 = [256 * j for j in range(9)]
+    idw, io, iow, xw = V("WB", 0, 512), V("IO", 0, 512), V("WBS", 0, 16), V("xt", 0, 2048)
+
+    dma("y", T.ki[:, 0:16], T.ka[:], "dka", [], [V("ki", 0, 16)[1]])
+    dma("y", T.ki[:, 16:32], T.kb[:], "dkb", [], [V("ki", 16, 32)[1]])
+    dma("s", T.ut[:], T.u[:], "du", [], [V("ut")[1]])
+    dma("y", T.xt[:, 1024:2048], T.x[:, 1024:2048], "dx1", [], [V("xt", 1024, 2048)[1]], 3.0)
+    dma("y", T.xt[:, 0:1024], T.x[:, 0:1024], "dx0", [[("late", 0, 1, False, 1)]], [V("xt", 0, 1024)[1]], 3.0)
+    dma("y", T.qw[:].bitcast(dt.uint8), T.wc[:], "dwc", [[("late", 0, 1, False, 1)]], [V("qw")[1]], 3.0)
+    dma("y", T.sw[:], T.ws[:], "dws", [[("late", 0, 1, False, 1)]], [V("sw")[1]])
+    dma("y", T.vt[:], T.v[:], "dv", [[("late", 0, 1, False, 1)]], [V("vt")[1]])
+
+    iota(V("PI", 0, 1), [[1, 1]], 0, 1)
+    iota(V("J48", 0, 16), [[1, 16]], 128, -1)
+    iota(V("UI"), [[16, 16]], 0, 0)
+    iota(idw, [[1, 512]], -256, 0, True)
+    iota(V("J48", 16, 32), [[4, 16]], 131, -1)
+    iota(V("J48", 32, 48), [[8, 16]], 135, -1)
+    ms(V("one"), 1.0)
+    ms(V("TWB", 255, 2304, 256), 0.0)
+    op("g", lambda: g.affine_select(T.zt[:, 0:516], T.one[:, 0:516], [[-1, 516]], A.is_equal, 0.0, 3, 4), [V("one", 0, 516)[1]], [V("zt", 0, 516)[1]], cost=1.2)
+    iota(V("IO"), [[1, 1024]], 0, 0, True)
+    iota(V("KO"), [[0, 768]], -2048, 0, True)
+    iota(tw(NF0, 512), [[-1, 2], [0, 256]], 1, 0, True)
+    iota(V("HIW", 0, 256), [[0, 256]], 255, 0, True)
+    iota(V("hz", 0, 4), [[0, 4]], 0, 0, True)
+    iota(V("CNT", 0, 1), [[0, 1]], 0, 0, True)
+    iota(V("ALV"), [[0, 128]], 0, 0, True)
+    ts(V("PI", 3, 4), V("PI", 0, 1), 15, A.bitwise_and)
+    ts(V("J48c", 0, 16), V("J48", 0, 16), 15, A.bitwise_and)
+    ts(V("J48c", 16, 48), V("J48", 16, 48), 15, A.bitwise_and)
+    ts(V("PI", 5, 6), V("PI", 0, 1), 3, A.bitwise_and)
+    cp(V("PF", 3, 4), V("PI", 3, 4))
+    ts(V("PI", 6, 7), V("PI", 0, 1), 1, A.logical_shift_right, 3, A.bitwise_and)
+    for j, th in enumerate([1.0, 4.0, 8.0]):
+        ts(V("C48b", 16 * j, 16 * j + 16), V("J48c", 16 * j, 16 * j + 16), th, A.is_lt, BIG, A.mult)
+        ts(V("C48a", 16 * j, 16 * j + 16), V("J48c", 16 * j, 16 * j + 16), 16.0 - th, A.is_ge, -HUGE, A.mult)
+        ts(V("QL", 16 * j, 16 * j + 16), V("J48", 0, 16), 0.0, A.mult, pf(3), A.add)
+    tt(V("C48", 0, 16), V("C48a", 0, 16), V("C48b", 0, 16), A.add)
+    tt(V("C48", 16, 48), V("C48a", 16, 48), V("C48b", 16, 48), A.add)
+    ts(iow, V("UI"), pf(3), A.add)
+    for k in range(4):
+        ts(V("PI", 7 + k, 8 + k), V("PI", 0, 1), k, A.logical_shift_right, 1, A.bitwise_and)
+    cp(V("UL"), V("UI", 0, 8))
+    cp(V("PF", 5, 11), V("PI", 5, 11))
+    act(col(cH), V("C48a", 15, 16), scale=-0.125, bias=-BIG / 8)
+    act(col(c16), V("C48a", 15, 16), scale=-1.0, bias=-BIG)
+    act(col(c4r), V("C48a", 19, 20), scale=-1.0, bias=-BIG)
+    act(col(c2c), V("C48a", 33, 34), scale=-1.0, bias=-BIG)
+    act(V("CPH"), ind(V("C48", 0, 16), V("QL", 0, 36)), scale=0.125)
+    act(V("CP16", 0, 256), V("CPH", 0, 256), scale=8.0)
+    act(V("CP16", 256, 512), V("CPH", 0, 256), scale=8.0)
+    act(V("CP2"), ind(V("C48", 32, 48), V("QL", 0, 8)))
+    act(V("CP4"), ind(V("C48", 16, 32), V("QL", 0, 24)))
+    act(V("WBS", 80, 96), iow)
+    act(V("WBS", 96, 112), iow, bias=256.0)
+    act(V("WD", 80, 96), iow, scale=0.0, bias=256.0)
+    act(V("WD", 96, 112), iow, scale=0.0, bias=-256.0)
+    for k in (1, 2, 3):
+        act(col(cP + k - 1), pf(7 + k), scale=-float(BASE[k]), bias=BASE[k] + 256.0)
+        act(col(cW1 + k - 1), col(cP + k - 1), bias=col(cH))
+    act(col(cF1), pf(7), scale=-4.0, bias=4.0)
+    act(col(cSA), pf(7), scale=4.0, bias=EPS)
+    act(col(cBA), pf(7), scale=1024.0, bias=pf(6))
+    act(col(cBB), col(cBA), bias=256 * EPS)
+    act(col(cTG), col(c16), bias=-1.5)
+    act(col(cB0), col(c16), bias=-0.5)
+    act(col(cN16), col(c16), scale=-1.0)
+    act(col(c4t), col(c4r), scale=4.0, bias=pf(5))
+    act(V("CONST0", 0, 256), V("IO", 0, 256), scale=col(cSA), bias=col(cBA))
+    act(V("CONST0", 256, 512), V("IO", 0, 256), scale=col(cSA), bias=col(cBB))
+    act(V("IOC"), V("IO", 0, 256), scale=col(cF1))
+    act(V("KFR"), V("IO", 0, 128), scale=EPS, bias=256.0 + EPS)
+    act(V("PW"), V("WBS", 0, 8), scale=-2.0, bias=col(cTG))
+    for b in range(4):
+        quant("qe", "se", 128 * b, 128 * b + 128, V("zt", 3 - b, 515 - b))
+
+    op("v", lambda: g.vector.tensor_scalar(V("KA2")[0], T.ki[:], 511, None, A.bitwise_and), [V("ki")[1]], [V("KA2")[1], [("late", 0, 1, True, 1)]])
+    prog[4:8], prog[len(prog) - 4:] = [], prog[len(prog) - 4:] + prog[4:8]
+    ts(V("MM"), V("ki"), 256.0, A.is_ge)
+    cp(V("KL16"), V("KA2"))
+    cp(V("WBS", 48, 80), V("KA2"))
+    cp(ind(V("SG0"), V("KL16")), idw)
+    quant("qu", "su", 0, 128, V("ut"))
+    quant("qv", "sv", 0, 128, V("vt"))
+    act(V("sup"), ind(V("su"), V("UL")), f=AF.Copy)
+    o_ = V("UL")
+    op("v", lambda: g.vector.tensor_copy(T.qup[:, 0:128].bitcast(dt.uint32), T.qu[:, 0:128].bitcast(dt.uint32).indirect(o_[0])), [V("qu")[1], o_[1]], [V("qup")[1]], cost=0.26)
+    tt(V("KP"), V("WBS", 48, 80), V("MM"), A.mult)
+    tt(V("WD", 48, 64), V("WBS", 64, 80), V("WBS", 48, 64), A.subtract)
+    tt(V("WBS", 16, 32), V("KP", 0, 16), iow, A.max)
+    tt(V("EW", 16, 32), V("KP", 16, 32), iow, A.max)
+    tt(V("DW"), V("EW", 16, 32), V("WBS", 16, 32), A.subtract)
+    tt(V("WD", 64, 80), V("WBS", 48, 64), V("WBS", 64, 80), A.subtract)
+    tt(V("XW"), V("MM", 16, 32), V("DW"), A.mult)
+    tt(V("YW"), V("MM", 0, 16), V("DW"), A.mult)
+    tt(V("UPD"), V("DW"), V("XW"), A.subtract)
+    tt(V("WD", 0, 16), V("EW", 16, 32), iow, A.subtract)
+    tt(V("WD", 32, 48), V("UPD"), V("YW"), A.subtract)
+    tt(V("WD", 16, 32), iow, V("WBS", 16, 32), A.subtract)
+    tt(V("WBS", 32, 48), V("WBS", 16, 32), V("XW"), A.add)
+
+    def state(t):
+        quant("qx", "sx", 256, 512, V("xt", 1024, 2048))
+        mm(V("pp", 0, 256), "qup", "sup", 0, "qx", "sx", 256, 512)
+        quant("qx", "sx", 0, 256, V("xt", 0, 1024))
+        ts(tw(t, 255), V("pp", 0, 255), 0.0, A.is_gt)
+        for b in range(4):
+            mm(V("pd", 512 * b, 512 * b + 512), "qe", "se", 128 * b, "qx", "sx", 0, 512)
+            act(V("xt", b, 2048, 4), V("pd", 512 * b, 512 * b + 512), f=AF.Copy)
+
+    state(TW0)
+    wrap("SOH", 0, tw(TW0), "CPH", 256)
+    ts(V("TWW"), V("SOH", 15, 256, 16), col(cH), A.add)
+    tt(V("WP"), ind(V("TWW"), V("QL", 0, 7)), V("WD"), A.mult)
+    wrap("SOG", 0, V("SG0"), "CPH", 512)
+    tt(V("WS"), V("WP"), V("WBS"), A.add)
+    ts(V("S0L"), V("SOG", 15, 512, 16), col(cH), A.add, 256.0, A.add)
+    cp(V("UN"), V("WS"))
+    ts(V("LS0", 32, 33), pf(7), -float(BASE[0]), A.mult, BASE[0] + 511.0, A.add)
+    act(V("VV", 256, 512), ind(idw, V("UN", 16, 32)))
+    cp(V("VV", 0, 256), ind(idw, V("UN", 0, 16)))
+    act(V("WB", BASE[0] + 256, BASE[0] + 512), ind(idw, V("UN", 32, 48)))
+    ts(V("LS0", 16, 32), V("WS", 32, 48), float(BASE[0]), A.add)
+    cp(V("WB", BASE[0], BASE[0] + 256), ind(V("VV"), V("S0L", 16, 32)))
+    wrap("SOH", 0, V("WB", BASE[0], BASE[0] + 256), "CPH", 256)
+    ts(V("LS0", 0, 16), V("SOH", 15, 256, 16), col(cH), A.add, 256.0 + BASE[0], A.add)
+    for j in range(2):
+        act(V("CH", 256 * j, 256 * j + 256), ind(io, V("UN", 48 + 16 * j, 64 + 16 * j)))
+        act(V("SG", 256 * j, 256 * j + 256), V("CH", 256 * j, 256 * j + 256), bias=-255.5, f=AF.Sign)
+        act(V("XT", 256 * j, 256 * j + 256), ind(io, V("UN", 80 + 16 * j, 96 + 16 * j)))
+    for j in range(2):
+        act(V("SR", 256 * j, 256 * j + 256), ind(V("XT"), V("S0L", 16 * j, 16 * j + 16)))
+    wrap("SOA", 0, V("SR", 0, 256), "CP16", 256)
+    ts(V("TGL", 0, 16), V("SOA", 15, 256, 16), col(c16), A.add)
+    tt(V("FLD0"), ind(V("CONST0"), V("TGL", 0, 16)), V("IOC"), A.add)
+    for k in range(8):
+        nc = 32 + CHUNK[k] // 16
+        ls, nx, o, vc, oc = "LS%d" % k, "LS%d" % (k + 1), BASE[k + 1], VCOLS[k], CHUNK[k] // 16
+        win = V("WB", 0, BASE[k] + 512)
+        act(V("WB", o + 16 * vc, o + 16 * nc), ind(win, V(ls, vc, nc)))
+        cp(V("WB", o, o + 16 * vc), ind(win, V(ls, 0, vc)))
+        if 4 <= k < 7:
+            ts(V(nx, nc, nc + oc), V(ls, 32, nc), float(BASE[k + 1] - BASE[k]), A.add)
+        if k < 7:
+            wrap("SOH", 0, V("WB", o, o + 16 * nc), "CPH", 16 * nc)
+            if k < 3:
+                ts(V(nx, 32, 33), V("SOH", 527, 528), col(cW1 + k), A.add)
+                ts(V(nx, 0, 32), V("SOH", 15, 512, 16), col(cH), A.add, 256.0 + o, A.add)
+            else:
+                ts(V(nx, 0, nc), V("SOH", 15, 16 * nc, 16), col(cH), A.add, 256.0 + o, A.add)
+        else:
+            ts(V(nx, 8, 16), V(ls, 32, nc), float(BASE[8] - BASE[7]), A.add)
+            wrap("SOH", 0, V("WB", o + 512, o + 640), "CPH", 128)
+            ts(V(nx, 0, 8), V("SOH", 15, 128, 16), col(cH), A.add, 256.0 + o, A.add)
+    win = V("WB", 0, BASE[8] + 512)
+    act(V("O256", 128, 256), ind(win, V("LS8", 8, 16)))
+    cp(V("O256", 0, 128), ind(win, V("LS8", 0, 8)))
+    ts(V("ORDW", 16, 32), V("LS8"), -float(BASE[8]), A.add)
+    wrap("SOH", 0, V("O256"), "CPH", 256)
+    ts(V("ORDW", 0, 16), V("SOH", 15, 256, 16), col(cH), A.add, 256.0, A.add)
+    act(V("D0", 256, 512), ind(V("SG"), V("ORDW", 16, 32)), scale=-0.5, bias=0.5 + EPS)
+    ts(V("D0", 0, 256), ind(V("CH", 0, 512), V("ORDW", 0, 16)), 256.0, A.is_lt, EPS, A.add)
+    scan(V("SX"), V("one", 0, 512), V("D0"), 0.5, A.mult, A.add)
+    cp(ind(V("SXR"), V("ORDW")), V("SX"))
+    act(V("FLDE", 128, 256), ind(V("SXR"), V("TGL", 8, 16)))
+    cp(V("FLDE", 0, 128), ind(V("SXR"), V("TGL", 0, 8)))
+    wrap("SOB", 0, V("FLDE"), "CP16", 256)
+    ts(V("TGL", 16, 32), V("SOB", 15, 256, 16), col(cTG), A.add)
+    cp(ind(V("BN0"), V("TGL", 16, 32)), V("FLD0"))
+
+    def fold(r):
+        h, bn = HS[r], "BN%d" % r
+        u = h // 8
+        wrap("SO2", 0, V(bn, 1, 2 * h, 2), "CP2", h)
+        ts(V("FL", 0, h // 2), V("SO2", 1, h, 2), col(c2c), A.add)
+        act(V("fg", 16 * u, 32 * u), ind(xw, V("FL", u, 2 * u)), scale=0.5)
+        act(V("fg", 32 * u, 64 * u), ind(xw, V("FL", 2 * u, 4 * u)), scale=0.5)
+        ts(V("fg", 0, 16 * u), ind(xw, V("FL", 0, u)), 0.5, A.mult)
+        tt(V("ft", 0, 2 * h), V("fg", 0, 4 * h, 2), V("fg", 1, 4 * h, 2), A.add)
+        tt(V("ft", 2 * h, 4 * h), V("fg", 4 * h, 8 * h, 2), V("fg", 4 * h + 1, 8 * h, 2), A.add)
+        quant("qf", "sf", 128 * r, 128 * r + 128, V("ft"))
+        peer = T.cores[rank ^ STEP[r]]
+        rid, pid, _ = topo.addr(peer)
+        eng = topo.engines(core, peer)[:8]
+        mask = sum(1 << e for e in eng)
+        a, lo, arr = 128 * r, LOFF[r], "arr%d" % r
+        op("g", lambda: g.remote_dma(T.lq[:, lo:lo + h].bitcast(dt.uint8), T.qf[:, a:a + h].bitcast(dt.uint8), T.sem[arr], T.sem.snt, pid, rid, mask),
+           [V("qf", a, a + h)[1]], [[(arr, 0, 1, True, 1)]], sem="snt", inc=len(eng), mark=False, cost=0.3, lat=2.5)
+        op("g", lambda: g.remote_dma(T.ls[:, lo:lo + h], T.sf[:, a:a + h], T.sem[arr], T.sem.snt, pid, rid, mask),
+           [V("sf", a, a + h)[1]], [[(arr, 1, 2, True, 1)]], sem="snt", inc=len(eng), mark=False, cost=0.3, lat=2.5)
+        op("a", None, [[(arr, 0, 2, False, 1)]], [V("lq", lo, lo + h)[1], V("ls", lo, lo + h)[1]], sem=arr, inc=2 * len(topo.engines(peer, core)[:8]), cost=0.0)
+
+    def book(r):
+        h, bn = HS[r], "BN%d" % r
+        c = h // 16
+        n = 2 * c if r == 0 else c
+        wrap("SO3", 0, V(bn, 1, 2 * h, 2), "CP16", h)
+        if r == 0:
+            wrap("SO3", h, V(bn, 0, 2 * h, 2), "CP16", h)
+        if r == 1:
+            cp(ind(V("BI"), V("NL", 0, 8)), V("IO", 0, 128))
+            wrap("SO3", h, V("BI", 0, 128, 2), "CP16", h)
+            ts(V("IE", 0, c), V("SO3", h + 15, 2 * h, 16), col(c16), A.add)
+        ts(V("R3", 0, n), V("SO3", 15, 16 * n, 16), MAGIC, A.add, -MAGIC, A.add)
+        tt(V("F3", 0, n), V("SO3", 15, 16 * n, 16), V("R3", 0, n), A.subtract)
+        ts(V("SWI", 0, c), V("F3", 0, c), 2048.0, A.mult)
+        ts(V("SWJ", 0, c), V("SWI", 0, c), 255, A.bitwise_and)
+        ts(V("OE", 0, n), V("F3", 0, n), 2048.0, A.mult)
+        lsw = V("OE", 0, c)
+        act(V("SV", 0, h), ind(V("CH", 256, 768), lsw))
+        ts(V("LPP", 0, c), V("SWJ", 0, c), 256.0, A.add)
+        tt(V("SV", h, 2 * h), ind(V("SR"), V("LPP", 0, c)), V("KFR", 0, h), A.add)
+        cp(ind(V("KO", 0, 512), V("LPP", 0, c)), V("SV", h, 2 * h))
+        act(V("RF", 0, h), ind(tw([NF0, NF1, NF2][r], 512), lsw), scale=-1.0, bias=1.0)
+        act(V("KO", 512, 768), V("KO", 256, 512))
+        act(V("LF", 0, h), V("RF", 0, h), scale=-1.0, bias=1.0)
+        act(V("T3", 0, h), V("SV", 0, h))
+        wrap("SO4", 0, V("SV", 0, 2 * h), "CP16", 2 * h)
+        ts(V("L2", 0, 2 * c), V("SO4", 15, 2 * h, 16), col(c16), A.add)
+        act(V("GL", 0, 2 * h), ind(V("KO"), V("L2", 0, 2 * c)), bias=1024.0)
+        gl, gr = V("GL", 0, h), V("GL", h, 2 * h)
+        tt(V("TA", 0, h), gl, V("RF", 0, h), A.mult)
+        tt(V("T3", 2 * h, 3 * h), gr, V("LF", 0, h), A.mult)
+        tt(V("T3", h, 2 * h), V("TA", 0, h), V("SV", 0, h), A.max)
+        tt(V("KX", 0, h), gl, gr, A.max)
+        wrap("SO5", 0, V("T3", 0, 3 * h), "CP4", 3 * h)
+        tt(V("SEL", 0, h), V("KX", 0, h), V("SV", h, 2 * h), A.max)
+        ts(V("L5", 0, h // 2), V("SO5", 3, 2 * h, 4), 4.0, A.mult, col(c4t), A.add)
+        ts(V("R5", 0, h // 4), V("SO5", 2 * h + 3, 3 * h, 4), MAGIC, A.add, -MAGIC, A.add)
+        wrap("SO6", 0, V("SEL", 0, h), "CP16", h)
+        tt(V("F5", 0, h // 4), V("SO5", 2 * h + 3, 3 * h, 4), V("R5", 0, h // 4), A.subtract)
+        ts(V("SI", 0, c), V("SO6", 15, h, 16), col(c16), A.add, -256.0, A.add)
+        ts(V("L5", h // 2, 3 * h // 4), V("F5", 0, h // 4), 8192.0, A.mult, pf(5), A.add)
+        ts(V("SJ", 0, c), V("SI", 0, c), 511, A.bitwise_and)
+
+    def relink(r):
+        h = HS[r]
+        c = h // 16
+        cp(V("L6", 0, c), V("SJ", 0, c))
+        cp(ind(V("CH", 0, 512), V("L6", 0, c)), V("SV", 0, h))
+        if r < 2:
+            act(V("SELC", 0, h), ind(io, V("L6", 0, c)))
+            cp(ind(V("SR"), V("L2", 0, c)), V("SELC", 0, h))
+            act(V("CH", 512, 768), V("CH", 0, 256))
+
+    def leaves(r):
+        m = HS[r - 1]
+        c = m // 16
+        lp, e0 = "LP%d" % r, 0 if r == 1 else 40
+        if r == 1:
+            wrap("SO9", m, V(lp, m, 3 * m), "CP16", 2 * m)
+            cp(V("EI", 0, c), V("OE", c, 2 * c))
+            cp(V("TL", 0, c), V("OE", c, 2 * c))
+            tt(V("Q9", 0, c), V("SO9", m + 15, 2 * m, 16), V("PW"), A.add)
+            ts(V("POS1", 0, c), V("Q9", 0, c), 2048.0, A.mult, -1.0, A.add)
+        else:
+            wrap("SO9", 0, V(lp, 0, 3 * m), "CP16", 3 * m)
+            ts(V("EI", 0, c), V("SO9", 15, m, 16), col(c16), A.add)
+            ts(V("TL", e0, e0 + c), V("SO9", 15, m, 16), col(c16), A.add)
+            ts(V("POS2", 0, c), V("SO9", m + 15, 2 * m, 16), col(c16), A.add)
+        ts(V("LID", 0, c), V("SO9", 2 * m + 15, 3 * m, 16), col(c16), A.add)
+        act(V("LC", 0, m), V(lp, 2 * m, 3 * m), scale=col(cF1))
+        ts(V("EJ", 0, c), V("EI", 0, c), 255, A.bitwise_and)
+        act(V("CSR", 0, m), ind(V("SR"), V("LID", 0, c)))
+        wrap("SOC", 0, V("CSR", 0, m), "CP16", m)
+        cp(V("BL", e0, e0 + c), V("EJ", 0, c))
+        ts(V("CSL", 0, c), V("SOC", 15, m, 16), col(c16), A.add)
+        tt(V("FLD%d" % r), ind(V("CONST0"), V("CSL", 0, c)), V("LC", 0, m), A.add)
+
+    def update(r):
+        h = HS[r]
+        lo = LOFF[r] + h - 128
+        for b in range(4):
+            mm(V("pd", 512 * b, 512 * b + 128), "qw", "sw", 128 * b, "lq", "ls", lo, lo + 128)
+            act(V("hz", 4 + b, 4 + 4 * h, 4), V("pd", 512 * b + 128 - h, 512 * b + 128), scale=0.03125, f=AF.Relu)
+        tt(V("vv", 0, 4 * h), ind(xw, V("L5", 0, h // 4)), V("hz", 4, 4 + 4 * h), A.add)
+        tt(V("uu", 0, 4 * h), ind(V("hz", 0, 4 + 4 * h), V("L5", h // 2, 3 * h // 4)), V("vv", 0, 4 * h), A.add)
+        cp(ind(V("xt"), V("L5", h // 4, h // 2)), V("uu", 0, 4 * h))
+
+    def number(r):
+        m = HS[r - 1]
+        c = m // 16
+        state(TW1 if r == 1 else TW2)
+        t, l0, ev, lf = (TW1, 0, m, 0) if r == 1 else (T2S, 8, 0, 512)
+        if r == 2:
+            tt(tw(T2S), tw(TW2), tw(NF0), A.mult)
+        tt(V("PROD", 0, 512 + m), ind(tw(t), V("BL", l0, l0 + 32 + c)), V("BV%d" % r), A.mult)
+        scan(V("SS"), V("one", 0, 512), V("PROD", ev, ev + 512), 0.0, A.mult, A.add)
+        tt(V("NU2", 0, m), V("PROD", lf, lf + m), V("IO", 0, m), A.add)
+        tt(V("NUM", 0, m), ind(V("SS"), V("POS%d" % r, 0, c)), V("NU2", 0, m), A.add)
+        wrap("SON", 0, V("NUM", 0, m), "CP16", m)
+        ts(V("NL", 0, c), V("SON", 15, m, 16), col(c16), A.add)
+        cp(ind(V("BN%d" % r), V("NL", 0, c)), V("FLD%d" % r))
+
+    fold(0)
+    act(V("CH", 512, 768), V("CH", 0, 256))
+    act(V("ZT", 0, 256), V("SR", 256, 512))
+    act(V("ZT", 256, 512), V("SR", 256, 512), bias=512.0)
+    wrap("SO1", 0, V("SXR"), "CP16", 512)
+    ts(V("XY", 0, 16), V("WS", 48, 64), 256.0, A.is_ge, 1024.0, A.mult)
+    ts(V("XY", 16, 32), V("WS", 48, 64), 256.0, A.is_ge)
+    act(V("SXW", 0, 32), V("SO1", 15, 512, 16), bias=col(cB0))
+    tt(V("HL"), V("SXW", 0, 16), V("XY", 16, 32), A.add)
+    tt(V("TGX"), V("SXW", 0, 16), V("XY", 0, 16), A.add)
+    cp(V("HIL"), V("SXW", 16, 32))
+    ts(V("HI", 0, 16), V("HL"), 0.5, A.mult, -0.25, A.add)
+    book(0)
+    act(V("LP1", 256, 384), ind(V("CH", 0, 512), V("OE", 8, 16)))
+    relink(0)
+    act(V("SXP", 0, 256), V("SXR", 0, 256))
+    act(V("SXP", 256, 512), V("SXR", 256, 512), bias=-EPS)
+    act(V("LP1", 128, 256), ind(V("SXP"), V("OE", 8, 16)))
+    act(V("HIW", 256, 512), ind(idw, V("HIL")))
+    act(V("MG"), ind(V("HIW"), V("UN", 48, 64)))
+    act(V("ZZ"), ind(V("ZT"), V("ORDW")))
+    update(0)
+    wrap("SOH", 0, V("MG"), "CPH", 256)
+    ts(V("MW"), V("SOH", 15, 256, 16), col(cH), A.add, 256.0, A.add)
+    wrap("SO8", 0, V("ZZ"), "CP16", 512)
+    tt(V("SXW", 32, 48), V("MW"), V("TGX"), A.min)
+    ts(V("TL", 8, 40), V("SO8", 15, 512, 16), col(c16), A.add)
+    ts(V("HI", 16, 48), V("SXW", 16, 48), 0.5, A.mult, 0.25, A.add)
+    ts(V("ZI"), V("SO8", 15, 512, 16), col(c16), A.add)
+    tt(V("DL", 0, 16), V("HI", 16, 32), V("HI", 32, 48), A.subtract)
+    tt(V("DL", 16, 32), V("HI", 0, 16), V("HI", 32, 48), A.subtract)
+    ts(V("ZJ"), V("ZI"), 255, A.bitwise_and)
+    ts(V("DLL"), V("DL"), 512.0, A.add)
+    act(V("TB1", 0, 512), ind(V("IO"), V("DLL")), bias=-512.0)
+    act(V("TB1", 512, 1024), V("TB1", 0, 512), scale=-1.0)
+    cp(V("BL", 8, 40), V("ZJ"))
+    cp(V("LM"), V("HI"))
+    leaves(1)
+    act(V("BV1"), ind(V("TB1"), V("TL", 0, 40)))
+
+    number(1)
+    fold(1)
+    act(tw(NF1), tw(TW1), scale=-1.0, bias=1.0)
+    act(V("LP1", 0, 128), ind(io, V("TL", 0, 8)))
+    act(V("LP1", 128, 256), ind(io, V("POS1")))
+    book(1)
+    cp(ind(V("ALV"), V("IE", 0, 4)), V("one", 0, 64))
+    relink(1)
+    scan(V("CNT", 1, 129), V("one", 0, 128), V("ALV"), 0.0, A.mult, A.add)
+    cn = V("CNT", 0, 129)
+    act(V("MR"), ind(cn, V("LM", 32, 48)))
+    for j in range(3):
+        act(V("LP2", 64 * j, 64 * j + 64), ind(V("LP1", 128 * j, 128 * j + 128), V("IE", 0, 4)))
+    act(tw(NF0), tw(TW1), scale=-2.0, bias=1.0)
+    update(1)
+    tt(V("TB2", 0, 256), ind(cn, V("LM", 16, 32)), V("MR"), A.subtract)
+    tt(V("TB2", 256, 512), ind(cn, V("LM", 0, 16)), V("MR"), A.subtract)
+    act(V("TB2", 512, 1024), V("TB2", 0, 512), scale=-1.0)
+    leaves(2)
+    act(V("BV2"), ind(V("TB2"), V("TL", 8, 44)))
+
+    number(2)
+    fold(2)
+    tt(tw(F2), tw(TW1), tw(T2S), A.add)
+    act(tw(NF2), tw(F2), scale=-1.0, bias=1.0)
+    book(2)
+    update(2)
+
+    for j in range(2):
+        quant("qx", "sx", 256 * j, 256 * j + 256, V("xt", 1024 * j, 1024 * j + 1024))
+        mm(V("pp", 512 * j, 512 * j + 256), "qv", "sv", 0, "qx", "sx", 256 * j, 256 * j + 256)
+        dma("y", T.oc[:, 1024 * j:1024 * j + 1024], T.qx[:, 256 * j:256 * j + 256].bitcast(dt.uint8), "outa", [V("qx", 256 * j, 256 * j + 256)[1]], [], 2.5)
+        act(V("yb", 256 * j, 256 * j + 256), V("pp", 512 * j, 512 * j + 256), f=AF.Copy)
+        dma("s", T.y[:, 256 * j:256 * j + 256], T.yb[:, 256 * j:256 * j + 256], "outb", [V("yb", 256 * j, 256 * j + 256)[1]], [], 2.5)
+    for k in range(4):
+        dma("y", T.osc[4 * k:4 * k + 4, :], T.sx[32 * k:32 * k + 4, :], "outa", [V("sx")[1]], [], 1.9)
+    wrap("SOH", 0, tw(F2), "CPH", 256)
+    relink(2)
+    wrap("SO1", 0, V("KO", 256, 512), "CP16", 256)
+    ts(V("FW2"), V("SOH", 15, 256, 16), col(cH), A.add, 256.0, A.mult)
+    ts(V("DM"), V("SO1", 15, 256, 16), col(cN16), A.is_ge, 512.0, A.mult)
+    tt(V("KL", 0, 16), V("WBS", 80, 96), V("FW2"), A.add)
+    tt(V("KL", 16, 32), V("WBS", 96, 112), V("FW2"), A.subtract)
+    tt(V("KK", 0, 16), V("KL", 0, 16), V("DM"), A.max)
+    tt(V("KK", 16, 32), V("KL", 16, 32), V("DM"), A.max)
+    ms(V("CH", 511, 513), -1.0)
+    cp(V("KLL"), V("KK"))
+    act(V("KID"), ind(V("CH", 0, 513), V("KLL")))
+    klo = PLACE["KID"][1]
+    dma("y", T.kid[:], T.f32[0:128:16, klo:klo + 512], "outa", [V("KID")[1]], [], 1.9)
+
+    for i in schedule(prog):
+        issue(*prog[i][:6])
+    for s in ("v", "p", "g", "s", "outa", "outb"):
+        need("y", s, cnt[s])
+    need("g", "snt", cnt["snt"])

@@ -2,16 +2,22 @@ from concourse.mybir import dt, AluOpType, ActivationFunctionType
 
 A = AluOpType
 AF = ActivationFunctionType
-BIG, HUGE, MAGIC, EPS = 4096.0, 8192.0, 12582912.0, 1.0 / 2048
-WAKE, PASSES, ORDER = 0.15, 12, {}
+BIG, HUGE, MAGIC, EPS = 1024.0, 2048.0, 12582912.0, 1.0 / 2048
+WAKE, SOON, PASSES, ORDER = 0.22, 0.1, 8, {}
+IFIX, VFIX, SFIX, CYC, GAT, SCA, PECOL = 0.055, 0.015, 0.04, 0.00085, 0.00112, 0.0023, 0.0007
+FLIGHT = [2.0, 1.5, 1.5]
 HS = [128, 64, 32]
 LOFF = [0, 128, 192]
 STEP = [1, 2, 4]
-CHUNK = [16, 16, 16, 16, 16, 32, 64, 128]
-BASE = [512]
-for _k in range(8):
-    BASE.append(BASE[-1] + 512 + (CHUNK[_k - 1] if _k else 0))
-VCOLS = [14, 14, 14, 14, 14, 16, 16, 18]
+CH = [1, 1, 1, 1, 1, 2, 4]
+OUT, BASE = [], [512]
+for _k in range(7):
+    OUT.append(BASE[-1] + 512)
+    BASE.append(OUT[-1] + 16 * CH[_k])
+VCOLS = [12, 12, 12, 12, 12, 12, 14]
+FOLD_V, RELU_V, YB_V = [12, 6, 0], 1, 2
+ON_V = {"NF0", "NEG", "SG1", "LAM", "L768", "ABT"}
+PARTS = [4, 2, 1]
 
 ARENA = {"f32": [], "b16": [], "u16": [], "i32": [], "h16": []}
 PLACE = {}
@@ -24,27 +30,22 @@ def _al(kind, **kw):
         PLACE[n] = (kind, lo, w)
 
 
-_al("f32", IO=1024, IOC=256, COL=32, PF=16, C48=48, C48a=48, C48b=48, CONST0=512, KFR=128, MM=32, KP=32, EW=32, DW=16, XW=16, YW=16, UPD=16,
-    WD=112, WBS=112, WP=112, WS=112, TWW=16, XT=512, CH=768, SG=512, FLD0=256, FLDE=256, D0=512, SX=512, SO1=512,
-    TGX=16, BN0=256, BN1=128, BN2=64, BI=128, SO2=128, SO3=256, R3=16, F3=16, SR=512, KO=768, SV=256, SO4=256,
-    GL=256, LF=128, RF=128, KX=128, SEL=128, SELC=128, T3=384, TA=128, SO5=384, R5=32, F5=32, SO6=128,
-    SXR=512, SXP=512, SXW=48, XY=32, HL=16, MW=16, DL=32, TB1=1024, TB2=1024, ZT=512, ZZ=512, SO8=512, SOA=256, SOB=256,
-    LP1=384, LP2=192, SO9=384, PW=8, Q9=16, CSR=128, SOC=128, LC=128, FLD1=128, FLD2=64, NUM=128, NU2=128, SON=128, ALV=128, CNT=144,
-    MR=256, FW2=16, DM=16, KL=32, KK=32, KID=512)
-_al("b16", CP16=512, CP4=384, CP2=128, CPH=576, TWB=2304, WB=BASE[8] + 640, O256=256, BV1=640, BV2=576, PROD=640, SS=512,
-    SG0=512, VV=512, HIW=512, MG=256)
-_al("h16", SOH=576, SOG=512)
-_al("u16", QL=48, UL=8, KL16=32, UN=112, S0L=32, LS0=48, LS1=48, LS2=48, LS3=48, LS4=48, LS5=48, LS6=48, LS7=48, LS8=16,
-    ORDW=32, TGL=32, FL=64, OE=16, IE=8, LPP=8, L2=16, L5=96, L6=8, TL=48, BL=48, POS1=8, POS2=8, LID=8, CSL=8, NL=8, LM=48,
-    HIL=16, DLL=32, KLL=32)
-_al("i32", PI=16, J48=48, J48c=48, UI=16, KA2=32, SWI=16, SWJ=16, ZI=32, ZJ=32, EI=16, EJ=16, HI=48, SI=8, SJ=8)
+_al("f32", OX=656, RESW=1280, KIDX=1536, COL=16, MUL=8, CM=8, PF=8, C32=32, C32a=32, C32b=32, KV=128, MM=32, KP=32, YW=32, UF=32, IW=32,
+    WBS=112, WD=96, WP=96, WS=96, TWW=16, DE=512, DD=512, SX=1040, L256=32, EV=64, DL=16, LAM=8, AB=32, L768=8, KW=64, KID=512)
+_al("b16", CPH=576, CP4=256, CP8=256, CP32=256, WB=BASE[7] + 512, OC=384, SGX=656, TWB=1792, VV=512, IDM=512,
+    LW=2304, AL=512, DT=512, DT2=512, AI=512, PE=512, BN0=256, BN1=128, BN2=64, IDL=256, BV1=640, BV2=576, PROD=640, SS=512,
+    SN=256, LT1=384, LT2=192, LU=192, LP1=256, LP2=128, BLJ=64, ALV=128, CNT=144, MR=256, NUM=128)
+_al("h16", SOH=576, SOG=512, SO4=256, SOA=256, SOB=384, SOC=512, SOD=256, SOE=384, SOF=256, SOI=256, SOK=512, RH=256, CPJ=256, FLDE=256, G1=640, PA=256, PB=256)
+_al("u16", QL=36, UL=8, KL16=32, UN=96, PARL=16, S0L=32, LS0=40, LS1=40, LS2=40, LS3=40, ORDW=40, EVL=64, P4L=64, NL0=16, FL=32, JL=16, SL=16,
+    ABL=32, L1=16, L5=96, STL=8, BL=68, NL=8, AB2=32, LM=8, KLL=32)
+_al("i32", QI=48, QJ=36, J32=32, J32c=32, UI=8, SI=32, SJ=32)
 
 C4, U8 = "float8_e4m3fn_x4", "uint8"
 SCRATCH = {"f32": ("sbuf", [128, sum(ARENA["f32"])], "float32"), "b16": ("sbuf", [128, sum(ARENA["b16"])], "bfloat16"),
            "h16": ("sbuf", [128, sum(ARENA["h16"])], "float16"), "u16": ("sbuf", [128, sum(ARENA["u16"])], "uint16"),
            "i32": ("sbuf", [128, sum(ARENA["i32"])], "int32"), "ki": ("sbuf", [128, 32], "int32"), "yb": ("sbuf", [128, 512], "float32"),
            "pd": ("psum", [128, 2048], "float32"), "pp": ("psum", [128, 1024], "float32")}
-for _n, _w in dict(xt=7168, ut=512, vt=512, one=528, zt=528, hz=528, vv=512, uu=512, fg=1024, ft=512).items():
+for _n, _w in dict(xt=2560, ut=512, vt=512, one=528, zt=528, hz=512, uu=512, fg=512, ft=512, fc=1024).items():
     SCRATCH[_n] = ("sbuf", [128, _w], "bfloat16")
 for _c, _s, _w in [("qx", "sx", 512), ("qe", "se", 512), ("qw", "sw", 512), ("qu", "su", 128), ("qup", "sup", 128), ("qv", "sv", 128),
                    ("qf", "sf", 384), ("lq", "ls", 224)]:
@@ -67,8 +68,8 @@ def note(log, acc, tag):
 
 def schedule(prog):
     n = len(prog)
-    if (n, WAKE) in ORDER:
-        return ORDER[(n, WAKE)]
+    if n in ORDER:
+        return ORDER[n]
     pred, seen = [], {}
     for i, p in enumerate(prog):
         pred.append({x[4] for r in p[2] for x in seen.get(r[0], []) if meets(r[1:], x)})
@@ -77,43 +78,39 @@ def schedule(prog):
     for i, d in enumerate(pred):
         for j in sorted(d):
             succ[j].append(i)
-    cost, lat = [q[6] for q in prog], [q[7] for q in prog]
+    queue, cost, lat = [q[0] for q in prog], [q[6] for q in prog], [q[7] for q in prog]
 
     def place(prio, back):
         before, after = (succ, pred) if back else (pred, succ)
         left = [len(d) for d in before]
         ready = [i for i in range(n) if not left[i]]
-        at, busy, start, end = [lat[i] if back else 0.0 for i in range(n)], {}, [0.0] * n, 0.0
+        at, free, start, order, end = [lat[i] if back else 0.0 for i in range(n)], {}, [0.0] * n, [], 0.0
         while ready:
-            i = max(ready, key=lambda i: (prio[i], -i))
+            t, e = min((max(at[i], free.get(queue[i], 0.0)), queue[i]) for i in ready)
+            i = max((i for i in ready if queue[i] == e and at[i] <= t + SOON), key=lambda i: (prio[i], -i))
             ready.remove(i)
-            t, c, slots = at[i], cost[i], busy.setdefault(prog[i][0], [])
-            k = 0
-            while k < len(slots) and slots[k][0] < t + c:
-                t = max(t, slots[k][1])
-                k += 1
-            slots.append((t, t + c))
-            slots.sort()
-            start[i] = t
-            end = max(end, t + c + (0.0 if back else lat[i]))
+            order.append(i)
+            start[i] = t = max(t, at[i])
+            free[e] = t + cost[i]
+            end = max(end, t + cost[i] + (0.0 if back else lat[i]))
             for j in after[i]:
-                at[j] = max(at[j], t + c + lat[j if back else i] + WAKE)
+                at[j] = max(at[j], t + cost[i] + lat[j if back else i] + WAKE)
                 left[j] -= 1
                 if not left[j]:
                     ready.append(j)
-        return start, end
+        return start, end, order
     prio = [0.0] * n
     for i in range(n - 1, -1, -1):
         prio[i] = cost[i] + lat[i] + max([prio[j] + WAKE for j in succ[i]] + [0.0])
     best = None
     for _ in range(PASSES):
-        start, end = place(prio, False)
+        start, end, order = place(prio, False)
         if best is None or end < best[0]:
-            best = (end, start)
+            best = (end, order)
         rev = place([start[i] + cost[i] + lat[i] for i in range(n)], True)[0]
         prio = [rev[i] + cost[i] for i in range(n)]
-    ORDER[(n, WAKE)] = sorted(range(n), key=lambda i: (best[1][i], i))
-    return ORDER[(n, WAKE)]
+    ORDER[n] = best[1]
+    return ORDER[n]
 
 
 def rank_program(g, core, T, topo):
@@ -131,11 +128,11 @@ def rank_program(g, core, T, topo):
         assert 0 <= a < b <= w, (name, a, b, w)
         ap = T[buf][:, lo + a:lo + b] if st == 1 else T[buf][:, lo + a:lo + b:st]
         if buf in ("pd", "pp"):
-            return (ap, [(buf, a // 512 * 512, (b + 511) // 512 * 512, True, 1)])
-        return (ap, [(buf, lo + a, lo + b, False, st)])
+            return (ap, [(buf, a // 512 * 512, (b + 511) // 512 * 512, True, 1)], (b - a + st - 1) // st)
+        return (ap, [(buf, lo + a, lo + b, False, st)], (b - a + st - 1) // st)
 
     def ind(w, o):
-        return (w[0].indirect(o[0]), w[1] + o[1])
+        return (w[0].indirect(o[0]), w[1] + o[1], 16 * o[2])
 
     def need(e, sem, c):
         if known[e].get(sem, 0) < c:
@@ -167,16 +164,13 @@ def rank_program(g, core, T, topo):
         clock[(sem, cnt[sem])] = dict(known[e])
         note(log, acc, (sem, cnt[sem]))
 
-    def est(out, ins, two=False, half=True):
-        def n(x):
-            r = x[1][-1]
-            return (r[2] - r[1] + r[4] - 1) // r[4] * (16 if len(x[1]) > 1 else 1)
+    def est(out, ins, fix, two=False, half=True):
         if len(out[1]) > 1:
-            return 0.05 + n(out) * 0.004
+            return IFIX + out[2] * SCA
         if any(len(x[1]) > 1 for x in ins):
-            return 0.05 + n(out) * 0.0016
+            return IFIX + out[2] * GAT + 0.3 * (fix - VFIX)
         k = 2.0 if two else 0.5 if half and all(x[1][0][0] not in ("f32", "i32", "pd", "pp", "yb", "ki") for x in ins + [out]) else 1.0
-        return 0.03 + max(64, min(n(x) for x in ins + [out]) * k) * 0.00104
+        return fix + max(64, out[2] * k) * CYC
 
     def sc(x):
         return (x[0], [x[1]]) if isinstance(x, tuple) else (x, [])
@@ -187,233 +181,265 @@ def rank_program(g, core, T, topo):
     def ts(out, a, s1, o0, s2=None, o1=None):
         (a1, r1), (a2, r2) = sc(s1), sc(s2)
         args = (a1, None, o0) if o1 is None else (a1, a2, o0, o1)
-        op("v", lambda: g.vector.tensor_scalar(out[0], a[0], *args), [a[1]] + r1 + r2, wr(out), cost=est(out, [a]))
+        op("v", lambda: g.vector.tensor_scalar(out[0], a[0], *args), [a[1]] + r1 + r2, wr(out), cost=est(out, [a], VFIX))
 
     def tt(out, a, b, o):
-        op("v", lambda: g.vector.tensor_tensor(out[0], a[0], b[0], o), [a[1], b[1]], wr(out), cost=est(out, [a, b], True))
+        op("v", lambda: g.vector.tensor_tensor(out[0], a[0], b[0], o), [a[1], b[1]], wr(out), cost=est(out, [a, b], VFIX, True))
 
     def cp(out, a):
-        op("v", lambda: g.vector.tensor_copy(out[0], a[0]), [a[1], out[1][1:]], wr(out), cost=est(out, [a]))
+        op("v", lambda: g.vector.tensor_copy(out[0], a[0]), [a[1], out[1][1:]], wr(out), cost=est(out, [a], VFIX))
 
     def ms(out, c):
-        op("v", lambda: g.vector.memset(out[0], c), [], wr(out), cost=est(out, []))
+        op("v", lambda: g.vector.memset(out[0], c), [], wr(out), cost=est(out, [], VFIX))
 
     def scan(out, d0, d1, init, o0, o1):
-        op("v", lambda: g.vector.tensor_tensor_scan(out[0], d0[0], d1[0], init, o0, o1), [d0[1], d1[1]], wr(out), cost=est(out, [d0, d1]))
+        a1, r1 = sc(init)
+        op("v", lambda: g.vector.tensor_tensor_scan(out[0], d0[0], d1[0], a1, o0, o1), [d0[1], d1[1]] + r1, wr(out), cost=est(out, [d0, d1], VFIX))
 
     def act(out, a, scale=1.0, bias=0.0, f=AF.Identity):
         (a1, r1), (a2, r2) = sc(scale), sc(bias)
         kw = {} if f == AF.Copy else {"bias": a2, "scale": a1}
-        op("s", lambda: g.scalar.activation(out[0], a[0], f, **kw), [a[1]] + r1 + r2, wr(out), cost=0.03 + est(out, [a], False, False))
+        op("s", lambda: g.scalar.activation(out[0], a[0], f, **kw), [a[1]] + r1 + r2, wr(out), cost=est(out, [a], SFIX, False, False))
 
-    def iota(out, pat, base, cm, flt=False):
-        kw = {"allow_small_or_imprecise_dtypes": True} if flt else {}
-        op("g", lambda: g.iota(out[0], pat, base, cm, **kw), [], wr(out), cost=0.1 + 2 * est(out, [], False, False) if flt else 0.16)
+    def lin(name, out, a, scale=1.0, bias=0.0):
+        if name in ON_V:
+            ts(out, a, scale, A.mult, bias, A.add)
+        else:
+            act(out, a, scale=scale, bias=bias)
+
+    def iota(out, pat, base, cm=0):
+        kw = {"allow_small_or_imprecise_dtypes": True} if out[1][0][0] != "i32" else {}
+        op("g", lambda: g.iota(out[0], pat, base, cm, **kw), [], wr(out), cost=0.15 + 2 * CYC * out[2])
+
+    def fill(out, c):
+        iota(out, [[0, out[2]]], c)
 
     def quant(q, s, a, b, src):
         o1, o2 = V(q, a, b), V(s, a, b)
-        op("v", lambda: g.vector.quantize_mx(o1[0], o2[0], src[0]), [src[1]], [o1[1], o2[1]], cost=0.012 + 0.0011 * (b - a))
+        op("v", lambda: g.vector.quantize_mx(o1[0], o2[0], src[0]), [src[1]], [o1[1], o2[1]], cost=0.04 + 0.0009 * (b - a))
 
     def mm(out, lq, ls, la, rq, rs, ra, rb):
         x = [V(lq, la, la + 128), V(ls, la, la + 128), V(rq, ra, rb), V(rs, ra, rb)]
-        op("p", lambda: g.tensor.matmul_mx(out[0], x[0][0], x[1][0], x[2][0], x[3][0], True, True), [y[1] for y in x], wr(out), cost=0.0006 * (rb - ra + 16))
+        op("p", lambda: g.tensor.matmul_mx(out[0], x[0][0], x[1][0], x[2][0], x[3][0], True, True), [y[1] for y in x], wr(out), cost=PECOL * (rb - ra + 16))
 
-    def dma(e, out, src, sem, reads, writes, lat=2.2):
+    def dma(e, out, src, sem, reads, writes, lat=2.1):
         op(e, lambda: Q[e].dma_start(out, src), reads, writes, sem=sem, inc=16, cost=0.06, lat=lat)
 
-    def wrap(out, at, data, pat, n):
-        scan(V(out, at, at + n), data, V(pat, 0, n), -(HUGE / 8 if pat == "CPH" else HUGE), A.max, A.add)
+    def wrap(out, at, data, pat="CPH"):
+        n = data[2]
+        scan(V(out, at, at + n), data, V(pat, 0, n), -HUGE, A.max, A.add)
+
+    def ends(buf, a, n, run=16):
+        return V(buf, a + run - 1, a + n, run)
 
     def col(j):
         return V("COL", j, j + 1)
+
+    def ch(times):
+        j = [1, -1, 256, -512].index(times)
+        return V("CM", j, j + 1)
 
     def pf(j):
         return V("PF", j, j + 1)
 
     def tw(a, n=256):
         return V("TWB", a, a + n)
-    cP, c16, c4t, c2c, cH, cF1, cN16, cSA, cBA, cBB, cTG, cB0, cW1, c4r = 0, 3, 4, 5, 6, 7, 8, 9, 10, 11, 12, 13, 14, 17
-    NF0, F0, TW0, NF1, TW1, TW2, T2S, NF2, F2 = [256 * j for j in range(9)]
-    idw, io, iow, xw = V("WB", 0, 512), V("IO", 0, 512), V("WBS", 0, 16), V("xt", 0, 2048)
 
-    dma("y", T.ki[:, 0:16], T.ka[:], "dka", [], [V("ki", 0, 16)[1]])
-    dma("y", T.ki[:, 16:32], T.kb[:], "dkb", [], [V("ki", 16, 32)[1]])
-    dma("s", T.ut[:], T.u[:], "du", [], [V("ut")[1]])
-    dma("y", T.xt[:, 1024:2048], T.x[:, 1024:2048], "dx1", [], [V("xt", 1024, 2048)[1]], 3.0)
-    dma("y", T.xt[:, 0:1024], T.x[:, 0:1024], "dx0", [[("late", 0, 1, False, 1)]], [V("xt", 0, 1024)[1]], 3.0)
-    dma("y", T.qw[:].bitcast(dt.uint8), T.wc[:], "dwc", [[("late", 0, 1, False, 1)]], [V("qw")[1]], 3.0)
-    dma("y", T.sw[:], T.ws[:], "dws", [[("late", 0, 1, False, 1)]], [V("sw")[1]])
-    dma("y", T.vt[:], T.v[:], "dv", [[("late", 0, 1, False, 1)]], [V("vt")[1]])
+    def listed(out, buf, a, n, add=None, run=16):
+        ts(out, ends(buf, a, n, run), ch(1), A.add) if add is None else ts(out, ends(buf, a, n, run), ch(1), A.add, float(add), A.add)
 
-    iota(V("PI", 0, 1), [[1, 1]], 0, 1)
-    iota(V("J48", 0, 16), [[1, 16]], 128, -1)
-    iota(V("UI"), [[16, 16]], 0, 0)
-    iota(idw, [[1, 512]], -256, 0, True)
-    iota(V("J48", 16, 32), [[4, 16]], 131, -1)
-    iota(V("J48", 32, 48), [[8, 16]], 135, -1)
+    def by_fours(out, buf, a, n, c, run=4):
+        ts(out, ends(buf, a, n, run), 4.0, A.mult, col(c), A.add)
+    cH, cW1, cT, c4r, c4t, c4u = 0, 1, 4, 5, 6, 7
+    TW0, NF0, TW1, T2S, SGR, SG1, TW2 = [256 * j for j in range(7)]
+    ALM, JTL, AFL, POSL, LG, PARN = 0, 256, 512, 768, 1024, 1536
+    idw, iow, xw = V("WB", 0, 512), V("IW", 0, 16), V("xt", 0, 2048)
+    sr, oxw, res = V("SGX", 16, 528), V("OX", 16, 656), V("RESW")
+
+    def sxr(a=0, b=512):
+        return V("SX", 528 + a, 528 + b)
+
+    def kids(a, b):
+        return V("KIDX", 256 + a, 256 + b)
+
+    def lw(a, n=256):
+        return V("LW", a, a + n)
+
+    late = [[("late", 0, 1, False, 1)]]
+    dma("y", T.ki[:, 16:32], T.ka[:], "dka", [], [V("ki", 16, 32)[1]])
+    dma("s", T.ki[:, 0:16], T.kb[:], "dkb", [], [V("ki", 0, 16)[1]])
+    dma("s", T.ut[:], T.u[:], "du", [], [V("ut")[1]], 2.4)
+    dma("y", T.xt[:, 1024:2048], T.x[:, 1024:2048], "dx1", [], [V("xt", 1024, 2048)[1]], 2.8)
+    dma("y", T.xt[:, 0:1024], T.x[:, 0:1024], "dx0", late, [V("xt", 0, 1024)[1]], 2.8)
+    dma("y", T.qw[:].bitcast(dt.uint8), T.wc[:], "dwc", late, [V("qw")[1]], 2.8)
+    dma("y", T.sw[:], T.ws[:], "dws", late, [V("sw")[1]])
+    dma("y", T.vt[:], T.v[:], "dv", late, [V("vt")[1]])
+
+    iota(V("QJ"), [[0, 36]], 0, 1)
+    iota(V("J32", 0, 16), [[1, 16]], 128, -1)
+    iota(V("J32", 16, 32), [[4, 16]], 131, -1)
+    iota(V("UI"), [[16, 8]], 0)
+    iota(V("UF"), [[0, 2], [16, 16]], 0)
+    iota(V("MUL", 0, 2), [[-2, 2]], 1)
+    iota(V("MUL", 2, 4), [[-768, 2]], 256)
     ms(V("one"), 1.0)
-    ms(V("TWB", 255, 2304, 256), 0.0)
-    op("g", lambda: g.affine_select(T.zt[:, 0:516], T.one[:, 0:516], [[-1, 516]], A.is_equal, 0.0, 3, 4), [V("one", 0, 516)[1]], [V("zt", 0, 516)[1]], cost=1.2)
-    iota(V("IO"), [[1, 1024]], 0, 0, True)
-    iota(V("KO"), [[0, 768]], -2048, 0, True)
-    iota(tw(NF0, 512), [[-1, 2], [0, 256]], 1, 0, True)
-    iota(V("HIW", 0, 256), [[0, 256]], 255, 0, True)
-    iota(V("hz", 0, 4), [[0, 4]], 0, 0, True)
-    iota(V("CNT", 0, 1), [[0, 1]], 0, 0, True)
-    iota(V("ALV"), [[0, 128]], 0, 0, True)
-    ts(V("PI", 3, 4), V("PI", 0, 1), 15, A.bitwise_and)
-    ts(V("J48c", 0, 16), V("J48", 0, 16), 15, A.bitwise_and)
-    ts(V("J48c", 16, 48), V("J48", 16, 48), 15, A.bitwise_and)
-    ts(V("PI", 5, 6), V("PI", 0, 1), 3, A.bitwise_and)
-    cp(V("PF", 3, 4), V("PI", 3, 4))
-    ts(V("PI", 6, 7), V("PI", 0, 1), 1, A.logical_shift_right, 3, A.bitwise_and)
-    for j, th in enumerate([1.0, 4.0, 8.0]):
-        ts(V("C48b", 16 * j, 16 * j + 16), V("J48c", 16 * j, 16 * j + 16), th, A.is_lt, BIG, A.mult)
-        ts(V("C48a", 16 * j, 16 * j + 16), V("J48c", 16 * j, 16 * j + 16), 16.0 - th, A.is_ge, -HUGE, A.mult)
-        ts(V("QL", 16 * j, 16 * j + 16), V("J48", 0, 16), 0.0, A.mult, pf(3), A.add)
-    tt(V("C48", 0, 16), V("C48a", 0, 16), V("C48b", 0, 16), A.add)
-    tt(V("C48", 16, 48), V("C48a", 16, 48), V("C48b", 16, 48), A.add)
-    ts(iow, V("UI"), pf(3), A.add)
-    for k in range(4):
-        ts(V("PI", 7 + k, 8 + k), V("PI", 0, 1), k, A.logical_shift_right, 1, A.bitwise_and)
-    cp(V("UL"), V("UI", 0, 8))
-    cp(V("PF", 5, 11), V("PI", 5, 11))
-    act(col(cH), V("C48a", 15, 16), scale=-0.125, bias=-BIG / 8)
-    act(col(c16), V("C48a", 15, 16), scale=-1.0, bias=-BIG)
-    act(col(c4r), V("C48a", 19, 20), scale=-1.0, bias=-BIG)
-    act(col(c2c), V("C48a", 33, 34), scale=-1.0, bias=-BIG)
-    act(V("CPH"), ind(V("C48", 0, 16), V("QL", 0, 36)), scale=0.125)
-    act(V("CP16", 0, 256), V("CPH", 0, 256), scale=8.0)
-    act(V("CP16", 256, 512), V("CPH", 0, 256), scale=8.0)
-    act(V("CP2"), ind(V("C48", 32, 48), V("QL", 0, 8)))
-    act(V("CP4"), ind(V("C48", 16, 32), V("QL", 0, 24)))
-    act(V("WBS", 80, 96), iow)
-    act(V("WBS", 96, 112), iow, bias=256.0)
-    act(V("WD", 80, 96), iow, scale=0.0, bias=256.0)
-    act(V("WD", 96, 112), iow, scale=0.0, bias=-256.0)
+    scan(idw, V("one", 0, 512), V("one", 0, 512), -257.0, A.mult, A.add)
+    op("g", lambda: g.affine_select(T.zt[:, 0:516], T.one[:, 0:516], [[-1, 516]], A.is_equal, 0.0, 3, 4), [V("one", 0, 516)[1]], [V("zt", 0, 516)[1]], cost=1.1)
+    iota(V("OX", 0, 528), [[1, 528]], -16)
+    fill(V("SGX", 527, 656), -1)
+    fill(V("TWB", 255, 1792, 256), 0)
+    fill(V("WD", 48, 64), 0)
+    iota(V("IDM"), [[0, 2], [1, 256]], -256)
+    iota(V("IDL"), [[1, 256]], 0)
+    iota(V("RESW", 0, 512), [[-1, 512]], 0)
+    iota(V("RESW", 768, 1280), [[-1, 512]], 0)
+    iota(V("KV"), [[1, 128]], 512)
+    fill(V("CNT", 0, 1), 0)
+    fill(V("ALV"), 0)
+    fill(V("CP8", 0, 256, 2), 0)
+    fill(V("CP32", 0, 256, 2), 0)
+    ts(V("QI", 0, 36), V("QJ"), 15, A.bitwise_and)
+    ts(V("J32c"), V("J32"), 15, A.bitwise_and)
+    cp(V("QL"), V("QI", 0, 36))
+    for j, bits in enumerate([3, 1, 2, 4, 8]):
+        ts(V("QI", 36 + j, 37 + j), V("QJ", 0, 1), bits, A.bitwise_and)
+    cp(V("PF", 0, 6), V("QI", 35, 41))
+    for j, th in enumerate([1.0, 4.0]):
+        ts(V("C32b", 16 * j, 16 * j + 16), V("J32c", 16 * j, 16 * j + 16), th, A.is_lt, BIG, A.mult)
+        ts(V("C32a", 16 * j, 16 * j + 16), V("J32c", 16 * j, 16 * j + 16), 16.0 - th, A.is_ge, -HUGE, A.mult)
+    tt(V("C32"), V("C32a"), V("C32b"), A.add)
+    cp(V("UL"), V("UI"))
+    act(V("IW"), V("UF"), bias=pf(0))
+    act(V("WBS", 32, 48), V("UF", 0, 16), bias=pf(0))
+    act(col(cH), V("C32a", 15, 16), scale=-1.0, bias=-BIG)
+    act(V("CPH"), ind(V("C32", 0, 16), V("QL", 0, 36)))
+    act(V("CM", 0, 4), V("MUL", 0, 4), scale=col(cH))
     for k in (1, 2, 3):
-        act(col(cP + k - 1), pf(7 + k), scale=-float(BASE[k]), bias=BASE[k] + 256.0)
-        act(col(cW1 + k - 1), col(cP + k - 1), bias=col(cH))
-    act(col(cF1), pf(7), scale=-4.0, bias=4.0)
-    act(col(cSA), pf(7), scale=4.0, bias=EPS)
-    act(col(cBA), pf(7), scale=1024.0, bias=pf(6))
-    act(col(cBB), col(cBA), bias=256 * EPS)
-    act(col(cTG), col(c16), bias=-1.5)
-    act(col(cB0), col(c16), bias=-0.5)
-    act(col(cN16), col(c16), scale=-1.0)
-    act(col(c4t), col(c4r), scale=4.0, bias=pf(5))
-    act(V("CONST0", 0, 256), V("IO", 0, 256), scale=col(cSA), bias=col(cBA))
-    act(V("CONST0", 256, 512), V("IO", 0, 256), scale=col(cSA), bias=col(cBB))
-    act(V("IOC"), V("IO", 0, 256), scale=col(cF1))
-    act(V("KFR"), V("IO", 0, 128), scale=EPS, bias=256.0 + EPS)
-    act(V("PW"), V("WBS", 0, 8), scale=-2.0, bias=col(cTG))
+        act(col(cW1 + k - 1), pf(2 + k), scale=BASE[k] / (1 << k), bias=col(cH))
+    act(col(cT), col(cH), bias=512.0)
+    act(col(c4r), V("C32a", 19, 20), scale=-1.0, bias=-BIG)
+    act(col(c4t), col(c4r), scale=4.0, bias=pf(1))
+    act(col(c4u), col(c4t), bias=1024.0)
+    act(V("CP4"), ind(V("C32", 16, 32), V("QL", 0, 16)))
+    lin("CP", V("CP8", 1, 256, 2), V("CP4", 0, 128))
+    lin("CP", V("CP32", 1, 256, 2), V("CPH", 0, 128))
+    lin("CPJ", V("CPJ"), V("CPH", 0, 256))
+    tt(V("CPJ", 15, 256, 16), V("CPH", 15, 256, 16), iow, A.add)
+    ts(V("LS0", 0, 1), pf(2), float(BASE[0]), A.mult, 511.0, A.add)
     for b in range(4):
         quant("qe", "se", 128 * b, 128 * b + 128, V("zt", 3 - b, 515 - b))
 
-    op("v", lambda: g.vector.tensor_scalar(V("KA2")[0], T.ki[:], 511, None, A.bitwise_and), [V("ki")[1]], [V("KA2")[1], [("late", 0, 1, True, 1)]])
+    o_ = V("KL16")
+    op("v", lambda: g.vector.tensor_scalar(o_[0], T.ki[:], 16.0, None, A.add), [V("ki")[1]], [o_[1], [("late", 0, 1, True, 1)]], cost=0.13)
     prog[4:8], prog[len(prog) - 4:] = [], prog[len(prog) - 4:] + prog[4:8]
-    ts(V("MM"), V("ki"), 256.0, A.is_ge)
-    cp(V("KL16"), V("KA2"))
-    cp(V("WBS", 48, 80), V("KA2"))
-    cp(ind(V("SG0"), V("KL16")), idw)
+    cp(ind(V("SGX"), V("KL16")), idw)
+    act(kids(0, 512), ind(V("OX", 0, 528), V("KL16")))
+    lin("KIDD", kids(512, 768), kids(0, 256))
     quant("qu", "su", 0, 128, V("ut"))
     quant("qv", "sv", 0, 128, V("vt"))
     act(V("sup"), ind(V("su"), V("UL")), f=AF.Copy)
-    o_ = V("UL")
-    op("v", lambda: g.vector.tensor_copy(T.qup[:, 0:128].bitcast(dt.uint32), T.qu[:, 0:128].bitcast(dt.uint32).indirect(o_[0])), [V("qu")[1], o_[1]], [V("qup")[1]], cost=0.26)
-    tt(V("KP"), V("WBS", 48, 80), V("MM"), A.mult)
-    tt(V("WD", 48, 64), V("WBS", 64, 80), V("WBS", 48, 64), A.subtract)
-    tt(V("WBS", 16, 32), V("KP", 0, 16), iow, A.max)
-    tt(V("EW", 16, 32), V("KP", 16, 32), iow, A.max)
-    tt(V("DW"), V("EW", 16, 32), V("WBS", 16, 32), A.subtract)
-    tt(V("WD", 64, 80), V("WBS", 48, 64), V("WBS", 64, 80), A.subtract)
-    tt(V("XW"), V("MM", 16, 32), V("DW"), A.mult)
-    tt(V("YW"), V("MM", 0, 16), V("DW"), A.mult)
-    tt(V("UPD"), V("DW"), V("XW"), A.subtract)
-    tt(V("WD", 0, 16), V("EW", 16, 32), iow, A.subtract)
-    tt(V("WD", 32, 48), V("UPD"), V("YW"), A.subtract)
-    tt(V("WD", 16, 32), iow, V("WBS", 16, 32), A.subtract)
-    tt(V("WBS", 32, 48), V("WBS", 16, 32), V("XW"), A.add)
+    u_ = V("UL")
+    op("v", lambda: g.vector.tensor_copy(T.qup[:, 0:128].bitcast(dt.uint32), T.qu[:, 0:128].bitcast(dt.uint32).indirect(u_[0])), [V("qu")[1], u_[1]], [V("qup")[1]], cost=0.24)
+    nb, na, eb, ea = V("WBS", 80, 96), V("WBS", 96, 112), V("WBS", 48, 64), V("WBS", 64, 80)
+    ts(V("MM"), V("ki"), 256.0, A.is_ge)
+    ts(V("WBS", 80, 112), V("ki"), 256.0, A.is_lt)
+    tt(V("KP"), V("ki"), V("MM"), A.mult)
+    tt(V("WBS", 48, 80), V("KP"), V("IW"), A.max)
+    tt(V("YW", 0, 16), nb, ea, A.mult)
+    tt(V("YW", 16, 32), na, eb, A.mult)
+    tt(V("WBS", 0, 32), V("KP"), V("YW"), A.add)
+    tt(V("WD", 0, 16), V("WBS", 0, 16), V("WBS", 16, 32), A.subtract)
+    tt(V("WD", 16, 32), ea, iow, A.subtract)
+    tt(V("WD", 32, 48), iow, eb, A.subtract)
+    tt(V("WD", 64, 80), na, nb, A.subtract)
+    tt(V("WD", 80, 96), nb, na, A.subtract)
 
-    def state(t):
+    def state(bits, *how):
         quant("qx", "sx", 256, 512, V("xt", 1024, 2048))
         mm(V("pp", 0, 256), "qup", "sup", 0, "qx", "sx", 256, 512)
         quant("qx", "sx", 0, 256, V("xt", 0, 1024))
-        ts(tw(t, 255), V("pp", 0, 255), 0.0, A.is_gt)
+        ts(bits, V("pp", 0, 255), 0.0, *how)
         for b in range(4):
             mm(V("pd", 512 * b, 512 * b + 512), "qe", "se", 128 * b, "qx", "sx", 0, 512)
             act(V("xt", b, 2048, 4), V("pd", 512 * b, 512 * b + 512), f=AF.Copy)
 
-    state(TW0)
-    wrap("SOH", 0, tw(TW0), "CPH", 256)
-    ts(V("TWW"), V("SOH", 15, 256, 16), col(cH), A.add)
-    tt(V("WP"), ind(V("TWW"), V("QL", 0, 7)), V("WD"), A.mult)
-    wrap("SOG", 0, V("SG0"), "CPH", 512)
-    tt(V("WS"), V("WP"), V("WBS"), A.add)
-    ts(V("S0L"), V("SOG", 15, 512, 16), col(cH), A.add, 256.0, A.add)
+    state(tw(TW0, 255), A.is_gt)
+    wrap("SOH", 0, tw(TW0))
+    listed(V("TWW"), "SOH", 0, 256)
+    tt(V("WP"), ind(V("TWW"), V("QL", 0, 6)), V("WD"), A.mult)
+    wrap("SOG", 0, sr)
+    tt(V("WS"), V("WP"), V("WBS", 16, 112), A.add)
+    listed(V("S0L"), "SOG", 0, 512, 256)
     cp(V("UN"), V("WS"))
-    ts(V("LS0", 32, 33), pf(7), -float(BASE[0]), A.mult, BASE[0] + 511.0, A.add)
-    act(V("VV", 256, 512), ind(idw, V("UN", 16, 32)))
-    cp(V("VV", 0, 256), ind(idw, V("UN", 0, 16)))
-    act(V("WB", BASE[0] + 256, BASE[0] + 512), ind(idw, V("UN", 32, 48)))
-    ts(V("LS0", 16, 32), V("WS", 32, 48), float(BASE[0]), A.add)
+    act(V("VV", 256, 512), ind(idw, V("UN", 32, 48)))
+    cp(V("VV", 0, 256), ind(idw, V("UN", 16, 32)))
+    act(V("WB", BASE[0] + 256, BASE[0] + 512), ind(idw, V("UN", 0, 16)))
+    ts(V("LS0", 17, 33), V("WS", 0, 16), float(BASE[0]), A.add)
     cp(V("WB", BASE[0], BASE[0] + 256), ind(V("VV"), V("S0L", 16, 32)))
-    wrap("SOH", 0, V("WB", BASE[0], BASE[0] + 256), "CPH", 256)
-    ts(V("LS0", 0, 16), V("SOH", 15, 256, 16), col(cH), A.add, 256.0 + BASE[0], A.add)
-    for j in range(2):
-        act(V("CH", 256 * j, 256 * j + 256), ind(io, V("UN", 48 + 16 * j, 64 + 16 * j)))
-        act(V("SG", 256 * j, 256 * j + 256), V("CH", 256 * j, 256 * j + 256), bias=-255.5, f=AF.Sign)
-        act(V("XT", 256 * j, 256 * j + 256), ind(io, V("UN", 80 + 16 * j, 96 + 16 * j)))
-    for j in range(2):
-        act(V("SR", 256 * j, 256 * j + 256), ind(V("XT"), V("S0L", 16 * j, 16 * j + 16)))
-    wrap("SOA", 0, V("SR", 0, 256), "CP16", 256)
-    ts(V("TGL", 0, 16), V("SOA", 15, 256, 16), col(c16), A.add)
-    tt(V("FLD0"), ind(V("CONST0"), V("TGL", 0, 16)), V("IOC"), A.add)
-    for k in range(8):
-        nc = 32 + CHUNK[k] // 16
-        ls, nx, o, vc, oc = "LS%d" % k, "LS%d" % (k + 1), BASE[k + 1], VCOLS[k], CHUNK[k] // 16
-        win = V("WB", 0, BASE[k] + 512)
-        act(V("WB", o + 16 * vc, o + 16 * nc), ind(win, V(ls, vc, nc)))
-        cp(V("WB", o, o + 16 * vc), ind(win, V(ls, 0, vc)))
-        if 4 <= k < 7:
-            ts(V(nx, nc, nc + oc), V(ls, 32, nc), float(BASE[k + 1] - BASE[k]), A.add)
-        if k < 7:
-            wrap("SOH", 0, V("WB", o, o + 16 * nc), "CPH", 16 * nc)
-            if k < 3:
-                ts(V(nx, 32, 33), V("SOH", 527, 528), col(cW1 + k), A.add)
-                ts(V(nx, 0, 32), V("SOH", 15, 512, 16), col(cH), A.add, 256.0 + o, A.add)
-            else:
-                ts(V(nx, 0, nc), V("SOH", 15, 16 * nc, 16), col(cH), A.add, 256.0 + o, A.add)
-        else:
-            ts(V(nx, 8, 16), V(ls, 32, nc), float(BASE[8] - BASE[7]), A.add)
-            wrap("SOH", 0, V("WB", o + 512, o + 640), "CPH", 128)
-            ts(V(nx, 0, 8), V("SOH", 15, 128, 16), col(cH), A.add, 256.0 + o, A.add)
-    win = V("WB", 0, BASE[8] + 512)
-    act(V("O256", 128, 256), ind(win, V("LS8", 8, 16)))
-    cp(V("O256", 0, 128), ind(win, V("LS8", 0, 8)))
-    ts(V("ORDW", 16, 32), V("LS8"), -float(BASE[8]), A.add)
-    wrap("SOH", 0, V("O256"), "CPH", 256)
-    ts(V("ORDW", 0, 16), V("SOH", 15, 256, 16), col(cH), A.add, 256.0, A.add)
-    act(V("D0", 256, 512), ind(V("SG"), V("ORDW", 16, 32)), scale=-0.5, bias=0.5 + EPS)
-    ts(V("D0", 0, 256), ind(V("CH", 0, 512), V("ORDW", 0, 16)), 256.0, A.is_lt, EPS, A.add)
-    scan(V("SX"), V("one", 0, 512), V("D0"), 0.5, A.mult, A.add)
-    cp(ind(V("SXR"), V("ORDW")), V("SX"))
-    act(V("FLDE", 128, 256), ind(V("SXR"), V("TGL", 8, 16)))
-    cp(V("FLDE", 0, 128), ind(V("SXR"), V("TGL", 0, 8)))
-    wrap("SOB", 0, V("FLDE"), "CP16", 256)
-    ts(V("TGL", 16, 32), V("SOB", 15, 256, 16), col(cTG), A.add)
-    cp(ind(V("BN0"), V("TGL", 16, 32)), V("FLD0"))
+    wrap("SOH", 0, V("WB", BASE[0], BASE[0] + 256))
+    listed(V("LS0", 1, 17), "SOH", 0, 256, 256 + BASE[0])
+    lin("NF0", tw(NF0), tw(TW0), -1.0, 1.0)
+    act(lw(LG, 512), ind(tw(TW0, 512), V("S0L")))
+    act(lw(PARN, 512), ind(V("IDM"), V("S0L")))
+    listed(V("SI"), "SOG", 0, 512, 256)
+    ts(V("SJ"), V("SI"), 255, A.bitwise_and)
+    wrap("SO4", 0, lw(PARN), "CP4")
+    by_fours(V("P4L"), "SO4", 0, 256, c4u)
+    wrap("SOC", 0, lw(LG, 512))
+    lin("L256", V("L256"), ends("SOC", 0, 512), 256.0, ch(256))
+    tt(V("EV", 0, 16), V("SJ", 0, 16), V("L256", 0, 16), A.add)
+    tt(V("EV", 16, 48), V("SJ"), V("L256"), A.subtract)
+    tt(V("EV", 48, 64), iow, V("L256", 16, 32), A.subtract)
+    ts(V("EVL"), V("EV"), 256.0, A.add)
+    act(V("DE"), ind(V("IDL"), V("UN", 64, 96)), bias=EPS)
 
-    def fold(r):
-        h, bn = HS[r], "BN%d" % r
-        u = h // 8
-        wrap("SO2", 0, V(bn, 1, 2 * h, 2), "CP2", h)
-        ts(V("FL", 0, h // 2), V("SO2", 1, h, 2), col(c2c), A.add)
-        act(V("fg", 16 * u, 32 * u), ind(xw, V("FL", u, 2 * u)), scale=0.5)
-        act(V("fg", 32 * u, 64 * u), ind(xw, V("FL", 2 * u, 4 * u)), scale=0.5)
-        ts(V("fg", 0, 16 * u), ind(xw, V("FL", 0, u)), 0.5, A.mult)
-        tt(V("ft", 0, 2 * h), V("fg", 0, 4 * h, 2), V("fg", 1, 4 * h, 2), A.add)
-        tt(V("ft", 2 * h, 4 * h), V("fg", 4 * h, 8 * h, 2), V("fg", 4 * h + 1, 8 * h, 2), A.add)
+    def folds(r):
+        n = 8 * HS[r]
+        w = n // PARTS[r]
+        for a in range(0, n, w):
+            leaf, at = V("xt", a, a + w), 0
+            if r:
+                leaf, at = V("fg", a, a + w), n // 16
+                act(leaf, ind(V("xt", 0, 1024), V("P4L", a // 16, (a + w) // 16)))
+            tt(V("fc", a, a + w), ind(V("xt", 1024, 2048), V("P4L", at + a // 16, at + (a + w) // 16)), leaf, A.add)
+    folds(0)
+    for k in range(7):
+        c, o, vc = CH[k], OUT[k], VCOLS[k]
+        nc, ls = 32 + c, "LS%d" % k if k < 4 else "ORDW"
+        win = V("WB", 0 if k < 4 else BASE[k], BASE[k] + 512)
+        act(V("WB", o + 16 * vc, o + 16 * nc), ind(win, V(ls, vc, nc)))
+        if vc:
+            cp(V("WB", o, o + 16 * vc), ind(win, V(ls, 0, vc)))
+        n = 16 * nc if k < 6 else 64
+        wrap("SOH", 0, V("WB", o, o + n))
+        if k < 3:
+            ts(V("LS%d" % (k + 1), 0, 1), V("SOH", 15, 16), col(cW1 + k), A.add, 256.0, A.add)
+            listed(V("LS%d" % (k + 1), 1, 33), "SOH", 16, 512, 256 + BASE[k + 1])
+        else:
+            at = c if k > 3 else 0
+            listed(V("ORDW", at, at + n // 16), "SOH", 0, n, 256)
+    for c in range(4):
+        if c < 3:
+            act(V("OC", 128 * c, 128 * c + 128), ind(V("WB", BASE[7], BASE[7] + 512), V("ORDW", 8 * c, 8 * c + 8)))
+            wrap("SOH", 128 * c + 64, V("OC", 128 * c, 128 * c + 128))
+            listed(V("ORDW", 8 * c + 8, 8 * c + 16), "SOH", 128 * c + 64, 128, 256)
+        act(V("DD", 128 * c, 128 * c + 128), ind(V("DE"), V("ORDW", 8 * c, 8 * c + 8)))
+        scan(V("SX", 16 + 128 * c, 144 + 128 * c), V("one", 0, 128), V("DD", 128 * c, 128 * c + 128), V("SX", 15 + 128 * c, 16 + 128 * c) if c else -EPS, A.mult, A.add)
+        cp(ind(sxr(), V("ORDW", 8 * c, 8 * c + 8)), V("SX", 16 + 128 * c, 144 + 128 * c))
+    ordw = V("ORDW", 0, 32)
+    act(V("FLDE", 128, 256), ind(sxr(-256), V("EVL", 8, 16)))
+    cp(V("FLDE", 0, 128), ind(sxr(-256), V("EVL", 0, 8)))
+    wrap("SOB", 0, V("FLDE"))
+    listed(V("NL0"), "SOB", 0, 256, -1.25)
+    cp(ind(V("BN0"), V("NL0")), V("IDL"))
+
+    def send(r):
+        h, u = HS[r], FOLD_V[r]
+        wrap("SO4", 0, V("BN%d" % r, 1, 2 * h, 2), "CP4")
+        by_fours(V("FL", 0, h // 4), "SO4", 0, h, c4t)
+        act(V("ft", 16 * u, 4 * h), ind(V("fc", 0, 8 * h), V("FL", u, h // 4)), scale=0.5)
+        if u:
+            ts(V("ft", 0, 16 * u), ind(V("fc", 0, 8 * h), V("FL", 0, u)), 0.5, A.mult)
         quant("qf", "sf", 128 * r, 128 * r + 128, V("ft"))
         peer = T.cores[rank ^ STEP[r]]
         rid, pid, _ = topo.addr(peer)
@@ -421,178 +447,169 @@ def rank_program(g, core, T, topo):
         mask = sum(1 << e for e in eng)
         a, lo, arr = 128 * r, LOFF[r], "arr%d" % r
         op("g", lambda: g.remote_dma(T.lq[:, lo:lo + h].bitcast(dt.uint8), T.qf[:, a:a + h].bitcast(dt.uint8), T.sem[arr], T.sem.snt, pid, rid, mask),
-           [V("qf", a, a + h)[1]], [[(arr, 0, 1, True, 1)]], sem="snt", inc=len(eng), mark=False, cost=0.3, lat=2.5)
+           [V("qf", a, a + h)[1]], [[(arr, 0, 1, True, 1)]], sem="snt", inc=len(eng), mark=False, cost=0.2, lat=FLIGHT[r])
         op("g", lambda: g.remote_dma(T.ls[:, lo:lo + h], T.sf[:, a:a + h], T.sem[arr], T.sem.snt, pid, rid, mask),
-           [V("sf", a, a + h)[1]], [[(arr, 1, 2, True, 1)]], sem="snt", inc=len(eng), mark=False, cost=0.3, lat=2.5)
+           [V("sf", a, a + h)[1]], [[(arr, 1, 2, True, 1)]], sem="snt", inc=len(eng), mark=False, cost=0.2, lat=FLIGHT[r])
         op("a", None, [[(arr, 0, 2, False, 1)]], [V("lq", lo, lo + h)[1], V("ls", lo, lo + h)[1]], sem=arr, inc=2 * len(topo.engines(peer, core)[:8]), cost=0.0)
 
     def book(r):
         h, bn = HS[r], "BN%d" % r
         c = h // 16
-        n = 2 * c if r == 0 else c
-        wrap("SO3", 0, V(bn, 1, 2 * h, 2), "CP16", h)
+        wrap("SOA", 0, V(bn, 1, 2 * h, 2))
+        if r < 2:
+            wrap("SOA", h, V(bn, 0, 2 * h, 2))
+        listed(V("JL", 0, c if r == 2 else 2 * c), "SOA", 0, h if r == 2 else 2 * h)
+        odd = V("JL", 0, c)
+        act(V("SN", 0, h), ind([sr, V("LT1", 128, 256), V("LT2", 64, 128)][r], odd))
         if r == 0:
-            wrap("SO3", h, V(bn, 0, 2 * h, 2), "CP16", h)
+            act(V("SN", h, 2 * h), ind(lw(PARN), odd))
+        else:
+            act(V("SN", h, 2 * h), ind(V("LP%d" % r, 2 * h, 4 * h), odd), bias=-256.0)
         if r == 1:
-            cp(ind(V("BI"), V("NL", 0, 8)), V("IO", 0, 128))
-            wrap("SO3", h, V("BI", 0, 128, 2), "CP16", h)
-            ts(V("IE", 0, c), V("SO3", h + 15, 2 * h, 16), col(c16), A.add)
-        ts(V("R3", 0, n), V("SO3", 15, 16 * n, 16), MAGIC, A.add, -MAGIC, A.add)
-        tt(V("F3", 0, n), V("SO3", 15, 16 * n, 16), V("R3", 0, n), A.subtract)
-        ts(V("SWI", 0, c), V("F3", 0, c), 2048.0, A.mult)
-        ts(V("SWJ", 0, c), V("SWI", 0, c), 255, A.bitwise_and)
-        ts(V("OE", 0, n), V("F3", 0, n), 2048.0, A.mult)
-        lsw = V("OE", 0, c)
-        act(V("SV", 0, h), ind(V("CH", 256, 768), lsw))
-        ts(V("LPP", 0, c), V("SWJ", 0, c), 256.0, A.add)
-        tt(V("SV", h, 2 * h), ind(V("SR"), V("LPP", 0, c)), V("KFR", 0, h), A.add)
-        cp(ind(V("KO", 0, 512), V("LPP", 0, c)), V("SV", h, 2 * h))
-        act(V("RF", 0, h), ind(tw([NF0, NF1, NF2][r], 512), lsw), scale=-1.0, bias=1.0)
-        act(V("KO", 512, 768), V("KO", 256, 512))
-        act(V("LF", 0, h), V("RF", 0, h), scale=-1.0, bias=1.0)
-        act(V("T3", 0, h), V("SV", 0, h))
-        wrap("SO4", 0, V("SV", 0, 2 * h), "CP16", 2 * h)
-        ts(V("L2", 0, 2 * c), V("SO4", 15, 2 * h, 16), col(c16), A.add)
-        act(V("GL", 0, 2 * h), ind(V("KO"), V("L2", 0, 2 * c)), bias=1024.0)
-        gl, gr = V("GL", 0, h), V("GL", h, 2 * h)
-        tt(V("TA", 0, h), gl, V("RF", 0, h), A.mult)
-        tt(V("T3", 2 * h, 3 * h), gr, V("LF", 0, h), A.mult)
-        tt(V("T3", h, 2 * h), V("TA", 0, h), V("SV", 0, h), A.max)
-        tt(V("KX", 0, h), gl, gr, A.max)
-        wrap("SO5", 0, V("T3", 0, 3 * h), "CP4", 3 * h)
-        tt(V("SEL", 0, h), V("KX", 0, h), V("SV", h, 2 * h), A.max)
-        ts(V("L5", 0, h // 2), V("SO5", 3, 2 * h, 4), 4.0, A.mult, col(c4t), A.add)
-        ts(V("R5", 0, h // 4), V("SO5", 2 * h + 3, 3 * h, 4), MAGIC, A.add, -MAGIC, A.add)
-        wrap("SO6", 0, V("SEL", 0, h), "CP16", h)
-        tt(V("F5", 0, h // 4), V("SO5", 2 * h + 3, 3 * h, 4), V("R5", 0, h // 4), A.subtract)
-        ts(V("SI", 0, c), V("SO6", 15, h, 16), col(c16), A.add, -256.0, A.add)
-        ts(V("L5", h // 2, 3 * h // 4), V("F5", 0, h // 4), 8192.0, A.mult, pf(5), A.add)
-        ts(V("SJ", 0, c), V("SI", 0, c), 511, A.bitwise_and)
+            act(V("SN", 2 * h, 3 * h), ind(V("LP1", 0, 128), V("JL", c, 2 * c)), bias=-256.0)
+        n = 3 * c if r == 1 else 2 * c
+        wrap("SOD", 0, V("SN", 0, 16 * n))
+        listed(V("SL", 0, n), "SOD", 0, 16 * n, 256)
+        sl, nl, o = V("SL", 0, c), V("SL", c, 2 * c), (2 + r) * h
+        cp(ind(V("RESW", 256, 512), nl), V("KV", 0, h))
+        act(V("G1", o, o + h), ind(kids(256, 768), sl))
+        act(V("G1", 0, h), ind(V("SGX", 272, 528), nl))
+        act(V("G1", h, 2 * h), ind(tw(TW0, 512), sl))
+        for j in range(r):
+            act(V("G1", (2 + j) * h, (3 + j) * h), ind(tw([TW1, T2S][j]), nl))
+        lin("OV", V("OX", 528, 528 + h), V("G1", o, o + h))
+        lin("RESD", V("RESW", 512, 768), V("RESW", 256, 512))
+        wrap("SOB", 0, V("G1", 0, o + h))
+        side, shift = ends("SOB", h, h), [1, None, -1][r]
+        for j in range(r):
+            tt(V("DL", 8 * j, 8 * j + c), side, ends("SOB", (2 + j) * h, h), A.subtract)
+            side = V("DL", 8 * j, 8 * j + c)
+        if r == 0:
+            lin("LAM", V("LAM", 0, c), side, 1.0, ch(1))
+        else:
+            act(V("LAM", 0, c), side, bias=ch(shift) if shift else 0.0, f=AF.Abs)
+        lin("L768", V("L768", 0, c), V("LAM", 0, c), 768.0)
+        lin("ABO", V("AB", c, 2 * c), ends("SOB", o, h), 1.0, ch(1))
+        lin("ABT", V("AB", 2 * c, 3 * c), ends("SOB", 0, h), 1.0, col(cT))
+        tt(V("AB", 0, c), V("AB", c, 2 * c), V("L768", 0, c), A.add)
+        tt(V("AB", 3 * c, 4 * c), V("AB", 2 * c, 3 * c), V("LAM", 0, c), A.mult)
+        cp(V("ABL", 0, 4 * c), V("AB", 0, 4 * c))
+        act(V("G1", o + h, o + 3 * h), ind(res, V("ABL", 0, 2 * c)), f=AF.Abs)
+        act(V("PB", 0, 2 * h, 2), ind(res, V("ABL", 3 * c, 4 * c)), f=AF.Relu)
+        wrap("SOE", 0, V("G1", o + h, o + 3 * h))
+        listed(V("L1", 0, 2 * c), "SOE", 0, 2 * h)
+        act(V("PB", 1, 2 * h, 2), ind(oxw, V("L1", 0, c)))
+        wrap("SOF", 0, V("G1", o, o + 2 * h), "CP4")
+        by_fours(V("L5", 0, h // 2), "SOF", 0, 2 * h, c4t)
+        wrap("SOI", 0, V("PB", 0, 2 * h), "CP8")
+        by_fours(V("L5", h // 2, 3 * h // 4), "SOI", 0, 2 * h, c4t, 8)
 
     def relink(r):
         h = HS[r]
         c = h // 16
-        cp(V("L6", 0, c), V("SJ", 0, c))
-        cp(ind(V("CH", 0, 512), V("L6", 0, c)), V("SV", 0, h))
+        act(V("PA", 1, 2 * h, 2), ind(oxw, V("L1", c, 2 * c)))
+        cp(ind(kids(-256, 512), V("ABL", 2 * c, 3 * c)), V("PA", 1, 2 * h, 2))
         if r < 2:
-            act(V("SELC", 0, h), ind(io, V("L6", 0, c)))
-            cp(ind(V("SR"), V("L2", 0, c)), V("SELC", 0, h))
-            act(V("CH", 512, 768), V("CH", 0, 256))
+            act(V("PA", 0, 2 * h, 2), ind(res, V("ABL", 2 * c, 3 * c)), f=AF.Relu)
+            wrap("SOD", 0, V("PA", 0, 2 * h), "CP32")
+            listed(V("STL", 0, c), "SOD", 0, 2 * h, run=32)
+            cp(ind(V("SGX", 16, 656), V("STL", 0, c)), V("G1", 0, h))
+            lin("KIDD", kids(512, 768), kids(0, 256))
 
     def leaves(r):
         m = HS[r - 1]
         c = m // 16
-        lp, e0 = "LP%d" % r, 0 if r == 1 else 40
-        if r == 1:
-            wrap("SO9", m, V(lp, m, 3 * m), "CP16", 2 * m)
-            cp(V("EI", 0, c), V("OE", c, 2 * c))
-            cp(V("TL", 0, c), V("OE", c, 2 * c))
-            tt(V("Q9", 0, c), V("SO9", m + 15, 2 * m, 16), V("PW"), A.add)
-            ts(V("POS1", 0, c), V("Q9", 0, c), 2048.0, A.mult, -1.0, A.add)
-        else:
-            wrap("SO9", 0, V(lp, 0, 3 * m), "CP16", 3 * m)
-            ts(V("EI", 0, c), V("SO9", 15, m, 16), col(c16), A.add)
-            ts(V("TL", e0, e0 + c), V("SO9", 15, m, 16), col(c16), A.add)
-            ts(V("POS2", 0, c), V("SO9", m + 15, 2 * m, 16), col(c16), A.add)
-        ts(V("LID", 0, c), V("SO9", 2 * m + 15, 3 * m, 16), col(c16), A.add)
-        act(V("LC", 0, m), V(lp, 2 * m, 3 * m), scale=col(cF1))
-        ts(V("EJ", 0, c), V("EI", 0, c), 255, A.bitwise_and)
-        act(V("CSR", 0, m), ind(V("SR"), V("LID", 0, c)))
-        wrap("SOC", 0, V("CSR", 0, m), "CP16", m)
-        cp(V("BL", e0, e0 + c), V("EJ", 0, c))
-        ts(V("CSL", 0, c), V("SOC", 15, m, 16), col(c16), A.add)
-        tt(V("FLD%d" % r), ind(V("CONST0"), V("CSL", 0, c)), V("LC", 0, m), A.add)
+        lt, lp = "LT%d" % r, "LP%d" % r
+        lid, par, now, at = (V("JL", 8, 16), 2 * m, m, 0) if r == 1 else (V("SL", 8, 12), 0, m, 56)
+        act(V(lt, par, par + m), ind(lw(PARN), lid))
+        act(V(lt, now, now + m), ind(sr, lid))
+        act(V(lt, 2 * m - par, 3 * m - par), ind(lw(POSL), lid))
+        wrap("SOE", 0, V(lt))
+        listed(V("BL", at, at + 3 * c), "SOE", 0, 3 * m, 256)
+        lin("LP", V(lp, 0, m), V("BN0", 0, 256, 2)) if r == 1 else lin("LP", V(lp, 0, m), V("SN", 128, 192), 1.0, 256.0)
+        act(V(lp, m, 2 * m), ind(V("IDM"), V("BL", at + c, at + 2 * c)), bias=256.0)
+        wrap("SO4", 0, V(lp), "CP4")
+        by_fours(V("P4L", 0, m // 2), "SO4", 0, 2 * m, c4t)
 
     def update(r):
         h = HS[r]
         lo = LOFF[r] + h - 128
         for b in range(4):
             mm(V("pd", 512 * b, 512 * b + 128), "qw", "sw", 128 * b, "lq", "ls", lo, lo + 128)
-            act(V("hz", 4 + b, 4 + 4 * h, 4), V("pd", 512 * b + 128 - h, 512 * b + 128), scale=0.03125, f=AF.Relu)
-        tt(V("vv", 0, 4 * h), ind(xw, V("L5", 0, h // 4)), V("hz", 4, 4 + 4 * h), A.add)
-        tt(V("uu", 0, 4 * h), ind(V("hz", 0, 4 + 4 * h), V("L5", h // 2, 3 * h // 4)), V("vv", 0, 4 * h), A.add)
-        cp(ind(V("xt"), V("L5", h // 4, h // 2)), V("uu", 0, 4 * h))
+            o, p = V("hz", b, 4 * h, 4), V("pd", 512 * b + 128 - h, 512 * b + 128)
+            if b >= 4 - RELU_V:
+                ts(o, p, 0.0, A.max, 0.03125, A.mult)
+            else:
+                act(o, p, scale=0.03125, f=AF.Relu)
+        tt(V("xt", 2048, 2048 + 4 * h), ind(xw, V("L5", 0, h // 4)), V("hz", 0, 4 * h), A.add)
+        tt(V("uu", 0, 4 * h), ind(V("xt"), V("L5", h // 4, h // 2)), V("hz", 0, 4 * h), A.add)
+        cp(ind(V("xt"), V("L5", h // 2, 3 * h // 4)), V("uu", 0, 4 * h))
 
     def number(r):
         m = HS[r - 1]
         c = m // 16
-        state(TW1 if r == 1 else TW2)
-        t, l0, ev, lf = (TW1, 0, m, 0) if r == 1 else (T2S, 8, 0, 512)
+        state(tw(TW1 if r == 1 else TW2, 255), A.is_gt)
+        folds(r)
+        t, l0, ev, lf, pos = (TW1, 16, m, 0, V("BL", 0, 8)) if r == 1 else (T2S, 24, 0, 512, V("BL", 64, 68))
         if r == 2:
-            tt(tw(T2S), tw(TW2), tw(NF0), A.mult)
+            tt(tw(T2S), tw(TW2), tw(SG1), A.mult)
         tt(V("PROD", 0, 512 + m), ind(tw(t), V("BL", l0, l0 + 32 + c)), V("BV%d" % r), A.mult)
         scan(V("SS"), V("one", 0, 512), V("PROD", ev, ev + 512), 0.0, A.mult, A.add)
-        tt(V("NU2", 0, m), V("PROD", lf, lf + m), V("IO", 0, m), A.add)
-        tt(V("NUM", 0, m), ind(V("SS"), V("POS%d" % r, 0, c)), V("NU2", 0, m), A.add)
-        wrap("SON", 0, V("NUM", 0, m), "CP16", m)
-        ts(V("NL", 0, c), V("SON", 15, m, 16), col(c16), A.add)
-        cp(ind(V("BN%d" % r), V("NL", 0, c)), V("FLD%d" % r))
+        tt(V("NUM", 0, m), ind(V("SS"), pos), V("PROD", lf, lf + m), A.add)
+        wrap("SOE", 0, V("NUM", 0, m), "CPJ")
+        listed(V("NL", 0, c), "SOE", 0, m)
+        cp(ind(V("BN%d" % r), V("NL", 0, c)), V("IDL", 0, m))
 
-    fold(0)
-    act(V("CH", 512, 768), V("CH", 0, 256))
-    act(V("ZT", 0, 256), V("SR", 256, 512))
-    act(V("ZT", 256, 512), V("SR", 256, 512), bias=512.0)
-    wrap("SO1", 0, V("SXR"), "CP16", 512)
-    ts(V("XY", 0, 16), V("WS", 48, 64), 256.0, A.is_ge, 1024.0, A.mult)
-    ts(V("XY", 16, 32), V("WS", 48, 64), 256.0, A.is_ge)
-    act(V("SXW", 0, 32), V("SO1", 15, 512, 16), bias=col(cB0))
-    tt(V("HL"), V("SXW", 0, 16), V("XY", 16, 32), A.add)
-    tt(V("TGX"), V("SXW", 0, 16), V("XY", 0, 16), A.add)
-    cp(V("HIL"), V("SXW", 16, 32))
-    ts(V("HI", 0, 16), V("HL"), 0.5, A.mult, -0.25, A.add)
+    send(0)
     book(0)
-    act(V("LP1", 256, 384), ind(V("CH", 0, 512), V("OE", 8, 16)))
-    relink(0)
-    act(V("SXP", 0, 256), V("SXR", 0, 256))
-    act(V("SXP", 256, 512), V("SXR", 256, 512), bias=-EPS)
-    act(V("LP1", 128, 256), ind(V("SXP"), V("OE", 8, 16)))
-    act(V("HIW", 256, 512), ind(idw, V("HIL")))
-    act(V("MG"), ind(V("HIW"), V("UN", 48, 64)))
-    act(V("ZZ"), ind(V("ZT"), V("ORDW")))
+    tt(V("DD", 0, 256), sxr(256), V("DE", 256, 512), A.subtract)
+    lin("AL", V("AL", 0, 256), sxr(0, 256), 0.5, 128.25)
+    lin("AL", V("AL", 256, 512), V("DD", 0, 256), 0.5, 128.25)
+    lin("RH", V("RH"), sxr(256), 1.0, 1024.0)
+    tt(V("DD", 256, 512), sxr(256), V("RH"), A.subtract)
+    cp(V("PARL"), V("SJ", 0, 16))
+    act(lw(POSL), ind(V("DD", 256, 512), V("PARL")), scale=2048.0, bias=2048.0 * 1024 - 256)
+    lin("PARD", lw(PARN + 512), lw(PARN + 256))
+    act(V("PE"), ind(lw(PARN + 256, 512), ordw))
+    wrap("SOG", 0, V("PE"))
+    listed(V("BL", 24, 56), "SOG", 0, 512, 256)
+    act(V("AI"), ind(V("AL"), V("EVL", 32, 64)))
+    tt(lw(ALM), ind(V("AL"), V("EVL", 16, 32)), lw(LG), A.subtract)
+    tt(V("DT", 256, 512), ind(V("AL"), V("EVL", 32, 48)), V("AI", 256, 512), A.subtract)
+    lin("NEG", V("DT", 0, 256), V("DT", 256, 512), -1.0)
+    act(V("BV1", 128, 640), ind(V("DT"), ordw))
+    tt(V("BV1", 0, 128), ind(lw(ALM), V("JL", 8, 16)), V("WB", 384, 512), A.subtract)
     update(0)
-    wrap("SOH", 0, V("MG"), "CPH", 256)
-    ts(V("MW"), V("SOH", 15, 256, 16), col(cH), A.add, 256.0, A.add)
-    wrap("SO8", 0, V("ZZ"), "CP16", 512)
-    tt(V("SXW", 32, 48), V("MW"), V("TGX"), A.min)
-    ts(V("TL", 8, 40), V("SO8", 15, 512, 16), col(c16), A.add)
-    ts(V("HI", 16, 48), V("SXW", 16, 48), 0.5, A.mult, 0.25, A.add)
-    ts(V("ZI"), V("SO8", 15, 512, 16), col(c16), A.add)
-    tt(V("DL", 0, 16), V("HI", 16, 32), V("HI", 32, 48), A.subtract)
-    tt(V("DL", 16, 32), V("HI", 0, 16), V("HI", 32, 48), A.subtract)
-    ts(V("ZJ"), V("ZI"), 255, A.bitwise_and)
-    ts(V("DLL"), V("DL"), 512.0, A.add)
-    act(V("TB1", 0, 512), ind(V("IO"), V("DLL")), bias=-512.0)
-    act(V("TB1", 512, 1024), V("TB1", 0, 512), scale=-1.0)
-    cp(V("BL", 8, 40), V("ZJ"))
-    cp(V("LM"), V("HI"))
+    relink(0)
     leaves(1)
-    act(V("BV1"), ind(V("TB1"), V("TL", 0, 40)))
 
     number(1)
-    fold(1)
-    act(tw(NF1), tw(TW1), scale=-1.0, bias=1.0)
-    act(V("LP1", 0, 128), ind(io, V("TL", 0, 8)))
-    act(V("LP1", 128, 256), ind(io, V("POS1")))
+    send(1)
     book(1)
-    cp(ind(V("ALV"), V("IE", 0, 4)), V("one", 0, 64))
-    relink(1)
+    lin("JTL", lw(JTL), V("FLDE"), 0.5, 127.5)
+    act(lw(AFL), ind(V("AL"), V("EVL", 16, 32)))
+    wrap("SOC", 0, V("AI"))
+    listed(V("AB2"), "SOC", 0, 512, -128)
+    lin("SG1", tw(SG1), tw(TW1), -2.0, 1.0)
+    for j, t in enumerate((AFL, JTL, LG)):
+        act(V("LU", 64 * j, 64 * j + 64), ind(lw(t), V("SL", 8, 12)))
+    wrap("SOA", 0, V("LU", 0, 128))
+    listed(V("LM"), "SOA", 0, 128, -128)
+    cp(ind(V("ALV"), V("LM", 4, 8)), V("one", 0, 64))
     scan(V("CNT", 1, 129), V("one", 0, 128), V("ALV"), 0.0, A.mult, A.add)
     cn = V("CNT", 0, 129)
-    act(V("MR"), ind(cn, V("LM", 32, 48)))
-    for j in range(3):
-        act(V("LP2", 64 * j, 64 * j + 64), ind(V("LP1", 128 * j, 128 * j + 128), V("IE", 0, 4)))
-    act(tw(NF0), tw(TW1), scale=-2.0, bias=1.0)
+    act(V("MR"), ind(cn, V("AB2", 16, 32)))
+    tt(V("BLJ"), ind(cn, V("LM", 4, 8)), V("LU", 128, 192), A.add)
+    tt(V("DT2", 256, 512), ind(cn, V("AB2", 0, 16)), V("MR"), A.subtract)
+    tt(V("BV2", 512, 576), ind(cn, V("LM", 0, 4)), V("BLJ"), A.subtract)
+    lin("NEG", V("DT2", 0, 256), V("DT2", 256, 512), -1.0)
+    act(V("BV2", 0, 512), ind(V("DT2"), ordw))
     update(1)
-    tt(V("TB2", 0, 256), ind(cn, V("LM", 16, 32)), V("MR"), A.subtract)
-    tt(V("TB2", 256, 512), ind(cn, V("LM", 0, 16)), V("MR"), A.subtract)
-    act(V("TB2", 512, 1024), V("TB2", 0, 512), scale=-1.0)
+    relink(1)
     leaves(2)
-    act(V("BV2"), ind(V("TB2"), V("TL", 8, 44)))
 
     number(2)
-    fold(2)
-    tt(tw(F2), tw(TW1), tw(T2S), A.add)
-    act(tw(NF2), tw(F2), scale=-1.0, bias=1.0)
+    send(2)
     book(2)
     update(2)
 
@@ -600,22 +617,26 @@ def rank_program(g, core, T, topo):
         quant("qx", "sx", 256 * j, 256 * j + 256, V("xt", 1024 * j, 1024 * j + 1024))
         mm(V("pp", 512 * j, 512 * j + 256), "qv", "sv", 0, "qx", "sx", 256 * j, 256 * j + 256)
         dma("y", T.oc[:, 1024 * j:1024 * j + 1024], T.qx[:, 256 * j:256 * j + 256].bitcast(dt.uint8), "outa", [V("qx", 256 * j, 256 * j + 256)[1]], [], 2.5)
-        act(V("yb", 256 * j, 256 * j + 256), V("pp", 512 * j, 512 * j + 256), f=AF.Copy)
+        if j >= 2 - YB_V:
+            cp(V("yb", 256 * j, 256 * j + 256), V("pp", 512 * j, 512 * j + 256))
+        else:
+            act(V("yb", 256 * j, 256 * j + 256), V("pp", 512 * j, 512 * j + 256), f=AF.Copy)
         dma("s", T.y[:, 256 * j:256 * j + 256], T.yb[:, 256 * j:256 * j + 256], "outb", [V("yb", 256 * j, 256 * j + 256)[1]], [], 2.5)
     for k in range(4):
         dma("y", T.osc[4 * k:4 * k + 4, :], T.sx[32 * k:32 * k + 4, :], "outa", [V("sx")[1]], [], 1.9)
-    wrap("SOH", 0, tw(F2), "CPH", 256)
     relink(2)
-    wrap("SO1", 0, V("KO", 256, 512), "CP16", 256)
-    ts(V("FW2"), V("SOH", 15, 256, 16), col(cH), A.add, 256.0, A.mult)
-    ts(V("DM"), V("SO1", 15, 256, 16), col(cN16), A.is_ge, 512.0, A.mult)
-    tt(V("KL", 0, 16), V("WBS", 80, 96), V("FW2"), A.add)
-    tt(V("KL", 16, 32), V("WBS", 96, 112), V("FW2"), A.subtract)
-    tt(V("KK", 0, 16), V("KL", 0, 16), V("DM"), A.max)
-    tt(V("KK", 16, 32), V("KL", 16, 32), V("DM"), A.max)
-    ms(V("CH", 511, 513), -1.0)
-    cp(V("KLL"), V("KK"))
-    act(V("KID"), ind(V("CH", 0, 513), V("KLL")))
+    fill(kids(512, 1024), -1)
+    ts(tw(SGR), V("RESW", 256, 512), 0.0, A.is_gt, 512.0, A.mult)
+    wrap("SOG", 0, tw(TW1, 512))
+    wrap("SOK", 256, tw(SGR), "CPJ")
+    tt(V("KW", 0, 16), V("TWW"), ends("SOG", 0, 256), A.subtract)
+    tt(V("KW", 16, 32), V("KW", 0, 16), ends("SOG", 256, 256), A.subtract)
+    act(V("KW", 0, 16), V("KW", 16, 32), scale=256.0, bias=ch(-512), f=AF.Abs)
+    tt(V("KW", 32, 48), ends("SOK", 256, 256), V("KW", 0, 16), A.subtract)
+    tt(V("KW", 48, 64), ends("SOK", 256, 256), V("KW", 0, 16), A.add)
+    ts(V("KLL", 0, 16), V("KW", 32, 48), ch(1), A.add, 256.0, A.add)
+    ts(V("KLL", 16, 32), V("KW", 48, 64), ch(1), A.add)
+    act(V("KID"), ind(kids(0, 1024), V("KLL")))
     klo = PLACE["KID"][1]
     dma("y", T.kid[:], T.f32[0:128:16, klo:klo + 512], "outa", [V("KID")[1]], [], 1.9)
 

@@ -3,21 +3,23 @@ from concourse.mybir import dt, AluOpType, ActivationFunctionType
 A = AluOpType
 AF = ActivationFunctionType
 BIG, HUGE, MAGIC, EPS = 1024.0, 2048.0, 12582912.0, 1.0 / 2048
-WAKE, SOON, PASSES, ORDER = 0.22, 0.1, 8, {}
-IFIX, VFIX, SFIX, CYC, GAT, SCA, PECOL = 0.055, 0.015, 0.04, 0.00085, 0.00112, 0.0023, 0.0007
+WAKE, SOON, PASSES, ORDER = 0.22, (0.4, 0.5, 0.6, 0.7, 0.8, 0.9), 6, {}
+IFIX, VFIX, SFIX, CYC, GAT, SCA, PECOL = 0.055, 0.015, 0.04, 0.00095, 0.0015, 0.0033, 0.0007
 FLIGHT = [2.0, 1.5, 1.5]
 HS = [128, 64, 32]
 LOFF = [0, 128, 192]
 STEP = [1, 2, 4]
-CH = [1, 1, 1, 1, 1, 2, 4]
+CH = [1, 1, 1, 1, 1, 2, 4, 8]
 OUT, BASE = [], [512]
-for _k in range(7):
+for _k in range(8):
     OUT.append(BASE[-1] + 512)
     BASE.append(OUT[-1] + 16 * CH[_k])
-VCOLS = [12, 12, 12, 12, 12, 12, 14]
-FOLD_V, RELU_V, YB_V = [12, 6, 0], 1, 2
-ON_V = {"NF0", "NEG", "SG1", "LAM", "L768", "ABT"}
-PARTS = [4, 2, 1]
+LANES = [[("v", 0), ("s", 8), ("v", 18), ("s", 24)], [("v", 0), ("v", 8), ("s", 16)]]
+PIECE = {"PAY": 96, "DX": 96, "TG": 128, "SC": 64, "WR": 256, "SG": 128}
+FOLD_V, RELU_V, YB_V = [16, 8, 4], 2, 1
+LEFT = 0.1875
+ON_V = {"NEG", "SG1", "GN", "GO"}
+PARTS = [8, 4, 2]
 
 ARENA = {"f32": [], "b16": [], "u16": [], "i32": [], "h16": []}
 PLACE = {}
@@ -30,14 +32,16 @@ def _al(kind, **kw):
         PLACE[n] = (kind, lo, w)
 
 
-_al("f32", OX=656, RESW=1280, KIDX=1536, COL=16, MUL=8, CM=8, PF=8, C32=32, C32a=32, C32b=32, KV=128, MM=32, KP=32, YW=32, UF=32, IW=32,
-    WBS=112, WD=96, WP=96, WS=96, TWW=16, DE=512, DD=512, SX=1040, L256=32, EV=64, DL=16, LAM=8, AB=32, L768=8, KW=64, KID=512)
-_al("b16", CPH=576, CP4=256, CP8=256, CP32=256, WB=BASE[7] + 512, OC=384, SGX=656, TWB=1792, VV=512, IDM=512,
-    LW=2304, AL=512, DT=512, DT2=512, AI=512, PE=512, BN0=256, BN1=128, BN2=64, IDL=256, BV1=640, BV2=576, PROD=640, SS=512,
-    SN=256, LT1=384, LT2=192, LU=192, LP1=256, LP2=128, BLJ=64, ALV=128, CNT=144, MR=256, NUM=128)
-_al("h16", SOH=576, SOG=512, SO4=256, SOA=256, SOB=384, SOC=512, SOD=256, SOE=384, SOF=256, SOI=256, SOK=512, RH=256, CPJ=256, FLDE=256, G1=640, PA=256, PB=256)
-_al("u16", QL=36, UL=8, KL16=32, UN=96, PARL=16, S0L=32, LS0=40, LS1=40, LS2=40, LS3=40, ORDW=40, EVL=64, P4L=64, NL0=16, FL=32, JL=16, SL=16,
-    ABL=32, L1=16, L5=96, STL=8, BL=68, NL=8, AB2=32, LM=8, KLL=32)
+_al("f32", OX=528, RESW=1024, RES2=1024, KIDS=1280, COL=16, MUL=8, CM=8, PF=8, C32=32, C32a=32, C32b=32, KV=128, MM=32, KP=32, YW=32, UF=32, IW=32,
+    WBS=96, DE=512, DD=512, DX=512, SX=1040, L256=32, EV=64, KW=80, KID=512, BN0=256, BN1=128, BN2=64, SOA=256,
+    OJ=256, TOPJ=256, AJ=512, BJ=512, PAY=256, C0=256, C1=128, CL=256, PM=128)
+_al("b16", CPH=576, CP4=256, CP8=256, CP32=256, WB=BASE[8] + 512, OC=256, SGX=656, TWB=1536, NFX=256, W5=1280, W6=768, VV=512, IDM=512,
+    LW=2304, AL=512, DT=512, DT2=512, AI=512, PE=512, IDL=256, BV1=640, BV2=576, BVS=576, PROD=640, SS=512, TJ=256, XJ=64, DJ=64,
+    LT1=384, LT2=192, LU=192, LP1=256, LP2=128, BLJ=64, ALV=128, CNT=144, MR=256, NUM=128)
+_al("h16", SOH=576, SOT=576, SOG=512, SO4=256, SO5=128, SO6=256, SOB=384, SOC=512, SOD=256, SOE=384, SOF=256, SOI=256, SOK=768, SOL=384, SOM=128, SON=128, SOO=128,
+    SOP=512, SOQ=128, SOR=256, RH=256, CPJ=256, FLDE=256, G1=768, GL=128, GZ=16, GT=128, PA=256, PB=256)
+_al("u16", QL=36, UL=8, KL16=32, UN=96, LB=16, PARL=32, S0L=32, LS0=40, LS1=40, LS2=40, LS3=40, ORDW=40, EVL=64, P4L=64, NL0=16, FL=32, JL=16, JX=16,
+    UL3=24, RL=24, NLJ=8, TLJ=8, L5=96, STL=8, BL=68, NL=8, AB2=32, LM=8, KLL=32)
 _al("i32", QI=48, QJ=36, J32=32, J32c=32, UI=8, SI=32, SJ=32)
 
 C4, U8 = "float8_e4m3fn_x4", "uint8"
@@ -80,14 +84,15 @@ def schedule(prog):
             succ[j].append(i)
     queue, cost, lat = [q[0] for q in prog], [q[6] for q in prog], [q[7] for q in prog]
 
-    def place(prio, back):
+    def place(prio, back, soon):
         before, after = (succ, pred) if back else (pred, succ)
         left = [len(d) for d in before]
         ready = [i for i in range(n) if not left[i]]
         at, free, start, order, end = [lat[i] if back else 0.0 for i in range(n)], {}, [0.0] * n, [], 0.0
         while ready:
-            t, e = min((max(at[i], free.get(queue[i], 0.0)), queue[i]) for i in ready)
-            i = max((i for i in ready if queue[i] == e and at[i] <= t + SOON), key=lambda i: (prio[i], -i))
+            done, e = min((max(at[i], free.get(queue[i], 0.0)) + cost[i], queue[i]) for i in ready)
+            t = max(free.get(e, 0.0), min(at[i] for i in ready if queue[i] == e))
+            i = max((i for i in ready if queue[i] == e and at[i] <= t + soon * (done - t)), key=lambda i: (prio[i], -i))
             ready.remove(i)
             order.append(i)
             start[i] = t = max(t, at[i])
@@ -99,16 +104,18 @@ def schedule(prog):
                 if not left[j]:
                     ready.append(j)
         return start, end, order
-    prio = [0.0] * n
+    rest = [0.0] * n
     for i in range(n - 1, -1, -1):
-        prio[i] = cost[i] + lat[i] + max([prio[j] + WAKE for j in succ[i]] + [0.0])
+        rest[i] = cost[i] + lat[i] + max([rest[j] + WAKE for j in succ[i]] + [0.0])
     best = None
-    for _ in range(PASSES):
-        start, end, order = place(prio, False)
-        if best is None or end < best[0]:
-            best = (end, order)
-        rev = place([start[i] + cost[i] + lat[i] for i in range(n)], True)[0]
-        prio = [rev[i] + cost[i] for i in range(n)]
+    for soon in SOON:
+        prio = rest
+        for _ in range(PASSES):
+            start, end, order = place(prio, False, soon)
+            if best is None or end < best[0]:
+                best = (end, order)
+            rev = place([start[i] + cost[i] + lat[i] for i in range(n)], True, soon)[0]
+            prio = [rev[i] + cost[i] for i in range(n)]
     ORDER[n] = best[1]
     return ORDER[n]
 
@@ -127,12 +134,18 @@ def rank_program(g, core, T, topo):
         b = w if b is None else b
         assert 0 <= a < b <= w, (name, a, b, w)
         ap = T[buf][:, lo + a:lo + b] if st == 1 else T[buf][:, lo + a:lo + b:st]
+        n, part = (b - a + st - 1) // st, lambda i, j: V(name, a + i * st, min(b, a + j * st), st)
         if buf in ("pd", "pp"):
-            return (ap, [(buf, a // 512 * 512, (b + 511) // 512 * 512, True, 1)], (b - a + st - 1) // st)
-        return (ap, [(buf, lo + a, lo + b, False, st)], (b - a + st - 1) // st)
+            return (ap, [(buf, a // 512 * 512, (b + 511) // 512 * 512, True, 1)], n, part)
+        return (ap, [(buf, lo + a, lo + b, False, st)], n, part)
 
     def ind(w, o):
-        return (w[0].indirect(o[0]), w[1] + o[1], 16 * o[2])
+        return (w[0].indirect(o[0]), w[1] + o[1], 16 * o[2], lambda i, j: ind(w, o[3](i // 16, j // 16)))
+
+    def bits(name, call, out, *ins, **kw):
+        w = PIECE.get(name, out[2])
+        for a in range(0, out[2], w):
+            call(*[x[3](a, min(a + w, out[2])) if isinstance(x, tuple) and x[2] == out[2] else x for x in (out,) + ins], **kw)
 
     def need(e, sem, c):
         if known[e].get(sem, 0) < c:
@@ -225,9 +238,9 @@ def rank_program(g, core, T, topo):
     def dma(e, out, src, sem, reads, writes, lat=2.1):
         op(e, lambda: Q[e].dma_start(out, src), reads, writes, sem=sem, inc=16, cost=0.06, lat=lat)
 
-    def wrap(out, at, data, pat="CPH"):
+    def wrap(out, at, data, pat="CPH", apart=False):
         n = data[2]
-        scan(V(out, at, at + n), data, V(pat, 0, n), -HUGE, A.max, A.add)
+        bits("WR" if apart else None, scan, V(out, at, at + n), data, V(pat, 0, n), -HUGE, A.max, A.add)
 
     def ends(buf, a, n, run=16):
         return V(buf, a + run - 1, a + n, run)
@@ -236,7 +249,7 @@ def rank_program(g, core, T, topo):
         return V("COL", j, j + 1)
 
     def ch(times):
-        j = [1, -1, 256, -512].index(times)
+        j = [1, 256, -256].index(times)
         return V("CM", j, j + 1)
 
     def pf(j):
@@ -250,17 +263,18 @@ def rank_program(g, core, T, topo):
 
     def by_fours(out, buf, a, n, c, run=4):
         ts(out, ends(buf, a, n, run), 4.0, A.mult, col(c), A.add)
-    cH, cW1, cT, c4r, c4t, c4u = 0, 1, 4, 5, 6, 7
-    TW0, NF0, TW1, T2S, SGR, SG1, TW2 = [256 * j for j in range(7)]
+    cH, cW1, cX, c4r, c4t, c4u, cY = 0, 1, 4, 5, 6, 7, 8
+    NF0, TW1, TW2, SGR, SG1 = [256 * j for j in range(1, 6)]
+    TW0 = 0
     ALM, JTL, AFL, POSL, LG, PARN = 0, 256, 512, 768, 1024, 1536
     idw, iow, xw = V("WB", 0, 512), V("IW", 0, 16), V("xt", 0, 2048)
-    sr, oxw, res = V("SGX", 16, 528), V("OX", 16, 656), V("RESW")
+    sr, res, res2 = V("SGX", 16, 528), V("RESW"), V("RES2")
 
     def sxr(a=0, b=512):
         return V("SX", 528 + a, 528 + b)
 
     def kids(a, b):
-        return V("KIDX", 256 + a, 256 + b)
+        return V("KIDS", a, b)
 
     def lw(a, n=256):
         return V("LW", a, a + n)
@@ -280,19 +294,22 @@ def rank_program(g, core, T, topo):
     iota(V("J32", 16, 32), [[4, 16]], 131, -1)
     iota(V("UI"), [[16, 8]], 0)
     iota(V("UF"), [[0, 2], [16, 16]], 0)
-    iota(V("MUL", 0, 2), [[-2, 2]], 1)
-    iota(V("MUL", 2, 4), [[-768, 2]], 256)
+    iota(V("MUL", 0, 2), [[255, 2]], 1)
+    fill(V("MUL", 2, 3), -256)
     ms(V("one"), 1.0)
     scan(idw, V("one", 0, 512), V("one", 0, 512), -257.0, A.mult, A.add)
     op("g", lambda: g.affine_select(T.zt[:, 0:516], T.one[:, 0:516], [[-1, 516]], A.is_equal, 0.0, 3, 4), [V("one", 0, 516)[1]], [V("zt", 0, 516)[1]], cost=1.1)
     iota(V("OX", 0, 528), [[1, 528]], -16)
     fill(V("SGX", 527, 656), -1)
-    fill(V("TWB", 255, 1792, 256), 0)
-    fill(V("WD", 48, 64), 0)
+    fill(V("TWB", 255, 1536, 256), 0)
+    fill(V("NFX", 255, 256), 256)
+    iota(V("W5", 768, 1024), [[1, 256]], -256)
     iota(V("IDM"), [[0, 2], [1, 256]], -256)
     iota(V("IDL"), [[1, 256]], 0)
-    iota(V("RESW", 0, 512), [[-1, 512]], 0)
-    iota(V("RESW", 768, 1280), [[-1, 512]], 0)
+    iota(V("RESW"), [[0, 2], [-1, 512]], 0)
+    iota(V("RES2"), [[0, 2], [1, 512]], 0)
+    fill(V("BJ", 0, 512, 2), 0)
+    fill(kids(768, 1280), -1)
     iota(V("KV"), [[1, 128]], 512)
     fill(V("CNT", 0, 1), 0)
     fill(V("ALV"), 0)
@@ -301,8 +318,8 @@ def rank_program(g, core, T, topo):
     ts(V("QI", 0, 36), V("QJ"), 15, A.bitwise_and)
     ts(V("J32c"), V("J32"), 15, A.bitwise_and)
     cp(V("QL"), V("QI", 0, 36))
-    for j, bits in enumerate([3, 1, 2, 4, 8]):
-        ts(V("QI", 36 + j, 37 + j), V("QJ", 0, 1), bits, A.bitwise_and)
+    for j, keep in enumerate([3, 1, 2, 4, 8]):
+        ts(V("QI", 36 + j, 37 + j), V("QJ", 0, 1), keep, A.bitwise_and)
     cp(V("PF", 0, 6), V("QI", 35, 41))
     for j, th in enumerate([1.0, 4.0]):
         ts(V("C32b", 16 * j, 16 * j + 16), V("J32c", 16 * j, 16 * j + 16), th, A.is_lt, BIG, A.mult)
@@ -310,13 +327,13 @@ def rank_program(g, core, T, topo):
     tt(V("C32"), V("C32a"), V("C32b"), A.add)
     cp(V("UL"), V("UI"))
     act(V("IW"), V("UF"), bias=pf(0))
-    act(V("WBS", 32, 48), V("UF", 0, 16), bias=pf(0))
     act(col(cH), V("C32a", 15, 16), scale=-1.0, bias=-BIG)
     act(V("CPH"), ind(V("C32", 0, 16), V("QL", 0, 36)))
-    act(V("CM", 0, 4), V("MUL", 0, 4), scale=col(cH))
+    act(V("CM", 0, 3), V("MUL", 0, 3), scale=col(cH))
     for k in (1, 2, 3):
         act(col(cW1 + k - 1), pf(2 + k), scale=BASE[k] / (1 << k), bias=col(cH))
-    act(col(cT), col(cH), bias=512.0)
+    act(col(cX), col(cH), scale=2.0, bias=0.3)
+    act(col(cY), col(cH), scale=2.0, bias=0.8)
     act(col(c4r), V("C32a", 19, 20), scale=-1.0, bias=-BIG)
     act(col(c4t), col(c4r), scale=4.0, bias=pf(1))
     act(col(c4u), col(c4t), bias=1024.0)
@@ -332,66 +349,91 @@ def rank_program(g, core, T, topo):
     o_ = V("KL16")
     op("v", lambda: g.vector.tensor_scalar(o_[0], T.ki[:], 16.0, None, A.add), [V("ki")[1]], [o_[1], [("late", 0, 1, True, 1)]], cost=0.13)
     prog[4:8], prog[len(prog) - 4:] = [], prog[len(prog) - 4:] + prog[4:8]
-    cp(ind(V("SGX"), V("KL16")), idw)
-    act(kids(0, 512), ind(V("OX", 0, 528), V("KL16")))
+    bits("SG", cp, ind(V("SGX"), V("KL16")), idw)
+    bits("SS", act, kids(0, 512), ind(V("OX", 0, 528), V("KL16")))
     lin("KIDD", kids(512, 768), kids(0, 256))
     quant("qu", "su", 0, 128, V("ut"))
     quant("qv", "sv", 0, 128, V("vt"))
     act(V("sup"), ind(V("su"), V("UL")), f=AF.Copy)
     u_ = V("UL")
     op("v", lambda: g.vector.tensor_copy(T.qup[:, 0:128].bitcast(dt.uint32), T.qu[:, 0:128].bitcast(dt.uint32).indirect(u_[0])), [V("qu")[1], u_[1]], [V("qup")[1]], cost=0.24)
-    nb, na, eb, ea = V("WBS", 80, 96), V("WBS", 96, 112), V("WBS", 48, 64), V("WBS", 64, 80)
+    nb, na, eb, ea = V("WBS", 64, 80), V("WBS", 80, 96), V("WBS", 32, 48), V("WBS", 48, 64)
     ts(V("MM"), V("ki"), 256.0, A.is_ge)
-    ts(V("WBS", 80, 112), V("ki"), 256.0, A.is_lt)
+    ts(V("WBS", 64, 96), V("ki"), 256.0, A.is_lt)
     tt(V("KP"), V("ki"), V("MM"), A.mult)
-    tt(V("WBS", 48, 80), V("KP"), V("IW"), A.max)
+    tt(V("WBS", 32, 64), V("KP"), V("IW"), A.max)
     tt(V("YW", 0, 16), nb, ea, A.mult)
     tt(V("YW", 16, 32), na, eb, A.mult)
     tt(V("WBS", 0, 32), V("KP"), V("YW"), A.add)
-    tt(V("WD", 0, 16), V("WBS", 0, 16), V("WBS", 16, 32), A.subtract)
-    tt(V("WD", 16, 32), ea, iow, A.subtract)
-    tt(V("WD", 32, 48), iow, eb, A.subtract)
-    tt(V("WD", 64, 80), na, nb, A.subtract)
-    tt(V("WD", 80, 96), nb, na, A.subtract)
+    cp(V("UN", 32, 96), V("WBS", 32, 96))
+    cp(V("UN", 0, 32), V("WBS", 0, 32))
+    act(V("W5", 512, 768), ind(idw, V("UN", 48, 64)))
+    act(V("W5", 1024, 1280), ind(idw, V("UN", 32, 48)))
+    act(V("W5", 0, 512), ind(idw, V("UN", 0, 32)))
+    bits("SS", act, V("W6", 0, 512), ind(V("IDL"), V("UN", 64, 96)))
+    lin("W6", V("W6", 512, 768), V("W6", 0, 256))
 
-    def state(bits, *how):
+    def state(turns, *how):
         quant("qx", "sx", 256, 512, V("xt", 1024, 2048))
         mm(V("pp", 0, 256), "qup", "sup", 0, "qx", "sx", 256, 512)
         quant("qx", "sx", 0, 256, V("xt", 0, 1024))
-        ts(bits, V("pp", 0, 255), 0.0, *how)
+        ts(turns, V("pp", 0, 255), 0.0, *how)
         for b in range(4):
             mm(V("pd", 512 * b, 512 * b + 512), "qe", "se", 128 * b, "qx", "sx", 0, 512)
-            act(V("xt", b, 2048, 4), V("pd", 512 * b, 512 * b + 512), f=AF.Copy)
+            bits("EV", act, V("xt", b, 2048, 4), V("pd", 512 * b, 512 * b + 512), f=AF.Copy)
 
-    state(tw(TW0, 255), A.is_gt)
-    wrap("SOH", 0, tw(TW0))
-    listed(V("TWW"), "SOH", 0, 256)
-    tt(V("WP"), ind(V("TWW"), V("QL", 0, 6)), V("WD"), A.mult)
+    state(V("NFX", 0, 255), A.is_le, 256.0, A.mult)
+    wrap("SOR", 0, V("NFX"), "CPJ")
+    listed(V("LB"), "SOR", 0, 256)
     wrap("SOG", 0, sr)
-    tt(V("WS"), V("WP"), V("WBS", 16, 112), A.add)
     listed(V("S0L"), "SOG", 0, 512, 256)
-    cp(V("UN"), V("WS"))
-    act(V("VV", 256, 512), ind(idw, V("UN", 32, 48)))
-    cp(V("VV", 0, 256), ind(idw, V("UN", 16, 32)))
-    act(V("WB", BASE[0] + 256, BASE[0] + 512), ind(idw, V("UN", 0, 16)))
-    ts(V("LS0", 17, 33), V("WS", 0, 16), float(BASE[0]), A.add)
+    act(V("VV", 256, 512), ind(V("W5", 768, 1280), V("LB")))
+    cp(V("VV", 0, 256), ind(V("W5", 512, 1024), V("LB")))
+    act(V("WB", BASE[0] + 256, BASE[0] + 512), ind(V("W5", 0, 512), V("LB")))
     cp(V("WB", BASE[0], BASE[0] + 256), ind(V("VV"), V("S0L", 16, 32)))
-    wrap("SOH", 0, V("WB", BASE[0], BASE[0] + 256))
-    listed(V("LS0", 1, 17), "SOH", 0, 256, 256 + BASE[0])
-    lin("NF0", tw(NF0), tw(TW0), -1.0, 1.0)
-    act(lw(LG, 512), ind(tw(TW0, 512), V("S0L")))
-    act(lw(PARN, 512), ind(V("IDM"), V("S0L")))
+    wrap("SOH", 0, V("WB", BASE[0], BASE[0] + 512))
+    listed(V("LS0", 1, 33), "SOH", 0, 512, 256 + BASE[0])
+    lin("TW0", tw(TW0), V("NFX"), -1.0 / 256, 1.0)
+    lin("TW0", tw(NF0), V("NFX"), 1.0 / 256)
+    bits("SS", act, lw(LG, 512), ind(tw(TW0, 512), V("S0L")))
+    bits("SS", act, lw(PARN, 512), ind(V("IDM"), V("S0L")))
     listed(V("SI"), "SOG", 0, 512, 256)
     ts(V("SJ"), V("SI"), 255, A.bitwise_and)
     wrap("SO4", 0, lw(PARN), "CP4")
     by_fours(V("P4L"), "SO4", 0, 256, c4u)
-    wrap("SOC", 0, lw(LG, 512))
+    wrap("SOC", 0, lw(LG, 512), apart=True)
     lin("L256", V("L256"), ends("SOC", 0, 512), 256.0, ch(256))
     tt(V("EV", 0, 16), V("SJ", 0, 16), V("L256", 0, 16), A.add)
     tt(V("EV", 16, 48), V("SJ"), V("L256"), A.subtract)
     tt(V("EV", 48, 64), iow, V("L256", 16, 32), A.subtract)
     ts(V("EVL"), V("EV"), 256.0, A.add)
-    act(V("DE"), ind(V("IDL"), V("UN", 64, 96)), bias=EPS)
+    for j in range(2):
+        act(V("DE", 256 * j, 256 * j + 256), ind(V("W6", 256 - 256 * j, 768 - 256 * j), V("LB")), bias=EPS)
+    cp(V("PARL"), V("SJ"))
+
+    def ahead(r, slot, parent):
+        m = 2 * HS[r]
+        act(V("AJ", 0, 2 * m, 2), ind(kids(256, 768), slot))
+        act(V("AJ", 1, 2 * m, 2), V("AJ", 0, 2 * m, 2), bias=512.0)
+        act(V("TJ", 0, m), ind(V("SGX", 272, 528), parent))
+        if r == 0:
+            top = ind(lw(PARN + 256), parent)
+            lin("CL", V("CL"), lw(LG), LEFT)
+            bits("PAY", tt, V("PAY"), V("CL"), V("IDL"), A.add)
+        else:
+            wrap("SOM", 0, V("TJ", 0, m))
+            listed(V("TLJ", 0, m // 16), "SOM", 0, m, 256)
+            top = ind(V("IDM"), V("TLJ", 0, m // 16))
+            if r == 1:
+                act(V("CL", 0, m), ind(tw(TW0, 512), slot), scale=LEFT)
+            else:
+                act(V("XJ"), ind(tw(TW0, 512), slot))
+                tt(V("DJ"), ind(tw(TW1), parent), V("XJ"), A.subtract)
+                act(V("CL", 0, m), V("DJ"), scale=LEFT, f=AF.Abs)
+            lin("C1", V("C1", 0, m), V("CL", 0, m), -2.0, LEFT)
+            tt(V("C0", 0, m), V("CL", 0, m), V("IDL", 0, m), A.add)
+        act(V("BJ", 1, 2 * m, 2), top, bias=512.0)
+    ahead(0, V("S0L", 0, 16), V("PARL", 0, 16))
 
     def folds(r):
         n = 8 * HS[r]
@@ -403,40 +445,47 @@ def rank_program(g, core, T, topo):
                 act(leaf, ind(V("xt", 0, 1024), V("P4L", a // 16, (a + w) // 16)))
             tt(V("fc", a, a + w), ind(V("xt", 1024, 2048), V("P4L", at + a // 16, at + (a + w) // 16)), leaf, A.add)
     folds(0)
-    for k in range(7):
-        c, o, vc = CH[k], OUT[k], VCOLS[k]
+    for k in range(8):
+        c, o, so = CH[k], OUT[k], "SOH" if k % 2 else "SOT"
         nc, ls = 32 + c, "LS%d" % k if k < 4 else "ORDW"
         win = V("WB", 0 if k < 4 else BASE[k], BASE[k] + 512)
-        act(V("WB", o + 16 * vc, o + 16 * nc), ind(win, V(ls, vc, nc)))
-        if vc:
-            cp(V("WB", o, o + 16 * vc), ind(win, V(ls, 0, vc)))
-        n = 16 * nc if k < 6 else 64
-        wrap("SOH", 0, V("WB", o, o + n))
-        if k < 3:
-            ts(V("LS%d" % (k + 1), 0, 1), V("SOH", 15, 16), col(cW1 + k), A.add, 256.0, A.add)
-            listed(V("LS%d" % (k + 1), 1, 33), "SOH", 16, 512, 256 + BASE[k + 1])
+        cuts = [a for e, a in LANES[k == 7]] + [nc]
+        for (e, a), b in zip(LANES[k == 7], cuts[1:]):
+            (cp if e == "v" else act)(V("WB", o + 16 * a, o + 16 * b), ind(win, V(ls, a, b)))
+        for a, b in zip(cuts, cuts[1:]) if k < 7 else [(0, 8)]:
+            wrap(so, 16 * a, V("WB", o + 16 * a, o + 16 * b))
+            if k < 3:
+                if a == 0:
+                    ts(V("LS%d" % (k + 1), 0, 1), V(so, 15, 16), col(cW1 + k), A.add, 256.0, A.add)
+                    a = 1
+                listed(V("LS%d" % (k + 1), a, b), so, 16 * a, 16 * (b - a), 256 + BASE[k + 1])
+            else:
+                at = c if k > 3 else 0
+                listed(V("ORDW", at + a, at + b), so, 16 * a, 16 * (b - a), 256)
+
+    def shared(out, a, win, lst, b, n):
+        act(V(out, a + n // 2, a + n), ind(win, V(lst, b + n // 32, b + n // 16)))
+        cp(V(out, a, a + n // 2), ind(win, V(lst, b, b + n // 32)))
+    shared("OC", 0, V("WB", BASE[8], BASE[8] + 512), "ORDW", 0, 256)
+    wrap("SOR", 0, V("OC"))
+    listed(V("ORDW", 16, 32), "SOR", 0, 256, 256)
+    for c in range(2):
+        if c:
+            shared("DD", 256, V("DE"), "ORDW", 16, 256)
         else:
-            at = c if k > 3 else 0
-            listed(V("ORDW", at, at + n // 16), "SOH", 0, n, 256)
-    for c in range(4):
-        if c < 3:
-            act(V("OC", 128 * c, 128 * c + 128), ind(V("WB", BASE[7], BASE[7] + 512), V("ORDW", 8 * c, 8 * c + 8)))
-            wrap("SOH", 128 * c + 64, V("OC", 128 * c, 128 * c + 128))
-            listed(V("ORDW", 8 * c + 8, 8 * c + 16), "SOH", 128 * c + 64, 128, 256)
-        act(V("DD", 128 * c, 128 * c + 128), ind(V("DE"), V("ORDW", 8 * c, 8 * c + 8)))
-        scan(V("SX", 16 + 128 * c, 144 + 128 * c), V("one", 0, 128), V("DD", 128 * c, 128 * c + 128), V("SX", 15 + 128 * c, 16 + 128 * c) if c else -EPS, A.mult, A.add)
-        cp(ind(sxr(), V("ORDW", 8 * c, 8 * c + 8)), V("SX", 16 + 128 * c, 144 + 128 * c))
+            act(V("DD", 0, 256), ind(V("DE"), V("ORDW", 0, 16)))
+        scan(V("SX", 16 + 256 * c, 272 + 256 * c), V("one", 0, 256), V("DD", 256 * c, 256 * c + 256), V("SX", 271, 272) if c else -EPS, A.mult, A.add)
+        cp(ind(sxr(), V("ORDW", 16 * c, 16 * c + 16)), V("SX", 16 + 256 * c, 272 + 256 * c))
     ordw = V("ORDW", 0, 32)
-    act(V("FLDE", 128, 256), ind(sxr(-256), V("EVL", 8, 16)))
-    cp(V("FLDE", 0, 128), ind(sxr(-256), V("EVL", 0, 8)))
+    shared("FLDE", 0, sxr(-256), "EVL", 0, 256)
     wrap("SOB", 0, V("FLDE"))
     listed(V("NL0"), "SOB", 0, 256, -1.25)
-    cp(ind(V("BN0"), V("NL0")), V("IDL"))
+    cp(ind(V("BN0"), V("NL0")), V("PAY"))
 
     def send(r):
         h, u = HS[r], FOLD_V[r]
-        wrap("SO4", 0, V("BN%d" % r, 1, 2 * h, 2), "CP4")
-        by_fours(V("FL", 0, h // 4), "SO4", 0, h, c4t)
+        wrap("SO5", 0, V("BN%d" % r, 1, 2 * h, 2), "CP4")
+        by_fours(V("FL", 0, h // 4), "SO5", 0, h, c4t)
         act(V("ft", 16 * u, 4 * h), ind(V("fc", 0, 8 * h), V("FL", u, h // 4)), scale=0.5)
         if u:
             ts(V("ft", 0, 16 * u), ind(V("fc", 0, 8 * h), V("FL", 0, u)), 0.5, A.mult)
@@ -456,80 +505,75 @@ def rank_program(g, core, T, topo):
         h, bn = HS[r], "BN%d" % r
         c = h // 16
         wrap("SOA", 0, V(bn, 1, 2 * h, 2))
-        if r < 2:
-            wrap("SOA", h, V(bn, 0, 2 * h, 2))
-        listed(V("JL", 0, c if r == 2 else 2 * c), "SOA", 0, h if r == 2 else 2 * h)
-        odd = V("JL", 0, c)
-        act(V("SN", 0, h), ind([sr, V("LT1", 128, 256), V("LT2", 64, 128)][r], odd))
+        ts(V("JX", 0, c), ends("SOA", 0, h), 2.0, A.mult, col(cX), A.add)
+        listed(V("JL", 0, c), "SOA", 0, h)
+        ts(V("JX", 8, 8 + c), ends("SOA", 0, h), 2.0, A.mult, col(cY), A.add)
+        odd, both, left = V("JL", 0, c), V("JX", 0, c), V("JX", 8, 8 + c)
+        act(V("G1", h, 2 * h), ind(V("AJ", 0, 4 * h), both))
+        act(V("G1", 2 * h, 3 * h), ind(V("BJ", 0, 4 * h), both))
         if r == 0:
-            act(V("SN", h, 2 * h), ind(lw(PARN), odd))
+            lin("GN", V("G1", 0, h), ind(lw(PARN), odd), 1.0, 256.0)
         else:
-            act(V("SN", h, 2 * h), ind(V("LP%d" % r, 2 * h, 4 * h), odd), bias=-256.0)
-        if r == 1:
-            act(V("SN", 2 * h, 3 * h), ind(V("LP1", 0, 128), V("JL", c, 2 * c)), bias=-256.0)
-        n = 3 * c if r == 1 else 2 * c
-        wrap("SOD", 0, V("SN", 0, 16 * n))
-        listed(V("SL", 0, n), "SOD", 0, 16 * n, 256)
-        sl, nl, o = V("SL", 0, c), V("SL", c, 2 * c), (2 + r) * h
-        cp(ind(V("RESW", 256, 512), nl), V("KV", 0, h))
-        act(V("G1", o, o + h), ind(kids(256, 768), sl))
-        act(V("G1", 0, h), ind(V("SGX", 272, 528), nl))
-        act(V("G1", h, 2 * h), ind(tw(TW0, 512), sl))
-        for j in range(r):
-            act(V("G1", (2 + j) * h, (3 + j) * h), ind(tw([TW1, T2S][j]), nl))
-        lin("OV", V("OX", 528, 528 + h), V("G1", o, o + h))
-        lin("RESD", V("RESW", 512, 768), V("RESW", 256, 512))
-        wrap("SOB", 0, V("G1", 0, o + h))
-        side, shift = ends("SOB", h, h), [1, None, -1][r]
-        for j in range(r):
-            tt(V("DL", 8 * j, 8 * j + c), side, ends("SOB", (2 + j) * h, h), A.subtract)
-            side = V("DL", 8 * j, 8 * j + c)
-        if r == 0:
-            lin("LAM", V("LAM", 0, c), side, 1.0, ch(1))
-        else:
-            act(V("LAM", 0, c), side, bias=ch(shift) if shift else 0.0, f=AF.Abs)
-        lin("L768", V("L768", 0, c), V("LAM", 0, c), 768.0)
-        lin("ABO", V("AB", c, 2 * c), ends("SOB", o, h), 1.0, ch(1))
-        lin("ABT", V("AB", 2 * c, 3 * c), ends("SOB", 0, h), 1.0, col(cT))
-        tt(V("AB", 0, c), V("AB", c, 2 * c), V("L768", 0, c), A.add)
-        tt(V("AB", 3 * c, 4 * c), V("AB", 2 * c, 3 * c), V("LAM", 0, c), A.mult)
-        cp(V("ABL", 0, 4 * c), V("AB", 0, 4 * c))
-        act(V("G1", o + h, o + 3 * h), ind(res, V("ABL", 0, 2 * c)), f=AF.Abs)
-        act(V("PB", 0, 2 * h, 2), ind(res, V("ABL", 3 * c, 4 * c)), f=AF.Relu)
-        wrap("SOE", 0, V("G1", o + h, o + 3 * h))
-        listed(V("L1", 0, 2 * c), "SOE", 0, 2 * h)
-        act(V("PB", 1, 2 * h, 2), ind(oxw, V("L1", 0, c)))
-        wrap("SOF", 0, V("G1", o, o + 2 * h), "CP4")
-        by_fours(V("L5", 0, h // 2), "SOF", 0, 2 * h, c4t)
+            lin("GN", V("G1", 0, h), ind(V("LP%d" % r, 2 * h, 4 * h), odd))
+        other = V("G1", 3 * h, 4 * h)
+        lin("GO", other, ind(V("AJ", 0, 4 * h), left), 1.0, -512.0)
+        wrap("SOB", 0, V("G1", 0, 3 * h))
+        listed(V("UL3", 0, 3 * c), "SOB", 0, 3 * h)
+        cp(ind(V("RESW", 256, 512), V("UL3", 0, c)), V("KV", 0, h))
+        cp(ind(V("RES2", 256, 512), V("UL3", 0, c)), other)
+        wrap("SOF", 0, other, "CP4")
+        by_fours(V("L5", 0, h // 4), "SOF", 0, h, c4t)
+        act(V("GL", 0, h), ind(res, V("UL3", c, 2 * c)), f=AF.Abs)
+        act(V("PB", 0, 2 * h, 2), ind(res, V("UL3", 2 * c, 3 * c)), f=AF.Relu)
+        act(V("PB", 1, 2 * h, 2), ind(res2, V("UL3", c, 2 * c)))
+        wrap("SON", 0, V("GL", 0, h), "CP4")
+        by_fours(V("L5", h // 4, h // 2), "SON", 0, h, c4t)
         wrap("SOI", 0, V("PB", 0, 2 * h), "CP8")
         by_fours(V("L5", h // 2, 3 * h // 4), "SOI", 0, 2 * h, c4t, 8)
+        act(V("G1", 4 * h, 5 * h), ind(V("TJ", 0, 2 * h), odd), bias=256.0)
+        n = 5 * h
+        if r < 2:
+            act(V("G1", 5 * h, 6 * h), ind(V("BJ", 0, 4 * h), left))
+            act(V("GT", 0, h), ind(V("TJ", 0, 2 * h), odd))
+            wrap("SOA", h, V(bn, 0, 2 * h, 2))
+            listed(V("JL", c, 2 * c), "SOA", h, h)
+            act(V("LP%d" % (r + 1), 0, h), ind(V("LP1", 0, 128) if r else V("IDL"), V("JL", c, 2 * c)))
+            n = 6 * h
+        if r == 1:
+            act(V("G1", 6 * h, 7 * h), V("LP2", 0, h))
+            n = 7 * h
+        wrap("SOL", 0, V("G1", 3 * h, n))
+        listed(V("RL", 0, n // 16 - 3 * c), "SOL", 0, n - 3 * h)
 
     def relink(r):
         h = HS[r]
         c = h // 16
-        act(V("PA", 1, 2 * h, 2), ind(oxw, V("L1", c, 2 * c)))
-        cp(ind(kids(-256, 512), V("ABL", 2 * c, 3 * c)), V("PA", 1, 2 * h, 2))
+        act(V("PA", 1, 2 * h, 2), ind(res2, V("RL", 0, c)))
+        bits("SC", cp, ind(kids(0, 512), V("RL", c, 2 * c)), V("PA", 1, 2 * h, 2))
         if r < 2:
-            act(V("PA", 0, 2 * h, 2), ind(res, V("ABL", 2 * c, 3 * c)), f=AF.Relu)
+            act(V("PA", 0, 2 * h, 2), ind(res, V("RL", 2 * c, 3 * c)), f=AF.Relu)
             wrap("SOD", 0, V("PA", 0, 2 * h), "CP32")
             listed(V("STL", 0, c), "SOD", 0, 2 * h, run=32)
-            cp(ind(V("SGX", 16, 656), V("STL", 0, c)), V("G1", 0, h))
+            bits("SC", cp, ind(V("SGX", 16, 656), V("STL", 0, c)), V("GT", 0, h))
             lin("KIDD", kids(512, 768), kids(0, 256))
 
     def leaves(r):
         m = HS[r - 1]
         c = m // 16
         lt, lp = "LT%d" % r, "LP%d" % r
-        lid, par, now, at = (V("JL", 8, 16), 2 * m, m, 0) if r == 1 else (V("SL", 8, 12), 0, m, 56)
+        lid, par, now, at = (V("JL", 8, 16), 2 * m, m, 0) if r == 1 else (V("RL", 12, 16), 0, m, 56)
         act(V(lt, par, par + m), ind(lw(PARN), lid))
         act(V(lt, now, now + m), ind(sr, lid))
         act(V(lt, 2 * m - par, 3 * m - par), ind(lw(POSL), lid))
         wrap("SOE", 0, V(lt))
         listed(V("BL", at, at + 3 * c), "SOE", 0, 3 * m, 256)
-        lin("LP", V(lp, 0, m), V("BN0", 0, 256, 2)) if r == 1 else lin("LP", V(lp, 0, m), V("SN", 128, 192), 1.0, 256.0)
-        act(V(lp, m, 2 * m), ind(V("IDM"), V("BL", at + c, at + 2 * c)), bias=256.0)
-        wrap("SO4", 0, V(lp), "CP4")
-        by_fours(V("P4L", 0, m // 2), "SO4", 0, 2 * m, c4t)
+        slot = V("BL", at + c, at + 2 * c)
+        act(V(lp, m, 2 * m), ind(V("IDM"), slot), bias=256.0)
+        wrap("SO6", 0, V(lp), "CP4")
+        by_fours(V("P4L", 0, m // 2), "SO6", 0, 2 * m, c4t)
+        wrap("SOO", 0, V(lp, m, 2 * m))
+        listed(V("NLJ", 0, c), "SOO", 0, m)
+        ahead(r, slot, V("NLJ", 0, c))
 
     def update(r):
         h = HS[r]
@@ -548,37 +592,39 @@ def rank_program(g, core, T, topo):
     def number(r):
         m = HS[r - 1]
         c = m // 16
-        state(tw(TW1 if r == 1 else TW2, 255), A.is_gt)
+        t, bv, ev, lf, par, pos = (TW1, "BV1", m, 0, V("BL", 16, 24), V("BL", 0, 8)) if r == 1 else (TW2, "BVS", 0, 512, V("BL", 56, 60), V("BL", 64, 68))
+        state(tw(t, 255), A.is_gt)
         folds(r)
-        t, l0, ev, lf, pos = (TW1, 16, m, 0, V("BL", 0, 8)) if r == 1 else (T2S, 24, 0, 512, V("BL", 64, 68))
-        if r == 2:
-            tt(tw(T2S), tw(TW2), tw(SG1), A.mult)
-        tt(V("PROD", 0, 512 + m), ind(tw(t), V("BL", l0, l0 + 32 + c)), V("BV%d" % r), A.mult)
-        scan(V("SS"), V("one", 0, 512), V("PROD", ev, ev + 512), 0.0, A.mult, A.add)
-        tt(V("NUM", 0, m), ind(V("SS"), pos), V("PROD", lf, lf + m), A.add)
-        wrap("SOE", 0, V("NUM", 0, m), "CPJ")
-        listed(V("NL", 0, c), "SOE", 0, m)
-        cp(ind(V("BN%d" % r), V("NL", 0, c)), V("IDL", 0, m))
+        tt(V("PROD", 0, 512), ind(tw(t), V("BL", 24, 56)), V(bv, ev, ev + 512), A.mult)
+        tt(V("PROD", 512, 512 + m), ind(tw(t), par), V(bv, lf, lf + m), A.mult)
+        scan(V("SS"), V("one", 0, 512), V("PROD", 0, 512), 0.0, A.mult, A.add)
+        tt(V("PM", 0, m), ind(tw(t), V("NLJ", 0, c)), V("C1", 0, m), A.mult)
+        tt(V("PAY", 0, m), V("PM", 0, m), V("C0", 0, m), A.add)
+        tt(V("NUM", 0, m), ind(V("SS"), pos), V("PROD", 512, 512 + m), A.add)
+        wrap("SOQ", 0, V("NUM", 0, m), "CPJ")
+        listed(V("NL", 0, c), "SOQ", 0, m)
+        cp(ind(V("BN%d" % r), V("NL", 0, c)), V("PAY", 0, m))
 
     send(0)
     book(0)
-    tt(V("DD", 0, 256), sxr(256), V("DE", 256, 512), A.subtract)
+    bits("DX", tt, V("DX", 0, 256), sxr(256), V("DE", 256, 512), A.subtract)
     lin("AL", V("AL", 0, 256), sxr(0, 256), 0.5, 128.25)
-    lin("AL", V("AL", 256, 512), V("DD", 0, 256), 0.5, 128.25)
+    lin("AL", V("AL", 256, 512), V("DX", 0, 256), 0.5, 128.25)
     lin("RH", V("RH"), sxr(256), 1.0, 1024.0)
-    tt(V("DD", 256, 512), sxr(256), V("RH"), A.subtract)
-    cp(V("PARL"), V("SJ", 0, 16))
-    act(lw(POSL), ind(V("DD", 256, 512), V("PARL")), scale=2048.0, bias=2048.0 * 1024 - 256)
+    bits("DX", tt, V("DX", 256, 512), sxr(256), V("RH"), A.subtract)
+    act(lw(POSL), ind(V("DX", 256, 512), V("PARL", 0, 16)), scale=2048.0, bias=2048.0 * 1024 - 256)
     lin("PARD", lw(PARN + 512), lw(PARN + 256))
-    act(V("PE"), ind(lw(PARN + 256, 512), ordw))
-    wrap("SOG", 0, V("PE"))
+    bits("SS", act, V("PE"), ind(lw(PARN + 256, 512), ordw))
+    wrap("SOG", 0, V("PE"), apart=True)
     listed(V("BL", 24, 56), "SOG", 0, 512, 256)
-    act(V("AI"), ind(V("AL"), V("EVL", 32, 64)))
-    tt(lw(ALM), ind(V("AL"), V("EVL", 16, 32)), lw(LG), A.subtract)
-    tt(V("DT", 256, 512), ind(V("AL"), V("EVL", 32, 48)), V("AI", 256, 512), A.subtract)
+    bits("SS", act, V("AI"), ind(V("AL"), V("EVL", 32, 64)))
+    act(lw(AFL), ind(V("AL"), V("EVL", 16, 32)))
+    bits("TG", tt, V("DT", 256, 512), ind(V("AL"), V("EVL", 32, 48)), V("AI", 256, 512), A.subtract)
     lin("NEG", V("DT", 0, 256), V("DT", 256, 512), -1.0)
-    act(V("BV1", 128, 640), ind(V("DT"), ordw))
-    tt(V("BV1", 0, 128), ind(lw(ALM), V("JL", 8, 16)), V("WB", 384, 512), A.subtract)
+    bits("SS", act, V("BV1", 128, 640), ind(V("DT"), ordw))
+    tt(lw(ALM, 128), ind(lw(LG), V("JL", 8, 16)), V("W5", 896, 1024), A.add)
+    act(lw(ALM + 128, 128), ind(lw(AFL), V("JL", 8, 16)), bias=-256.0)
+    tt(V("BV1", 0, 128), lw(ALM + 128, 128), lw(ALM, 128), A.subtract)
     update(0)
     relink(0)
     leaves(1)
@@ -587,26 +633,27 @@ def rank_program(g, core, T, topo):
     send(1)
     book(1)
     lin("JTL", lw(JTL), V("FLDE"), 0.5, 127.5)
-    act(lw(AFL), ind(V("AL"), V("EVL", 16, 32)))
-    wrap("SOC", 0, V("AI"))
-    listed(V("AB2"), "SOC", 0, 512, -128)
+    wrap("SOP", 0, V("AI"), apart=True)
+    listed(V("AB2"), "SOP", 0, 512, -128)
     lin("SG1", tw(SG1), tw(TW1), -2.0, 1.0)
     for j, t in enumerate((AFL, JTL, LG)):
-        act(V("LU", 64 * j, 64 * j + 64), ind(lw(t), V("SL", 8, 12)))
-    wrap("SOA", 0, V("LU", 0, 128))
-    listed(V("LM"), "SOA", 0, 128, -128)
+        act(V("LU", 64 * j, 64 * j + 64), ind(lw(t), V("RL", 12, 16)))
+    wrap("SOR", 0, V("LU", 0, 128))
+    listed(V("LM"), "SOR", 0, 128, -128)
     cp(ind(V("ALV"), V("LM", 4, 8)), V("one", 0, 64))
     scan(V("CNT", 1, 129), V("one", 0, 128), V("ALV"), 0.0, A.mult, A.add)
     cn = V("CNT", 0, 129)
     act(V("MR"), ind(cn, V("AB2", 16, 32)))
     tt(V("BLJ"), ind(cn, V("LM", 4, 8)), V("LU", 128, 192), A.add)
-    tt(V("DT2", 256, 512), ind(cn, V("AB2", 0, 16)), V("MR"), A.subtract)
+    bits("TG", tt, V("DT", 0, 256), ind(cn, V("AB2", 0, 16)), V("MR"), A.subtract)
+    bits("TG", tt, V("DT2", 256, 512), ind(tw(SG1), V("PARL", 16, 32)), V("DT", 0, 256), A.mult)
     tt(V("BV2", 512, 576), ind(cn, V("LM", 0, 4)), V("BLJ"), A.subtract)
     lin("NEG", V("DT2", 0, 256), V("DT2", 256, 512), -1.0)
-    act(V("BV2", 0, 512), ind(V("DT2"), ordw))
+    bits("SS", act, V("BVS", 0, 512), ind(V("DT2"), ordw))
     update(1)
     relink(1)
     leaves(2)
+    tt(V("BVS", 512, 576), ind(tw(SG1), V("BL", 56, 60)), V("BV2", 512, 576), A.mult)
 
     number(2)
     send(2)
@@ -625,18 +672,20 @@ def rank_program(g, core, T, topo):
     for k in range(4):
         dma("y", T.osc[4 * k:4 * k + 4, :], T.sx[32 * k:32 * k + 4, :], "outa", [V("sx")[1]], [], 1.9)
     relink(2)
-    fill(kids(512, 1024), -1)
-    ts(tw(SGR), V("RESW", 256, 512), 0.0, A.is_gt, 512.0, A.mult)
-    wrap("SOG", 0, tw(TW1, 512))
+    ts(tw(SGR), V("RESW", 256, 512), 0.0, A.is_gt, 768.0, A.mult)
+    wrap("SOK", 0, tw(TW0))
+    wrap("SOK", 512, tw(TW1))
+    wrap("SOG", 0, tw(TW2))
     wrap("SOK", 256, tw(SGR), "CPJ")
-    tt(V("KW", 0, 16), V("TWW"), ends("SOG", 0, 256), A.subtract)
-    tt(V("KW", 16, 32), V("KW", 0, 16), ends("SOG", 256, 256), A.subtract)
-    act(V("KW", 0, 16), V("KW", 16, 32), scale=256.0, bias=ch(-512), f=AF.Abs)
+    tt(V("KW", 64, 80), ends("SOK", 0, 256), ends("SOK", 512, 256), A.subtract)
+    act(V("KW", 0, 16), V("KW", 64, 80), f=AF.Abs)
+    tt(V("KW", 16, 32), V("KW", 0, 16), ends("SOG", 0, 256), A.subtract)
+    act(V("KW", 0, 16), V("KW", 16, 32), scale=256.0, bias=ch(-256), f=AF.Abs)
     tt(V("KW", 32, 48), ends("SOK", 256, 256), V("KW", 0, 16), A.subtract)
     tt(V("KW", 48, 64), ends("SOK", 256, 256), V("KW", 0, 16), A.add)
     ts(V("KLL", 0, 16), V("KW", 32, 48), ch(1), A.add, 256.0, A.add)
     ts(V("KLL", 16, 32), V("KW", 48, 64), ch(1), A.add)
-    act(V("KID"), ind(kids(0, 1024), V("KLL")))
+    act(V("KID"), ind(V("KIDS"), V("KLL")))
     klo = PLACE["KID"][1]
     dma("y", T.kid[:], T.f32[0:128:16, klo:klo + 512], "outa", [V("KID")[1]], [], 1.9)
 

@@ -1,10 +1,14 @@
+import numpy as np
 from concourse.mybir import dt, AluOpType, ActivationFunctionType
 
 A = AluOpType
 AF = ActivationFunctionType
-BIG, HUGE, MAGIC, EPS = 1024.0, 2048.0, 12582912.0, 1.0 / 2048
+BIG, HUGE, EPS = 1024.0, 2048.0, 1.0 / 4096
+TOUR, PAIRED, HALVES = [0, 256, 512], (1, 2), (0, 1, 2)
+SHARE = {"OC": 8, "DD": 8, "FLDE": 8}
 WAKE, SOON, PASSES, ORDER = 0.22, (0.4, 0.5, 0.6, 0.7, 0.8, 0.9), 6, {}
-IFIX, VFIX, SFIX, CYC, GAT, SCA, PECOL = 0.055, 0.015, 0.04, 0.00095, 0.0015, 0.0033, 0.0007
+IFIX, VFIX, SFIX, SLOW, WEIGHT, MIX = 0.055, 0.015, 0.04, 1.35, (0.6, 0.4), (0.1, 0.2, 0.3, 0.4, 0.5)
+CYC, GAT, SCA, PECOL = [np.array(x) for x in ([0.00085, 0.0011], [0.0011, 0.0021], [0.0022, 0.005], [0.0006, 0.001])]
 FLIGHT = [2.0, 1.5, 1.5]
 HS = [128, 64, 32]
 LOFF = [0, 128, 192]
@@ -14,12 +18,12 @@ OUT, BASE = [], [512]
 for _k in range(8):
     OUT.append(BASE[-1] + 512)
     BASE.append(OUT[-1] + 16 * CH[_k])
-LANES = [[("v", 0), ("s", 8), ("v", 18), ("s", 24)], [("v", 0), ("v", 8), ("s", 16)]]
-PIECE = {"PAY": 96, "DX": 96, "TG": 128, "SC": 64, "WR": 256, "SG": 128}
-FOLD_V, RELU_V, YB_V = [16, 8, 4], 2, 1
+LANES = [[("v", 0), ("s", 8), ("v", 18), ("s", 24)], [("v", 0), ("v", 8), ("s", 22)]]
+PIECE = {"PAY": 96, "DX": 96, "TG": 128, "SC": 128, "WR": 256, "SG": 128, "SS": 256, "U0": 256, "U1": 128, "U2": 128, "PR": 512, "OUT": 128, "FL": 128}
+FOLD_V, RELU_V, YB_V = [12, 8, 4], 2, 1
 LEFT = 0.1875
-ON_V = {"NEG", "SG1", "GN", "GO"}
-PARTS = [8, 4, 2]
+ON_V = {"NEG", "SG1", "GN", "GO", "CP", "NF", "PARD"}
+PARTS = [8, 2, 1]
 
 ARENA = {"f32": [], "b16": [], "u16": [], "i32": [], "h16": []}
 PLACE = {}
@@ -32,24 +36,24 @@ def _al(kind, **kw):
         PLACE[n] = (kind, lo, w)
 
 
-_al("f32", OX=528, RESW=1024, RES2=1024, KIDS=1280, COL=16, MUL=8, CM=8, PF=8, C32=32, C32a=32, C32b=32, KV=128, MM=32, KP=32, YW=32, UF=32, IW=32,
-    WBS=96, DE=512, DD=512, DX=512, SX=1040, L256=32, EV=64, KW=80, KID=512, BN0=256, BN1=128, BN2=64, SOA=256,
+_al("f32", OX=528, RESW=1024, KIDS=1280, COL=16, MUL=8, CM=8, PF=8, C32=32, C32a=32, C32b=32, KV=128, MM=32, KP=32, YW=32, UF=32, IW=32,
+    WBS=96, DQ=80, DE=512, DD=528, DX=256, SX=1040, L256=32, EV=64, KW=80, KID=512, BN0=256, BN1=128, BN2=64, SOA=256,
     OJ=256, TOPJ=256, AJ=512, BJ=512, PAY=256, C0=256, C1=128, CL=256, PM=128)
-_al("b16", CPH=576, CP4=256, CP8=256, CP32=256, WB=BASE[8] + 512, OC=256, SGX=656, TWB=1536, NFX=256, W5=1280, W6=768, VV=512, IDM=512,
+_al("b16", CPH=576, CP4=256, CP8=256, CP64=512, GT=272, SEL=128, PA=512, WB=BASE[8] + 512, OC=256, SGX=528, TWB=2560, LN=128, NFX=256, W5=1280, ALT=512, VV=512, IDM=512,
     LW=2304, AL=512, DT=512, DT2=512, AI=512, PE=512, IDL=256, BV1=640, BV2=576, BVS=576, PROD=640, SS=512, TJ=256, XJ=64, DJ=64,
-    LT1=384, LT2=192, LU=192, LP1=256, LP2=128, BLJ=64, ALV=128, CNT=144, MR=256, NUM=128)
-_al("h16", SOH=576, SOT=576, SOG=512, SO4=256, SO5=128, SO6=256, SOB=384, SOC=512, SOD=256, SOE=384, SOF=256, SOI=256, SOK=768, SOL=384, SOM=128, SON=128, SOO=128,
-    SOP=512, SOQ=128, SOR=256, RH=256, CPJ=256, FLDE=256, G1=768, GL=128, GZ=16, GT=128, PA=256, PB=256)
+    LT1=256, LT2=128, LU=192, LP1=256, LP2=128, BLJ=64, ALV=128, CNT=144, MR=256, NUM=128)
+_al("h16", SOH=576, SOT=576, SOG=512, SO4=256, SO5=128, SO6=256, SOB=384, SOC=512, SOD=512, SOE=384, SOF=256, SOI=256, SOK=768, SOL=384, SOM=128, SON=128, SOO=128,
+    SOP=512, SOQ=128, SOR=256, SOU=256, RH=256, CPJ=256, FLDE=256, G1=640, GL=128, SOS=128, PB=256)
 _al("u16", QL=36, UL=8, KL16=32, UN=96, LB=16, PARL=32, S0L=32, LS0=40, LS1=40, LS2=40, LS3=40, ORDW=40, EVL=64, P4L=64, NL0=16, FL=32, JL=16, JX=16,
-    UL3=24, RL=24, NLJ=8, TLJ=8, L5=96, STL=8, BL=68, NL=8, AB2=32, LM=8, KLL=32)
+    UL3=24, RL=24, NLJ=8, TLJ=8, L5=96, STL=16, BL=68, NL=8, AB2=32, LM=8, KLL=32)
 _al("i32", QI=48, QJ=36, J32=32, J32c=32, UI=8, SI=32, SJ=32)
 
 C4, U8 = "float8_e4m3fn_x4", "uint8"
 SCRATCH = {"f32": ("sbuf", [128, sum(ARENA["f32"])], "float32"), "b16": ("sbuf", [128, sum(ARENA["b16"])], "bfloat16"),
            "h16": ("sbuf", [128, sum(ARENA["h16"])], "float16"), "u16": ("sbuf", [128, sum(ARENA["u16"])], "uint16"),
            "i32": ("sbuf", [128, sum(ARENA["i32"])], "int32"), "ki": ("sbuf", [128, 32], "int32"), "yb": ("sbuf", [128, 512], "float32"),
-           "pd": ("psum", [128, 2048], "float32"), "pp": ("psum", [128, 1024], "float32")}
-for _n, _w in dict(xt=2560, ut=512, vt=512, one=528, zt=528, hz=512, uu=512, fg=512, ft=512, fc=1024).items():
+           "pd": ("psum", [128, 3072], "float32"), "pp": ("psum", [128, 1024], "float32")}
+for _n, _w in dict(xt=2560, ut=512, vt=512, one=528, zt=528, hz=528, vv=1024, uu=1024, fg=1024, ft=512, fc=1024).items():
     SCRATCH[_n] = ("sbuf", [128, _w], "bfloat16")
 for _c, _s, _w in [("qx", "sx", 512), ("qe", "se", 512), ("qw", "sw", 512), ("qu", "su", 128), ("qup", "sup", 128), ("qv", "sv", 128),
                    ("qf", "sf", 384), ("lq", "ls", 224)]:
@@ -82,13 +86,43 @@ def schedule(prog):
     for i, d in enumerate(pred):
         for j in sorted(d):
             succ[j].append(i)
-    queue, cost, lat = [q[0] for q in prog], [q[6] for q in prog], [q[7] for q in prog]
+    queue = [q[0] for q in prog]
+    costs = [[float((q[6] + 0 * CYC)[m]) for q in prog] for m in range(2)]
+    lats = [[q[7] * (SLOW if m and q[7] > 0 else 1.0) for q in prog] for m in range(2)]
 
-    def place(prio, back, soon):
+    def length(order):
+        total = 0.0
+        for cost, lat, weight in zip(costs, lats, WEIGHT):
+            free, fin = {}, [0.0] * n
+            for i in order:
+                t = max([free.get(queue[i], 0.0)] + [fin[j] for j in pred[i]])
+                free[queue[i]], fin[i] = t + cost[i], t + cost[i] + lat[i] + WAKE
+            total += weight * max(fin)
+        return total
+
+    def place(prio, back, soon, cost, lat):
         before, after = (succ, pred) if back else (pred, succ)
         left = [len(d) for d in before]
         ready = [i for i in range(n) if not left[i]]
         at, free, start, order, end = [lat[i] if back else 0.0 for i in range(n)], {}, [0.0] * n, [], 0.0
+        while ready and soon < 0:
+            i = max(ready, key=lambda i: (prio[i], -i))
+            ready.remove(i)
+            t, slots = at[i], free.setdefault(queue[i], [])
+            for a, b in slots:
+                if a >= t + cost[i] + soon:
+                    break
+                t = max(t, b)
+            slots.append((t, t + cost[i]))
+            slots.sort()
+            start[i] = t
+            for j in after[i]:
+                at[j] = max(at[j], t + cost[i] + lat[j if back else i] + WAKE)
+                left[j] -= 1
+                if not left[j]:
+                    ready.append(j)
+            if not ready:
+                order = sorted(range(n), key=lambda i: (start[i], i))
         while ready:
             done, e = min((max(at[i], free.get(queue[i], 0.0)) + cost[i], queue[i]) for i in ready)
             t = max(free.get(e, 0.0), min(at[i] for i in ready if queue[i] == e))
@@ -104,18 +138,21 @@ def schedule(prog):
                 if not left[j]:
                     ready.append(j)
         return start, end, order
-    rest = [0.0] * n
-    for i in range(n - 1, -1, -1):
-        rest[i] = cost[i] + lat[i] + max([rest[j] + WAKE for j in succ[i]] + [0.0])
     best = None
-    for soon in SOON:
-        prio = rest
-        for _ in range(PASSES):
-            start, end, order = place(prio, False, soon)
-            if best is None or end < best[0]:
-                best = (end, order)
-            rev = place([start[i] + cost[i] + lat[i] for i in range(n)], True, soon)[0]
-            prio = [rev[i] + cost[i] for i in range(n)]
+    for mix in MIX:
+        cost, lat = [[(1 - mix) * a + mix * b for a, b in zip(*x)] for x in (costs, lats)]
+        rest = [0.0] * n
+        for i in range(n - 1, -1, -1):
+            rest[i] = cost[i] + lat[i] + max([rest[j] + WAKE for j in succ[i]] + [0.0])
+        for soon in SOON:
+            prio = rest
+            for _ in range(PASSES):
+                start, end, order = place(prio, False, soon, cost, lat)
+                end = length(order)
+                if best is None or end < best[0]:
+                    best = (end, order)
+                rev = place([start[i] + cost[i] + lat[i] for i in range(n)], True, soon, cost, lat)[0]
+                prio = [rev[i] + cost[i] for i in range(n)]
     ORDER[n] = best[1]
     return ORDER[n]
 
@@ -163,7 +200,7 @@ def rank_program(g, core, T, topo):
         if fn is None:
             note(log, [r for r in acc if r[3]], (sem, inc))
             return
-        deps = {}
+        deps, acc = {}, [r for r in acc if r[0] != "order"]
         for r in acc:
             for x in log.get(r[0], []):
                 if meets(r[1:], x):
@@ -229,7 +266,7 @@ def rank_program(g, core, T, topo):
 
     def quant(q, s, a, b, src):
         o1, o2 = V(q, a, b), V(s, a, b)
-        op("v", lambda: g.vector.quantize_mx(o1[0], o2[0], src[0]), [src[1]], [o1[1], o2[1]], cost=0.04 + 0.0009 * (b - a))
+        op("v", lambda: g.vector.quantize_mx(o1[0], o2[0], src[0]), [src[1]], [o1[1], o2[1]], cost=0.02 + 1.06 * CYC * (b - a))
 
     def mm(out, lq, ls, la, rq, rs, ra, rb):
         x = [V(lq, la, la + 128), V(ls, la, la + 128), V(rq, ra, rb), V(rs, ra, rb)]
@@ -241,6 +278,9 @@ def rank_program(g, core, T, topo):
     def wrap(out, at, data, pat="CPH", apart=False):
         n = data[2]
         bits("WR" if apart else None, scan, V(out, at, at + n), data, V(pat, 0, n), -HUGE, A.max, A.add)
+
+    def counted(out, rising, small):
+        scan(out, rising, small, -HUGE, A.max, A.add)
 
     def ends(buf, a, n, run=16):
         return V(buf, a + run - 1, a + n, run)
@@ -263,12 +303,12 @@ def rank_program(g, core, T, topo):
 
     def by_fours(out, buf, a, n, c, run=4):
         ts(out, ends(buf, a, n, run), 4.0, A.mult, col(c), A.add)
-    cH, cW1, cX, c4r, c4t, c4u, cY = 0, 1, 4, 5, 6, 7, 8
+    cH, cW1, cX, c4r, c4t, c4u, cY, c8t = 0, 1, 4, 5, 6, 7, 8, 9
     NF0, TW1, TW2, SGR, SG1 = [256 * j for j in range(1, 6)]
-    TW0 = 0
+    TW0, FLIP = 0, [0, 1536, 2048]
     ALM, JTL, AFL, POSL, LG, PARN = 0, 256, 512, 768, 1024, 1536
     idw, iow, xw = V("WB", 0, 512), V("IW", 0, 16), V("xt", 0, 2048)
-    sr, res, res2 = V("SGX", 16, 528), V("RESW"), V("RES2")
+    sr, res = V("SGX", 16, 528), V("RESW")
 
     def sxr(a=0, b=512):
         return V("SX", 528 + a, 528 + b)
@@ -300,21 +340,26 @@ def rank_program(g, core, T, topo):
     scan(idw, V("one", 0, 512), V("one", 0, 512), -257.0, A.mult, A.add)
     op("g", lambda: g.affine_select(T.zt[:, 0:516], T.one[:, 0:516], [[-1, 516]], A.is_equal, 0.0, 3, 4), [V("one", 0, 516)[1]], [V("zt", 0, 516)[1]], cost=1.1)
     iota(V("OX", 0, 528), [[1, 528]], -16)
-    fill(V("SGX", 527, 656), -1)
+    fill(V("SGX", 527, 528), -1)
     fill(V("TWB", 255, 1536, 256), 0)
     fill(V("NFX", 255, 256), 256)
     iota(V("W5", 768, 1024), [[1, 256]], -256)
     iota(V("IDM"), [[0, 2], [1, 256]], -256)
     iota(V("IDL"), [[1, 256]], 0)
     iota(V("RESW"), [[0, 2], [-1, 512]], 0)
-    iota(V("RES2"), [[0, 2], [1, 512]], 0)
+    fill(V("hz", 0, 4), 0)
+    iota(V("ALT"), [[0, 256], [1, 2]], 0)
+    fill(V("DD", 15, 16), 0)
+    fill(V("GT", 128, 272), 0)
+    iota(V("PA", 2, 512, 4), [[1, 128]], 0)
+    fill(V("PA", 3, 512, 4), 0)
     fill(V("BJ", 0, 512, 2), 0)
     fill(kids(768, 1280), -1)
     iota(V("KV"), [[1, 128]], 512)
     fill(V("CNT", 0, 1), 0)
     fill(V("ALV"), 0)
     fill(V("CP8", 0, 256, 2), 0)
-    fill(V("CP32", 0, 256, 2), 0)
+    fill(V("CP64"), 0)
     ts(V("QI", 0, 36), V("QJ"), 15, A.bitwise_and)
     ts(V("J32c"), V("J32"), 15, A.bitwise_and)
     cp(V("QL"), V("QI", 0, 36))
@@ -328,7 +373,7 @@ def rank_program(g, core, T, topo):
     cp(V("UL"), V("UI"))
     act(V("IW"), V("UF"), bias=pf(0))
     act(col(cH), V("C32a", 15, 16), scale=-1.0, bias=-BIG)
-    act(V("CPH"), ind(V("C32", 0, 16), V("QL", 0, 36)))
+    bits("SS", act, V("CPH"), ind(V("C32", 0, 16), V("QL", 0, 36)))
     act(V("CM", 0, 3), V("MUL", 0, 3), scale=col(cH))
     for k in (1, 2, 3):
         act(col(cW1 + k - 1), pf(2 + k), scale=BASE[k] / (1 << k), bias=col(cH))
@@ -337,9 +382,10 @@ def rank_program(g, core, T, topo):
     act(col(c4r), V("C32a", 19, 20), scale=-1.0, bias=-BIG)
     act(col(c4t), col(c4r), scale=4.0, bias=pf(1))
     act(col(c4u), col(c4t), bias=1024.0)
+    act(col(c8t), col(c4t), scale=2.0, bias=1.0)
     act(V("CP4"), ind(V("C32", 16, 32), V("QL", 0, 16)))
     lin("CP", V("CP8", 1, 256, 2), V("CP4", 0, 128))
-    lin("CP", V("CP32", 1, 256, 2), V("CPH", 0, 128))
+    lin("CP", V("CP64", 3, 512, 4), V("CPH", 0, 128))
     lin("CPJ", V("CPJ"), V("CPH", 0, 256))
     tt(V("CPJ", 15, 256, 16), V("CPH", 15, 256, 16), iow, A.add)
     ts(V("LS0", 0, 1), pf(2), float(BASE[0]), A.mult, 511.0, A.add)
@@ -356,7 +402,7 @@ def rank_program(g, core, T, topo):
     quant("qv", "sv", 0, 128, V("vt"))
     act(V("sup"), ind(V("su"), V("UL")), f=AF.Copy)
     u_ = V("UL")
-    op("v", lambda: g.vector.tensor_copy(T.qup[:, 0:128].bitcast(dt.uint32), T.qu[:, 0:128].bitcast(dt.uint32).indirect(u_[0])), [V("qu")[1], u_[1]], [V("qup")[1]], cost=0.24)
+    op("v", lambda: g.vector.tensor_copy(T.qup[:, 0:128].bitcast(dt.uint32), T.qu[:, 0:128].bitcast(dt.uint32).indirect(u_[0])), [V("qu")[1], u_[1]], [V("qup")[1]], cost=IFIX + 128 * GAT)
     nb, na, eb, ea = V("WBS", 64, 80), V("WBS", 80, 96), V("WBS", 32, 48), V("WBS", 48, 64)
     ts(V("MM"), V("ki"), 256.0, A.is_ge)
     ts(V("WBS", 64, 96), V("ki"), 256.0, A.is_lt)
@@ -365,34 +411,36 @@ def rank_program(g, core, T, topo):
     tt(V("YW", 0, 16), nb, ea, A.mult)
     tt(V("YW", 16, 32), na, eb, A.mult)
     tt(V("WBS", 0, 32), V("KP"), V("YW"), A.add)
-    cp(V("UN", 32, 96), V("WBS", 32, 96))
+    cp(V("UN", 32, 64), V("WBS", 32, 64))
     cp(V("UN", 0, 32), V("WBS", 0, 32))
     act(V("W5", 512, 768), ind(idw, V("UN", 48, 64)))
     act(V("W5", 1024, 1280), ind(idw, V("UN", 32, 48)))
     act(V("W5", 0, 512), ind(idw, V("UN", 0, 32)))
-    bits("SS", act, V("W6", 0, 512), ind(V("IDL"), V("UN", 64, 96)))
-    lin("W6", V("W6", 512, 768), V("W6", 0, 256))
 
-    def state(turns, *how):
+    def state(r, turns, *how):
         quant("qx", "sx", 256, 512, V("xt", 1024, 2048))
         mm(V("pp", 0, 256), "qup", "sup", 0, "qx", "sx", 256, 512)
         quant("qx", "sx", 0, 256, V("xt", 0, 1024))
         ts(turns, V("pp", 0, 255), 0.0, *how)
-        for b in range(4):
-            mm(V("pd", 512 * b, 512 * b + 512), "qe", "se", 128 * b, "qx", "sx", 0, 512)
-            bits("EV", act, V("xt", b, 2048, 4), V("pd", 512 * b, 512 * b + 512), f=AF.Copy)
+        for j, (lo, hi) in enumerate([(256, 512), (0, 256)] if r in HALVES else [(0, 512)]):
+            for b in range(4):
+                p = V("pd", 512 * ((4 * j + b) % 6), 512 * ((4 * j + b) % 6) + hi - lo)
+                mm(p, "qe", "se", 128 * b, "qx", "sx", lo, hi)
+                act(V("xt", 4 * lo + b, 4 * hi, 4), p, f=AF.Copy)
 
-    state(V("NFX", 0, 255), A.is_le, 256.0, A.mult)
+    state(0, V("NFX", 0, 255), A.is_le, 256.0, A.mult)
     wrap("SOR", 0, V("NFX"), "CPJ")
     listed(V("LB"), "SOR", 0, 256)
-    wrap("SOG", 0, sr)
-    listed(V("S0L"), "SOG", 0, 512, 256)
+    for a in (256, 0):
+        wrap("SOG", a, V("SGX", 16 + a, 272 + a))
+        listed(V("S0L", a // 16, a // 16 + 16), "SOG", a, 256, 256)
     act(V("VV", 256, 512), ind(V("W5", 768, 1280), V("LB")))
     cp(V("VV", 0, 256), ind(V("W5", 512, 1024), V("LB")))
     act(V("WB", BASE[0] + 256, BASE[0] + 512), ind(V("W5", 0, 512), V("LB")))
     cp(V("WB", BASE[0], BASE[0] + 256), ind(V("VV"), V("S0L", 16, 32)))
-    wrap("SOH", 0, V("WB", BASE[0], BASE[0] + 512))
-    listed(V("LS0", 1, 33), "SOH", 0, 512, 256 + BASE[0])
+    for a in (256, 0):
+        wrap("SOH", a, V("WB", BASE[0] + a, BASE[0] + a + 256))
+        listed(V("LS0", 1 + a // 16, 17 + a // 16), "SOH", a, 256, 256 + BASE[0])
     lin("TW0", tw(TW0), V("NFX"), -1.0 / 256, 1.0)
     lin("TW0", tw(NF0), V("NFX"), 1.0 / 256)
     bits("SS", act, lw(LG, 512), ind(tw(TW0, 512), V("S0L")))
@@ -407,8 +455,14 @@ def rank_program(g, core, T, topo):
     tt(V("EV", 16, 48), V("SJ"), V("L256"), A.subtract)
     tt(V("EV", 48, 64), iow, V("L256", 16, 32), A.subtract)
     ts(V("EVL"), V("EV"), 256.0, A.add)
-    for j in range(2):
-        act(V("DE", 256 * j, 256 * j + 256), ind(V("W6", 256 - 256 * j, 768 - 256 * j), V("LB")), bias=EPS)
+    tt(V("DQ", 0, 16), ends("SOR", 0, 256), iow, A.subtract)
+    tt(V("DQ", 16, 32), nb, na, A.subtract)
+    ts(V("DQ", 32, 48), V("DQ", 0, 16), ch(1), A.add, 1.0 / 256, A.mult)
+    tt(V("DQ", 0, 16), V("DQ", 32, 48), V("DQ", 16, 32), A.mult)
+    tt(V("DQ", 48, 64), na, V("DQ", 0, 16), A.add)
+    tt(V("DQ", 64, 80), nb, V("DQ", 0, 16), A.subtract)
+    cp(V("UN", 64, 96), V("DQ", 48, 80))
+    bits("SS", act, V("DE"), ind(V("IDL"), V("UN", 64, 96)), scale=0.5, bias=EPS / 2)
     cp(V("PARL"), V("SJ"))
 
     def ahead(r, slot, parent):
@@ -419,19 +473,11 @@ def rank_program(g, core, T, topo):
         if r == 0:
             top = ind(lw(PARN + 256), parent)
             lin("CL", V("CL"), lw(LG), LEFT)
-            bits("PAY", tt, V("PAY"), V("CL"), V("IDL"), A.add)
+            counted(V("PAY"), V("IDL"), V("CL"))
         else:
             wrap("SOM", 0, V("TJ", 0, m))
             listed(V("TLJ", 0, m // 16), "SOM", 0, m, 256)
             top = ind(V("IDM"), V("TLJ", 0, m // 16))
-            if r == 1:
-                act(V("CL", 0, m), ind(tw(TW0, 512), slot), scale=LEFT)
-            else:
-                act(V("XJ"), ind(tw(TW0, 512), slot))
-                tt(V("DJ"), ind(tw(TW1), parent), V("XJ"), A.subtract)
-                act(V("CL", 0, m), V("DJ"), scale=LEFT, f=AF.Abs)
-            lin("C1", V("C1", 0, m), V("CL", 0, m), -2.0, LEFT)
-            tt(V("C0", 0, m), V("CL", 0, m), V("IDL", 0, m), A.add)
         act(V("BJ", 1, 2 * m, 2), top, bias=512.0)
     ahead(0, V("S0L", 0, 16), V("PARL", 0, 16))
 
@@ -439,11 +485,16 @@ def rank_program(g, core, T, topo):
         n = 8 * HS[r]
         w = n // PARTS[r]
         for a in range(0, n, w):
-            leaf, at = V("xt", a, a + w), 0
-            if r:
-                leaf, at = V("fg", a, a + w), n // 16
-                act(leaf, ind(V("xt", 0, 1024), V("P4L", a // 16, (a + w) // 16)))
-            tt(V("fc", a, a + w), ind(V("xt", 1024, 2048), V("P4L", at + a // 16, at + (a + w) // 16)), leaf, A.add)
+            if r == 0:
+                tt(V("fc", a, a + w), ind(V("xt", 1024, 2048), V("P4L", a // 16, (a + w) // 16)), V("xt", a, a + w), A.add)
+                continue
+            if r not in PAIRED:
+                act(V("fg", a, a + w), ind(V("xt", 0, 1024), V("P4L", a // 16, (a + w) // 16)))
+                tt(V("fc", a, a + w), ind(V("xt", 1024, 2048), V("P4L", (n + a) // 16, (n + a + w) // 16)), V("fg", a, a + w), A.add)
+                continue
+            for j in range(2):
+                act(V("fg", 2 * a + j, 2 * (a + w), 2), ind(V("xt", 1024 * j, 1024 * j + 1024), V("P4L", (j * n + a) // 16, (j * n + a + w) // 16)))
+            scan(V("fc", 2 * a, 2 * (a + w)), V("ALT", 0, 2 * w), V("fg", 2 * a, 2 * (a + w)), 0.0, A.mult, A.add)
     folds(0)
     for k in range(8):
         c, o, so = CH[k], OUT[k], "SOH" if k % 2 else "SOT"
@@ -463,32 +514,35 @@ def rank_program(g, core, T, topo):
                 at = c if k > 3 else 0
                 listed(V("ORDW", at + a, at + b), so, 16 * a, 16 * (b - a), 256)
 
-    def shared(out, a, win, lst, b, n):
-        act(V(out, a + n // 2, a + n), ind(win, V(lst, b + n // 32, b + n // 16)))
-        cp(V(out, a, a + n // 2), ind(win, V(lst, b, b + n // 32)))
+    def shared(out, a, win, lst, b, n, bias=0.0):
+        u = SHARE[out]
+        act(V(out, a + 16 * u, a + n), ind(win, V(lst, b + u, b + n // 16)), bias=bias)
+        ts(V(out, a, a + 16 * u), ind(win, V(lst, b, b + u)), bias, A.add)
     shared("OC", 0, V("WB", BASE[8], BASE[8] + 512), "ORDW", 0, 256)
-    wrap("SOR", 0, V("OC"))
-    listed(V("ORDW", 16, 32), "SOR", 0, 256, 256)
-    for c in range(2):
-        if c:
-            shared("DD", 256, V("DE"), "ORDW", 16, 256)
+    wrap("SOU", 0, V("OC"))
+    listed(V("ORDW", 16, 32), "SOU", 0, 256, 256)
+    for a, b in zip(TOUR, TOUR[1:]):
+        if a == 256:
+            shared("DD", 272, V("DE"), "ORDW", 16, 256)
         else:
-            act(V("DD", 0, 256), ind(V("DE"), V("ORDW", 0, 16)))
-        scan(V("SX", 16 + 256 * c, 272 + 256 * c), V("one", 0, 256), V("DD", 256 * c, 256 * c + 256), V("SX", 271, 272) if c else -EPS, A.mult, A.add)
-        cp(ind(sxr(), V("ORDW", 16 * c, 16 * c + 16)), V("SX", 16 + 256 * c, 272 + 256 * c))
+            act(V("DD", 16 + a, 16 + b), ind(V("DE"), V("ORDW", a // 16, b // 16)))
+        scan(V("SX", 16 + a, 16 + b), V("DD", 15 + a, 15 + b), V("DD", 16 + a, 16 + b), V("SX", 15 + a, 16 + a) if a else -EPS / 2, A.add, A.add)
+        cp(ind(sxr(), V("ORDW", a // 16, b // 16)), V("SX", 16 + a, 16 + b))
     ordw = V("ORDW", 0, 32)
-    shared("FLDE", 0, sxr(-256), "EVL", 0, 256)
+    shared("FLDE", 0, sxr(-256), "EVL", 0, 256, -0.5)
     wrap("SOB", 0, V("FLDE"))
-    listed(V("NL0"), "SOB", 0, 256, -1.25)
+    listed(V("NL0"), "SOB", 0, 256)
     cp(ind(V("BN0"), V("NL0")), V("PAY"))
 
     def send(r):
         h, u = HS[r], FOLD_V[r]
         wrap("SO5", 0, V("BN%d" % r, 1, 2 * h, 2), "CP4")
-        by_fours(V("FL", 0, h // 4), "SO5", 0, h, c4t)
-        act(V("ft", 16 * u, 4 * h), ind(V("fc", 0, 8 * h), V("FL", u, h // 4)), scale=0.5)
+        two = r in PAIRED
+        ts(V("FL", 0, h // 4), ends("SO5", 0, h, 4), 8.0 if two else 4.0, A.mult, col(c8t if two else c4t), A.add)
+        fc = V("fc", 0, 16 * h if two else 8 * h)
+        act(V("ft", 16 * u, 4 * h), ind(fc, V("FL", u, h // 4)), scale=0.5)
         if u:
-            ts(V("ft", 0, 16 * u), ind(V("fc", 0, 8 * h), V("FL", 0, u)), 0.5, A.mult)
+            ts(V("ft", 0, 16 * u), ind(fc, V("FL", 0, u)), 0.5, A.mult)
         quant("qf", "sf", 128 * r, 128 * r + 128, V("ft"))
         peer = T.cores[rank ^ STEP[r]]
         rid, pid, _ = topo.addr(peer)
@@ -499,7 +553,7 @@ def rank_program(g, core, T, topo):
            [V("qf", a, a + h)[1]], [[(arr, 0, 1, True, 1)]], sem="snt", inc=len(eng), mark=False, cost=0.2, lat=FLIGHT[r])
         op("g", lambda: g.remote_dma(T.ls[:, lo:lo + h], T.sf[:, a:a + h], T.sem[arr], T.sem.snt, pid, rid, mask),
            [V("sf", a, a + h)[1]], [[(arr, 1, 2, True, 1)]], sem="snt", inc=len(eng), mark=False, cost=0.2, lat=FLIGHT[r])
-        op("a", None, [[(arr, 0, 2, False, 1)]], [V("lq", lo, lo + h)[1], V("ls", lo, lo + h)[1]], sem=arr, inc=2 * len(topo.engines(peer, core)[:8]), cost=0.0)
+        op("a", None, [[(arr, 0, 2, False, 1)]], [V("lq", lo, lo + h)[1], V("ls", lo, lo + h)[1]], sem=arr, inc=2 * len(topo.engines(peer, core)[:8]), cost=0.0, lat=-WAKE)
 
     def book(r):
         h, bn = HS[r], "BN%d" % r
@@ -520,54 +574,61 @@ def rank_program(g, core, T, topo):
         wrap("SOB", 0, V("G1", 0, 3 * h))
         listed(V("UL3", 0, 3 * c), "SOB", 0, 3 * h)
         cp(ind(V("RESW", 256, 512), V("UL3", 0, c)), V("KV", 0, h))
-        cp(ind(V("RES2", 256, 512), V("UL3", 0, c)), other)
         wrap("SOF", 0, other, "CP4")
         by_fours(V("L5", 0, h // 4), "SOF", 0, h, c4t)
-        act(V("GL", 0, h), ind(res, V("UL3", c, 2 * c)), f=AF.Abs)
-        act(V("PB", 0, 2 * h, 2), ind(res, V("UL3", 2 * c, 3 * c)), f=AF.Relu)
-        act(V("PB", 1, 2 * h, 2), ind(res2, V("UL3", c, 2 * c)))
+        lin("PBO", V("PB", 0, 2 * h, 2), other)
+        act(V("GL", 0, h), ind(res, V("UL3", 2 * c, 3 * c)), bias=-511.0, f=AF.Relu)
+        act(V("PB", 1, 2 * h, 2), ind(res, V("UL3", c, 2 * c)), f=AF.Relu)
         wrap("SON", 0, V("GL", 0, h), "CP4")
         by_fours(V("L5", h // 4, h // 2), "SON", 0, h, c4t)
         wrap("SOI", 0, V("PB", 0, 2 * h), "CP8")
         by_fours(V("L5", h // 2, 3 * h // 4), "SOI", 0, 2 * h, c4t, 8)
-        act(V("G1", 4 * h, 5 * h), ind(V("TJ", 0, 2 * h), odd), bias=256.0)
-        n = 5 * h
+        act(V("G1", 4 * h, 5 * h), ind(V("BJ", 0, 4 * h), left))
+        act(V("GT", 0, h), ind(V("TJ", 0, 2 * h), odd))
+        lin("GT", V("GT", 129, 129 + h), V("GT", 0, h))
         if r < 2:
-            act(V("G1", 5 * h, 6 * h), ind(V("BJ", 0, 4 * h), left))
-            act(V("GT", 0, h), ind(V("TJ", 0, 2 * h), odd))
             wrap("SOA", h, V(bn, 0, 2 * h, 2))
             listed(V("JL", c, 2 * c), "SOA", h, h)
             act(V("LP%d" % (r + 1), 0, h), ind(V("LP1", 0, 128) if r else V("IDL"), V("JL", c, 2 * c)))
-            n = 6 * h
+        n = 5 * h
         if r == 1:
-            act(V("G1", 6 * h, 7 * h), V("LP2", 0, h))
-            n = 7 * h
+            act(V("G1", 5 * h, 6 * h), V("LP2", 0, h))
+            n = 6 * h
         wrap("SOL", 0, V("G1", 3 * h, n))
         listed(V("RL", 0, n // 16 - 3 * c), "SOL", 0, n - 3 * h)
 
     def relink(r):
         h = HS[r]
         c = h // 16
-        act(V("PA", 1, 2 * h, 2), ind(res2, V("RL", 0, c)))
-        bits("SC", cp, ind(kids(0, 512), V("RL", c, 2 * c)), V("PA", 1, 2 * h, 2))
+        for j in range(2):
+            act(V("PA", j, 4 * h, 4), ind(res, V("RL", j * c, j * c + c)), bias=-383.0, f=AF.Relu)
+        wrap("SOD", 0, V("PA", 0, 4 * h), "CP64")
+        listed(V("STL", 0, c), "SOD", 0, 4 * h, run=64)
+        act(V("SEL", 0, h), ind(V("GT"), V("STL", 0, c)))
+        wrap("SOS", 0, V("SEL", 0, h))
+        listed(V("STL", 8, 8 + c), "SOS", 0, h, 256)
+        bits("SC", cp, ind(kids(0, 512), V("STL", 8, 8 + c)), V("G1", 3 * h, 4 * h))
         if r < 2:
-            act(V("PA", 0, 2 * h, 2), ind(res, V("RL", 2 * c, 3 * c)), f=AF.Relu)
-            wrap("SOD", 0, V("PA", 0, 2 * h), "CP32")
-            listed(V("STL", 0, c), "SOD", 0, 2 * h, run=32)
-            bits("SC", cp, ind(V("SGX", 16, 656), V("STL", 0, c)), V("GT", 0, h))
+            bits("SC", cp, ind(sr, V("RL", 0, c)), V("SEL", 0, h))
             lin("KIDD", kids(512, 768), kids(0, 256))
 
     def leaves(r):
         m = HS[r - 1]
         c = m // 16
         lt, lp = "LT%d" % r, "LP%d" % r
-        lid, par, now, at = (V("JL", 8, 16), 2 * m, m, 0) if r == 1 else (V("RL", 12, 16), 0, m, 56)
-        act(V(lt, par, par + m), ind(lw(PARN), lid))
-        act(V(lt, now, now + m), ind(sr, lid))
-        act(V(lt, 2 * m - par, 3 * m - par), ind(lw(POSL), lid))
+        if r == 1:
+            lid, at, slot = V("JL", 8, 16), 8, V("BL", 0, 8)
+            for j, t in enumerate((POSL, PARN)):
+                act(V(lt, j * m, j * m + m), ind(lw(t), lid))
+        else:
+            lid, at, slot = V("RL", 8, 12), 56, V("BL", 64, 68)
+            for j in range(2):
+                act(V(lt, j * m, j * m + m), ind(V("LT1", 128 - 128 * j, 256 - 128 * j), V("JL", 4, 8)))
         wrap("SOE", 0, V(lt))
-        listed(V("BL", at, at + 3 * c), "SOE", 0, 3 * m, 256)
-        slot = V("BL", at + c, at + 2 * c)
+        listed(V("BL", at, at + 2 * c), "SOE", 0, 2 * m, 256)
+        act(V("LN", 0, m), ind(sr, lid))
+        wrap("SOE", 256, V("LN", 0, m))
+        listed(slot, "SOE", 256, m, 256)
         act(V(lp, m, 2 * m), ind(V("IDM"), slot), bias=256.0)
         wrap("SO6", 0, V(lp), "CP4")
         by_fours(V("P4L", 0, m // 2), "SO6", 0, 2 * m, c4t)
@@ -580,26 +641,36 @@ def rank_program(g, core, T, topo):
         lo = LOFF[r] + h - 128
         for b in range(4):
             mm(V("pd", 512 * b, 512 * b + 128), "qw", "sw", 128 * b, "lq", "ls", lo, lo + 128)
-            o, p = V("hz", b, 4 * h, 4), V("pd", 512 * b + 128 - h, 512 * b + 128)
+            o, p = V("hz", 4 + b, 4 + 4 * h, 4), V("pd", 512 * b + 128 - h, 512 * b + 128)
             if b >= 4 - RELU_V:
                 ts(o, p, 0.0, A.max, 0.03125, A.mult)
             else:
                 act(o, p, scale=0.03125, f=AF.Relu)
-        tt(V("xt", 2048, 2048 + 4 * h), ind(xw, V("L5", 0, h // 4)), V("hz", 0, 4 * h), A.add)
-        tt(V("uu", 0, 4 * h), ind(V("xt"), V("L5", h // 4, h // 2)), V("hz", 0, 4 * h), A.add)
-        cp(ind(V("xt"), V("L5", h // 2, 3 * h // 4)), V("uu", 0, 4 * h))
+        bits("U%d" % r, tt, V("vv", 1, 8 * h, 2), ind(xw, V("L5", 0, h // 4)), V("hz", 4, 4 + 4 * h), A.add)
+        bits("U%d" % r, act, V("vv", 0, 8 * h, 2), ind(V("hz", 0, 4 + 4 * h), V("L5", h // 4, h // 2)))
+        w = 2 * PIECE["U%d" % r]
+        for a in range(0, 8 * h, w):
+            scan(V("uu", a, a + w), V("ALT", 0, w), V("vv", a, a + w), 0.0, A.mult, A.add)
+        cp(ind(V("xt"), V("L5", h // 2, 3 * h // 4)), V("uu", 1, 8 * h, 2))
 
     def number(r):
         m = HS[r - 1]
         c = m // 16
-        t, bv, ev, lf, par, pos = (TW1, "BV1", m, 0, V("BL", 16, 24), V("BL", 0, 8)) if r == 1 else (TW2, "BVS", 0, 512, V("BL", 56, 60), V("BL", 64, 68))
-        state(tw(t, 255), A.is_gt)
+        t, bv, ev, lf, par, pos = (TW1, "BV1", m, 0, V("BL", 16, 24), V("BL", 8, 16)) if r == 1 else (TW2, "BVS", 0, 512, V("BL", 56, 60), V("BL", 60, 64))
+        state(r, tw(t, 255), A.is_gt)
         folds(r)
-        tt(V("PROD", 0, 512), ind(tw(t), V("BL", 24, 56)), V(bv, ev, ev + 512), A.mult)
+        bits("PR", tt, V("PROD", 0, 512), ind(tw(t), V("BL", 24, 56)), V(bv, ev, ev + 512), A.mult)
+        prog[-1][2].append(("order", r, r + 1, True, 1))
+        for a in (0, 128):
+            tt(tw(FLIP[r] + a, 128), tw(FLIP[r - 1] + a, 128), tw(t + a, 128), A.not_equal)
+            prog[-1][2].append(("order", r, r + 1, False, 1))
+        lin("NF", tw(FLIP[r] + 256), tw(FLIP[r]), -1.0, 1.0)
+        act(V("CL", 0, m), ind(tw(FLIP[r], 512), V("BL", 0, 8) if r == 1 else V("BL", 64, 68)), scale=LEFT)
         tt(V("PROD", 512, 512 + m), ind(tw(t), par), V(bv, lf, lf + m), A.mult)
-        scan(V("SS"), V("one", 0, 512), V("PROD", 0, 512), 0.0, A.mult, A.add)
-        tt(V("PM", 0, m), ind(tw(t), V("NLJ", 0, c)), V("C1", 0, m), A.mult)
-        tt(V("PAY", 0, m), V("PM", 0, m), V("C0", 0, m), A.add)
+        w = PIECE["PR"]
+        for a in range(0, 512, w):
+            scan(V("SS", a, a + w), V("one", 0, w), V("PROD", a, a + w), V("SS", a - 1, a) if a else 0.0, A.mult, A.add)
+        counted(V("PAY", 0, m), V("IDL", 0, m), V("CL", 0, m))
         tt(V("NUM", 0, m), ind(V("SS"), pos), V("PROD", 512, 512 + m), A.add)
         wrap("SOQ", 0, V("NUM", 0, m), "CPJ")
         listed(V("NL", 0, c), "SOQ", 0, m)
@@ -607,12 +678,11 @@ def rank_program(g, core, T, topo):
 
     send(0)
     book(0)
-    bits("DX", tt, V("DX", 0, 256), sxr(256), V("DE", 256, 512), A.subtract)
-    lin("AL", V("AL", 0, 256), sxr(0, 256), 0.5, 128.25)
-    lin("AL", V("AL", 256, 512), V("DX", 0, 256), 0.5, 128.25)
-    lin("RH", V("RH"), sxr(256), 1.0, 1024.0)
-    bits("DX", tt, V("DX", 256, 512), sxr(256), V("RH"), A.subtract)
-    act(lw(POSL), ind(V("DX", 256, 512), V("PARL", 0, 16)), scale=2048.0, bias=2048.0 * 1024 - 256)
+    lin("AL", V("AL", 0, 256), sxr(0, 256), 0.5, 128.375)
+    lin("AL", V("AL", 256, 512), sxr(256), 0.5, 128.125)
+    lin("RH", V("RH"), sxr(256), 1.0, 512.0)
+    bits("DX", tt, V("DX"), sxr(256), V("RH"), A.subtract)
+    act(lw(POSL), ind(V("DX"), V("PARL", 0, 16)), scale=1 / EPS, bias=512 / EPS - 256)
     lin("PARD", lw(PARN + 512), lw(PARN + 256))
     bits("SS", act, V("PE"), ind(lw(PARN + 256, 512), ordw))
     wrap("SOG", 0, V("PE"), apart=True)
@@ -622,9 +692,10 @@ def rank_program(g, core, T, topo):
     bits("TG", tt, V("DT", 256, 512), ind(V("AL"), V("EVL", 32, 48)), V("AI", 256, 512), A.subtract)
     lin("NEG", V("DT", 0, 256), V("DT", 256, 512), -1.0)
     bits("SS", act, V("BV1", 128, 640), ind(V("DT"), ordw))
-    tt(lw(ALM, 128), ind(lw(LG), V("JL", 8, 16)), V("W5", 896, 1024), A.add)
-    act(lw(ALM + 128, 128), ind(lw(AFL), V("JL", 8, 16)), bias=-256.0)
-    tt(V("BV1", 0, 128), lw(ALM + 128, 128), lw(ALM, 128), A.subtract)
+    act(lw(ALM + 128, 128), ind(lw(LG), V("JL", 8, 16)))
+    counted(lw(ALM, 128), V("WB", 384, 512), lw(ALM + 128, 128))
+    tt(V("BV1", 0, 128), ind(lw(AFL), V("JL", 8, 16)), lw(ALM, 128), A.subtract)
+    act(lw(JTL, 128), ind(lw(AFL), V("JL", 8, 16)))
     update(0)
     relink(0)
     leaves(1)
@@ -632,19 +703,19 @@ def rank_program(g, core, T, topo):
     number(1)
     send(1)
     book(1)
-    lin("JTL", lw(JTL), V("FLDE"), 0.5, 127.5)
     wrap("SOP", 0, V("AI"), apart=True)
     listed(V("AB2"), "SOP", 0, 512, -128)
     lin("SG1", tw(SG1), tw(TW1), -2.0, 1.0)
-    for j, t in enumerate((AFL, JTL, LG)):
-        act(V("LU", 64 * j, 64 * j + 64), ind(lw(t), V("RL", 12, 16)))
-    wrap("SOR", 0, V("LU", 0, 128))
-    listed(V("LM"), "SOR", 0, 128, -128)
-    cp(ind(V("ALV"), V("LM", 4, 8)), V("one", 0, 64))
+    stay = V("JL", 4, 8)
+    for j, t in enumerate((JTL, ALM + 128)):
+        act(V("LU", 64 * j, 64 * j + 64), ind(lw(t, 128), stay))
+    wrap("SOR", 0, V("LU", 0, 64))
+    listed(V("LM", 0, 4), "SOR", 0, 64, -128)
+    cp(ind(V("ALV"), stay), V("one", 0, 64))
     scan(V("CNT", 1, 129), V("one", 0, 128), V("ALV"), 0.0, A.mult, A.add)
     cn = V("CNT", 0, 129)
     act(V("MR"), ind(cn, V("AB2", 16, 32)))
-    tt(V("BLJ"), ind(cn, V("LM", 4, 8)), V("LU", 128, 192), A.add)
+    tt(V("BLJ"), ind(cn, stay), V("LU", 64, 128), A.add)
     bits("TG", tt, V("DT", 0, 256), ind(cn, V("AB2", 0, 16)), V("MR"), A.subtract)
     bits("TG", tt, V("DT2", 256, 512), ind(tw(SG1), V("PARL", 16, 32)), V("DT", 0, 256), A.mult)
     tt(V("BV2", 512, 576), ind(cn, V("LM", 0, 4)), V("BLJ"), A.subtract)
@@ -660,27 +731,24 @@ def rank_program(g, core, T, topo):
     book(2)
     update(2)
 
-    for j in range(2):
-        quant("qx", "sx", 256 * j, 256 * j + 256, V("xt", 1024 * j, 1024 * j + 1024))
-        mm(V("pp", 512 * j, 512 * j + 256), "qv", "sv", 0, "qx", "sx", 256 * j, 256 * j + 256)
-        dma("y", T.oc[:, 1024 * j:1024 * j + 1024], T.qx[:, 256 * j:256 * j + 256].bitcast(dt.uint8), "outa", [V("qx", 256 * j, 256 * j + 256)[1]], [], 2.5)
-        if j >= 2 - YB_V:
-            cp(V("yb", 256 * j, 256 * j + 256), V("pp", 512 * j, 512 * j + 256))
+    w = PIECE["OUT"]
+    for j, a in enumerate(range(0, 512, w)):
+        quant("qx", "sx", a, a + w, V("xt", 4 * a, 4 * (a + w)))
+        mm(V("pd", 512 * j, 512 * j + w), "qv", "sv", 0, "qx", "sx", a, a + w)
+        if (a + w) % 256 == 0:
+            dma("y", T.oc[:, 4 * (a + w) - 1024:4 * (a + w)], T.qx[:, a + w - 256:a + w].bitcast(dt.uint8), "outa", [V("qx", a + w - 256, a + w)[1]], [], 2.5)
+        if a + w > 512 - w * YB_V:
+            cp(V("yb", a, a + w), V("pd", 512 * j, 512 * j + w))
         else:
-            act(V("yb", 256 * j, 256 * j + 256), V("pp", 512 * j, 512 * j + 256), f=AF.Copy)
-        dma("s", T.y[:, 256 * j:256 * j + 256], T.yb[:, 256 * j:256 * j + 256], "outb", [V("yb", 256 * j, 256 * j + 256)[1]], [], 2.5)
+            act(V("yb", a, a + w), V("pd", 512 * j, 512 * j + w), f=AF.Copy)
+        dma("s" if j % 2 else "y", T.y[:, a:a + w], T.yb[:, a:a + w], "outb" if j % 2 else "outa", [V("yb", a, a + w)[1]], [], 2.1 + w / 640)
     for k in range(4):
         dma("y", T.osc[4 * k:4 * k + 4, :], T.sx[32 * k:32 * k + 4, :], "outa", [V("sx")[1]], [], 1.9)
     relink(2)
     ts(tw(SGR), V("RESW", 256, 512), 0.0, A.is_gt, 768.0, A.mult)
-    wrap("SOK", 0, tw(TW0))
-    wrap("SOK", 512, tw(TW1))
-    wrap("SOG", 0, tw(TW2))
+    wrap("SOK", 0, tw(FLIP[2]))
     wrap("SOK", 256, tw(SGR), "CPJ")
-    tt(V("KW", 64, 80), ends("SOK", 0, 256), ends("SOK", 512, 256), A.subtract)
-    act(V("KW", 0, 16), V("KW", 64, 80), f=AF.Abs)
-    tt(V("KW", 16, 32), V("KW", 0, 16), ends("SOG", 0, 256), A.subtract)
-    act(V("KW", 0, 16), V("KW", 16, 32), scale=256.0, bias=ch(-256), f=AF.Abs)
+    lin("KW", V("KW", 0, 16), ends("SOK", 0, 256), 256.0, ch(256))
     tt(V("KW", 32, 48), ends("SOK", 256, 256), V("KW", 0, 16), A.subtract)
     tt(V("KW", 48, 64), ends("SOK", 256, 256), V("KW", 0, 16), A.add)
     ts(V("KLL", 0, 16), V("KW", 32, 48), ch(1), A.add, 256.0, A.add)

import numpy as np
from concourse.mybir import dt, AluOpType, ActivationFunctionType

A = AluOpType
AF = ActivationFunctionType
BIG, HUGE, EPS = 1024.0, 2048.0, 1.0 / 4096
TOUR, PAIRED, HALVES = [0, 256, 512], (1, 2), (0, 1, 2)
SHARE = {"OC": 8, "DD": 8, "FLDE": 8}
WAKE, SOON, PASSES, ORDER = 0.22, (0.4, 0.5, 0.6, 0.7, 0.8, 0.9), 6, {}
IFIX, VFIX, SFIX, SLOW, WEIGHT, MIX = 0.055, 0.015, 0.04, 1.35, (0.6, 0.4), (0.1, 0.2, 0.3, 0.4, 0.5)
CYC, GAT, SCA, PECOL = [np.array(x) for x in ([0.00085, 0.0011], [0.0011, 0.0021], [0.0022, 0.005], [0.0006, 0.001])]
FLIGHT = [2.0, 1.5, 1.5]
HS = [128, 64, 32]
LOFF = [0, 128, 192]
STEP = [1, 2, 4]
CH = [1, 1, 1, 1, 1, 2, 4, 8]
OUT, BASE = [], [512]
for _k in range(8):
    OUT.append(BASE[-1] + 512)
    BASE.append(OUT[-1] + 16 * CH[_k])
LANES = [[("v", 0), ("s", 8), ("v", 18), ("s", 24)], [("v", 0), ("v", 8), ("s", 22)]]
PIECE = {"PAY": 96, "DX": 96, "TG": 128, "SC": 128, "WR": 256, "SG": 128, "SS": 256, "U0": 256, "U1": 128, "U2": 128, "PR": 512, "OUT": 128, "FL": 128}
FOLD_V, RELU_V, YB_V = [12, 8, 4], 2, 1
LEFT = 0.1875
ON_V = {"NEG", "SG1", "GN", "GO", "CP", "NF", "PARD"}
PARTS = [8, 2, 1]

ARENA = {"f32": [], "b16": [], "u16": [], "i32": [], "h16": []}
PLACE = {}


def _al(kind, **kw):
    for n, w in kw.items():
        lo = sum(ARENA[kind])
        ARENA[kind].append((w + 15) // 16 * 16)
        PLACE[n] = (kind, lo, w)


_al("f32", OX=528, RESW=1024, KIDS=1280, COL=16, MUL=8, CM=8, PF=8, C32=32, C32a=32, C32b=32, KV=128, MM=32, KP=32, YW=32, UF=32, IW=32,
    WBS=96, DQ=80, DE=512, DD=528, DX=256, SX=1040, L256=32, EV=64, KW=80, KID=512, BN0=256, BN1=128, BN2=64, SOA=256,
    OJ=256, TOPJ=256, AJ=512, BJ=512, PAY=256, C0=256, C1=128, CL=256, PM=128)
_al("b16", CPH=576, CP4=256, CP8=256, CP64=512, GT=272, SEL=128, PA=512, WB=BASE[8] + 512, OC=256, SGX=528, TWB=2560, LN=128, NFX=256, W5=1280, ALT=512, VV=512, IDM=512,
    LW=2304, AL=512, DT=512, DT2=512, AI=512, PE=512, IDL=256, BV1=640, BV2=576, BVS=576, PROD=640, SS=512, TJ=256, XJ=64, DJ=64,
    LT1=256, LT2=128, LU=192, LP1=256, LP2=128, BLJ=64, ALV=128, CNT=144, MR=256, NUM=128)
_al("h16", SOH=576, SOT=576, SOG=512, SO4=256, SO5=128, SO6=256, SOB=384, SOC=512, SOD=512, SOE=384, SOF=256, SOI=256, SOK=768, SOL=384, SOM=128, SON=128, SOO=128,
    SOP=512, SOQ=128, SOR=256, SOU=256, RH=256, CPJ=256, FLDE=256, G1=640, GL=128, SOS=128, PB=256)
_al("u16", QL=36, UL=8, KL16=32, UN=96, LB=16, PARL=32, S0L=32, LS0=40, LS1=40, LS2=40, LS3=40, ORDW=40, EVL=64, P4L=64, NL0=16, FL=32, JL=16, JX=16,
    UL3=24, RL=24, NLJ=8, TLJ=8, L5=96, STL=16, BL=68, NL=8, AB2=32, LM=8, KLL=32)
_al("i32", QI=48, QJ=36, J32=32, J32c=32, UI=8, SI=32, SJ=32)

C4, U8 = "float8_e4m3fn_x4", "uint8"
SCRATCH = {"f32": ("sbuf", [128, sum(ARENA["f32"])], "float32"), "b16": ("sbuf", [128, sum(ARENA["b16"])], "bfloat16"),
           "h16": ("sbuf", [128, sum(ARENA["h16"])], "float16"), "u16": ("sbuf", [128, sum(ARENA["u16"])], "uint16"),
           "i32": ("sbuf", [128, sum(ARENA["i32"])], "int32"), "ki": ("sbuf", [128, 32], "int32"), "yb": ("sbuf", [128, 512], "float32"),
           "pd": ("psum", [128, 3072], "float32"), "pp": ("psum", [128, 1024], "float32")}
for _n, _w in dict(xt=2560, ut=512, vt=512, one=528, zt=528, hz=528, vv=1024, uu=1024, fg=1024, ft=512, fc=1024).items():
    SCRATCH[_n] = ("sbuf", [128, _w], "bfloat16")
for _c, _s, _w in [("qx", "sx", 512), ("qe", "se", 512), ("qw", "sw", 512), ("qu", "su", 128), ("qup", "sup", 128), ("qv", "sv", 128),
                   ("qf", "sf", 384), ("lq", "ls", 224)]:
    SCRATCH[_c] = ("sbuf", [128, _w], C4)
    SCRATCH[_s] = ("sbuf", [128, _w], U8)
SEMAPHORES = ["v", "s", "p", "g", "dka", "dkb", "dx1", "dx0", "du", "dwc", "dws", "dv", "arr0", "arr1", "arr2", "snt", "outa", "outb"]


def meets(a, b):
    return b[0] < a[1] and a[0] < b[1] and (a[2] or b[2]) and not (a[3] == b[3] and (a[0] - b[0]) % a[3])


def note(log, acc, tag):
    for buf, lo, hi, w, st in acc:
        old = log.get(buf, [])
        if w and st == 1:
            old = [x for x in old if not (lo <= x[0] and x[1] <= hi)]
        log[buf] = old + [(lo, hi, w, st, tag)]


def schedule(prog):
    n = len(prog)
    if n in ORDER:
        return ORDER[n]
    pred, seen = [], {}
    for i, p in enumerate(prog):
        pred.append({x[4] for r in p[2] for x in seen.get(r[0], []) if meets(r[1:], x)})
        note(seen, p[2], i)
    succ = [[] for _ in prog]
    for i, d in enumerate(pred):
        for j in sorted(d):
            succ[j].append(i)
    queue = [q[0] for q in prog]
    costs = [[float((q[6] + 0 * CYC)[m]) for q in prog] for m in range(2)]
    lats = [[q[7] * (SLOW if m and q[7] > 0 else 1.0) for q in prog] for m in range(2)]

    def length(order):
        total = 0.0
        for cost, lat, weight in zip(costs, lats, WEIGHT):
            free, fin = {}, [0.0] * n
            for i in order:
                t = max([free.get(queue[i], 0.0)] + [fin[j] for j in pred[i]])
                free[queue[i]], fin[i] = t + cost[i], t + cost[i] + lat[i] + WAKE
            total += weight * max(fin)
        return total

    def place(prio, back, soon, cost, lat):
        before, after = (succ, pred) if back else (pred, succ)
        left = [len(d) for d in before]
        ready = [i for i in range(n) if not left[i]]
        at, free, start, order, end = [lat[i] if back else 0.0 for i in range(n)], {}, [0.0] * n, [], 0.0
        while ready and soon < 0:
            i = max(ready, key=lambda i: (prio[i], -i))
            ready.remove(i)
            t, slots = at[i], free.setdefault(queue[i], [])
            for a, b in slots:
                if a >= t + cost[i] + soon:
                    break
                t = max(t, b)
            slots.append((t, t + cost[i]))
            slots.sort()
            start[i] = t
            for j in after[i]:
                at[j] = max(at[j], t + cost[i] + lat[j if back else i] + WAKE)
                left[j] -= 1
                if not left[j]:
                    ready.append(j)
            if not ready:
                order = sorted(range(n), key=lambda i: (start[i], i))
        while ready:
            done, e = min((max(at[i], free.get(queue[i], 0.0)) + cost[i], queue[i]) for i in ready)
            t = max(free.get(e, 0.0), min(at[i] for i in ready if queue[i] == e))
            i = max((i for i in ready if queue[i] == e and at[i] <= t + soon * (done - t)), key=lambda i: (prio[i], -i))
            ready.remove(i)
            order.append(i)
            start[i] = t = max(t, at[i])
            free[e] = t + cost[i]
            end = max(end, t + cost[i] + (0.0 if back else lat[i]))
            for j in after[i]:
                at[j] = max(at[j], t + cost[i] + lat[j if back else i] + WAKE)
                left[j] -= 1
                if not left[j]:
                    ready.append(j)
        return start, end, order
    best = None
    for mix in MIX:
        cost, lat = [[(1 - mix) * a + mix * b for a, b in zip(*x)] for x in (costs, lats)]
        rest = [0.0] * n
        for i in range(n - 1, -1, -1):
            rest[i] = cost[i] + lat[i] + max([rest[j] + WAKE for j in succ[i]] + [0.0])
        for soon in SOON:
            prio = rest
            for _ in range(PASSES):
                start, end, order = place(prio, False, soon, cost, lat)
                end = length(order)
                if best is None or end < best[0]:
                    best = (end, order)
                rev = place([start[i] + cost[i] + lat[i] for i in range(n)], True, soon, cost, lat)[0]
                prio = [rev[i] + cost[i] for i in range(n)]
    ORDER[n] = best[1]
    return ORDER[n]


def rank_program(g, core, T, topo):
    rank = T.rank_of(core)
    if rank is None:
        return
    Q = {"v": g.vector, "s": g.scalar, "p": g.tensor, "g": g, "y": g.sync}
    cnt, clock, log, prog = {}, {}, {}, []
    known = {e: {} for e in Q}

    def V(name, a=None, b=None, st=1):
        buf, lo, w = PLACE[name] if name in PLACE else (name, 0, SCRATCH[name][1][1])
        a = 0 if a is None else a
        b = w if b is None else b
        assert 0 <= a < b <= w, (name, a, b, w)
        ap = T[buf][:, lo + a:lo + b] if st == 1 else T[buf][:, lo + a:lo + b:st]
        n, part = (b - a + st - 1) // st, lambda i, j: V(name, a + i * st, min(b, a + j * st), st)
        if buf in ("pd", "pp"):
            return (ap, [(buf, a // 512 * 512, (b + 511) // 512 * 512, True, 1)], n, part)
        return (ap, [(buf, lo + a, lo + b, False, st)], n, part)

    def ind(w, o):
        return (w[0].indirect(o[0]), w[1] + o[1], 16 * o[2], lambda i, j: ind(w, o[3](i // 16, j // 16)))

    def bits(name, call, out, *ins, **kw):
        w = PIECE.get(name, out[2])
        for a in range(0, out[2], w):
            call(*[x[3](a, min(a + w, out[2])) if isinstance(x, tuple) and x[2] == out[2] else x for x in (out,) + ins], **kw)

    def need(e, sem, c):
        if known[e].get(sem, 0) < c:
            Q[e].wait_ge(T.sem[sem], c)
            known[e][sem] = c
            for k2, v2 in clock.get((sem, c), {}).items():
                if known[e].get(k2, 0) < v2:
                    known[e][k2] = v2

    def op(e, fn, reads, writes, sem=None, inc=1, mark=True, cost=0.1, lat=0.0):
        acc = [r for x in reads for r in x] + [(r[0], r[1], r[2], True, r[4]) for x in writes for r in x]
        prog.append((e, fn, acc, sem or e, inc, mark, cost, lat))

    def issue(e, fn, acc, sem, inc, mark):
        if fn is None:
            note(log, [r for r in acc if r[3]], (sem, inc))
            return
        deps, acc = {}, [r for r in acc if r[0] != "order"]
        for r in acc:
            for x in log.get(r[0], []):
                if meets(r[1:], x):
                    deps[x[4][0]] = max(deps.get(x[4][0], 0), x[4][1])
        for s2 in sorted(deps, key=lambda s: s == sem):
            need(e, s2, deps[s2])
        ins = fn()
        cnt[sem] = cnt.get(sem, 0) + inc
        if mark:
            ins.then_inc(T.sem[sem], inc)
        clock[(sem, cnt[sem])] = dict(known[e])
        note(log, acc, (sem, cnt[sem]))

    def est(out, ins, fix, two=False, half=True):
        if len(out[1]) > 1:
            return IFIX + out[2] * SCA
        if any(len(x[1]) > 1 for x in ins):
            return IFIX + out[2] * GAT + 0.3 * (fix - VFIX)
        k = 2.0 if two else 0.5 if half and all(x[1][0][0] not in ("f32", "i32", "pd", "pp", "yb", "ki") for x in ins + [out]) else 1.0
        return fix + max(64, out[2] * k) * CYC

    def sc(x):
        return (x[0], [x[1]]) if isinstance(x, tuple) else (x, [])

    def wr(out):
        return [out[1][:1]]

    def ts(out, a, s1, o0, s2=None, o1=None):
        (a1, r1), (a2, r2) = sc(s1), sc(s2)
        args = (a1, None, o0) if o1 is None else (a1, a2, o0, o1)
        op("v", lambda: g.vector.tensor_scalar(out[0], a[0], *args), [a[1]] + r1 + r2, wr(out), cost=est(out, [a], VFIX))

    def tt(out, a, b, o):
        op("v", lambda: g.vector.tensor_tensor(out[0], a[0], b[0], o), [a[1], b[1]], wr(out), cost=est(out, [a, b], VFIX, True))

    def cp(out, a):
        op("v", lambda: g.vector.tensor_copy(out[0], a[0]), [a[1], out[1][1:]], wr(out), cost=est(out, [a], VFIX))

    def ms(out, c):
        op("v", lambda: g.vector.memset(out[0], c), [], wr(out), cost=est(out, [], VFIX))

    def scan(out, d0, d1, init, o0, o1):
        a1, r1 = sc(init)
        op("v", lambda: g.vector.tensor_tensor_scan(out[0], d0[0], d1[0], a1, o0, o1), [d0[1], d1[1]] + r1, wr(out), cost=est(out, [d0, d1], VFIX))

    def act(out, a, scale=1.0, bias=0.0, f=AF.Identity):
        (a1, r1), (a2, r2) = sc(scale), sc(bias)
        kw = {} if f == AF.Copy else {"bias": a2, "scale": a1}
        op("s", lambda: g.scalar.activation(out[0], a[0], f, **kw), [a[1]] + r1 + r2, wr(out), cost=est(out, [a], SFIX, False, False))

    def lin(name, out, a, scale=1.0, bias=0.0):
        if name in ON_V:
            ts(out, a, scale, A.mult, bias, A.add)
        else:
            act(out, a, scale=scale, bias=bias)

    def iota(out, pat, base, cm=0):
        kw = {"allow_small_or_imprecise_dtypes": True} if out[1][0][0] != "i32" else {}
        op("g", lambda: g.iota(out[0], pat, base, cm, **kw), [], wr(out), cost=0.15 + 2 * CYC * out[2])

    def fill(out, c):
        iota(out, [[0, out[2]]], c)

    def quant(q, s, a, b, src):
        o1, o2 = V(q, a, b), V(s, a, b)
        op("v", lambda: g.vector.quantize_mx(o1[0], o2[0], src[0]), [src[1]], [o1[1], o2[1]], cost=0.02 + 1.06 * CYC * (b - a))

    def mm(out, lq, ls, la, rq, rs, ra, rb):
        x = [V(lq, la, la + 128), V(ls, la, la + 128), V(rq, ra, rb), V(rs, ra, rb)]
        op("p", lambda: g.tensor.matmul_mx(out[0], x[0][0], x[1][0], x[2][0], x[3][0], True, True), [y[1] for y in x], wr(out), cost=PECOL * (rb - ra + 16))

    def dma(e, out, src, sem, reads, writes, lat=2.1):
        op(e, lambda: Q[e].dma_start(out, src), reads, writes, sem=sem, inc=16, cost=0.06, lat=lat)

    def wrap(out, at, data, pat="CPH", apart=False):
        n = data[2]
        bits("WR" if apart else None, scan, V(out, at, at + n), data, V(pat, 0, n), -HUGE, A.max, A.add)

    def counted(out, rising, small):
        scan(out, rising, small, -HUGE, A.max, A.add)

    def ends(buf, a, n, run=16):
        return V(buf, a + run - 1, a + n, run)

    def col(j):
        return V("COL", j, j + 1)

    def ch(times):
        j = [1, 256, -256].index(times)
        return V("CM", j, j + 1)

    def pf(j):
        return V("PF", j, j + 1)

    def tw(a, n=256):
        return V("TWB", a, a + n)

    def listed(out, buf, a, n, add=None, run=16):
        ts(out, ends(buf, a, n, run), ch(1), A.add) if add is None else ts(out, ends(buf, a, n, run), ch(1), A.add, float(add), A.add)

    def by_fours(out, buf, a, n, c, run=4):
        ts(out, ends(buf, a, n, run), 4.0, A.mult, col(c), A.add)
    cH, cW1, cX, c4r, c4t, c4u, cY, c8t = 0, 1, 4, 5, 6, 7, 8, 9
    NF0, TW1, TW2, SGR, SG1 = [256 * j for j in range(1, 6)]
    TW0, FLIP = 0, [0, 1536, 2048]
    ALM, JTL, AFL, POSL, LG, PARN = 0, 256, 512, 768, 1024, 1536
    idw, iow, xw = V("WB", 0, 512), V("IW", 0, 16), V("xt", 0, 2048)
    sr, res = V("SGX", 16, 528), V("RESW")

    def sxr(a=0, b=512):
        return V("SX", 528 + a, 528 + b)

    def kids(a, b):
        return V("KIDS", a, b)

    def lw(a, n=256):
        return V("LW", a, a + n)

    late = [[("late", 0, 1, False, 1)]]
    dma("y", T.ki[:, 16:32], T.ka[:], "dka", [], [V("ki", 16, 32)[1]])
    dma("s", T.ki[:, 0:16], T.kb[:], "dkb", [], [V("ki", 0, 16)[1]])
    dma("s", T.ut[:], T.u[:], "du", [], [V("ut")[1]], 2.4)
    dma("y", T.xt[:, 1024:2048], T.x[:, 1024:2048], "dx1", [], [V("xt", 1024, 2048)[1]], 2.8)
    dma("y", T.xt[:, 0:1024], T.x[:, 0:1024], "dx0", late, [V("xt", 0, 1024)[1]], 2.8)
    dma("y", T.qw[:].bitcast(dt.uint8), T.wc[:], "dwc", late, [V("qw")[1]], 2.8)
    dma("y", T.sw[:], T.ws[:], "dws", late, [V("sw")[1]])
    dma("y", T.vt[:], T.v[:], "dv", late, [V("vt")[1]])

    iota(V("QJ"), [[0, 36]], 0, 1)
    iota(V("J32", 0, 16), [[1, 16]], 128, -1)
    iota(V("J32", 16, 32), [[4, 16]], 131, -1)
    iota(V("UI"), [[16, 8]], 0)
    iota(V("UF"), [[0, 2], [16, 16]], 0)
    iota(V("MUL", 0, 2), [[255, 2]], 1)
    fill(V("MUL", 2, 3), -256)
    ms(V("one"), 1.0)
    scan(idw, V("one", 0, 512), V("one", 0, 512), -257.0, A.mult, A.add)
    op("g", lambda: g.affine_select(T.zt[:, 0:516], T.one[:, 0:516], [[-1, 516]], A.is_equal, 0.0, 3, 4), [V("one", 0, 516)[1]], [V("zt", 0, 516)[1]], cost=1.1)
    iota(V("OX", 0, 528), [[1, 528]], -16)
    fill(V("SGX", 527, 528), -1)
    fill(V("TWB", 255, 1536, 256), 0)
    fill(V("NFX", 255, 256), 256)
    iota(V("W5", 768, 1024), [[1, 256]], -256)
    iota(V("IDM"), [[0, 2], [1, 256]], -256)
    iota(V("IDL"), [[1, 256]], 0)
    iota(V("RESW"), [[0, 2], [-1, 512]], 0)
    fill(V("hz", 0, 4), 0)
    iota(V("ALT"), [[0, 256], [1, 2]], 0)
    fill(V("DD", 15, 16), 0)
    fill(V("GT", 128, 272), 0)
    iota(V("PA", 2, 512, 4), [[1, 128]], 0)
    fill(V("PA", 3, 512, 4), 0)
    fill(V("BJ", 0, 512, 2), 0)
    fill(kids(768, 1280), -1)
    iota(V("KV"), [[1, 128]], 512)
    fill(V("CNT", 0, 1), 0)
    fill(V("ALV"), 0)
    fill(V("CP8", 0, 256, 2), 0)
    fill(V("CP64"), 0)
    ts(V("QI", 0, 36), V("QJ"), 15, A.bitwise_and)
    ts(V("J32c"), V("J32"), 15, A.bitwise_and)
    cp(V("QL"), V("QI", 0, 36))
    for j, keep in enumerate([3, 1, 2, 4, 8]):
        ts(V("QI", 36 + j, 37 + j), V("QJ", 0, 1), keep, A.bitwise_and)
    cp(V("PF", 0, 6), V("QI", 35, 41))
    for j, th in enumerate([1.0, 4.0]):
        ts(V("C32b", 16 * j, 16 * j + 16), V("J32c", 16 * j, 16 * j + 16), th, A.is_lt, BIG, A.mult)
        ts(V("C32a", 16 * j, 16 * j + 16), V("J32c", 16 * j, 16 * j + 16), 16.0 - th, A.is_ge, -HUGE, A.mult)
    tt(V("C32"), V("C32a"), V("C32b"), A.add)
    cp(V("UL"), V("UI"))
    act(V("IW"), V("UF"), bias=pf(0))
    act(col(cH), V("C32a", 15, 16), scale=-1.0, bias=-BIG)
    bits("SS", act, V("CPH"), ind(V("C32", 0, 16), V("QL", 0, 36)))
    act(V("CM", 0, 3), V("MUL", 0, 3), scale=col(cH))
    for k in (1, 2, 3):
        act(col(cW1 + k - 1), pf(2 + k), scale=BASE[k] / (1 << k), bias=col(cH))
    act(col(cX), col(cH), scale=2.0, bias=0.3)
    act(col(cY), col(cH), scale=2.0, bias=0.8)
    act(col(c4r), V("C32a", 19, 20), scale=-1.0, bias=-BIG)
    act(col(c4t), col(c4r), scale=4.0, bias=pf(1))
    act(col(c4u), col(c4t), bias=1024.0)
    act(col(c8t), col(c4t), scale=2.0, bias=1.0)
    act(V("CP4"), ind(V("C32", 16, 32), V("QL", 0, 16)))
    lin("CP", V("CP8", 1, 256, 2), V("CP4", 0, 128))
    lin("CP", V("CP64", 3, 512, 4), V("CPH", 0, 128))
    lin("CPJ", V("CPJ"), V("CPH", 0, 256))
    tt(V("CPJ", 15, 256, 16), V("CPH", 15, 256, 16), iow, A.add)
    ts(V("LS0", 0, 1), pf(2), float(BASE[0]), A.mult, 511.0, A.add)
    for b in range(4):
        quant("qe", "se", 128 * b, 128 * b + 128, V("zt", 3 - b, 515 - b))

    o_ = V("KL16")
    op("v", lambda: g.vector.tensor_scalar(o_[0], T.ki[:], 16.0, None, A.add), [V("ki")[1]], [o_[1], [("late", 0, 1, True, 1)]], cost=0.13)
    prog[4:8], prog[len(prog) - 4:] = [], prog[len(prog) - 4:] + prog[4:8]
    bits("SG", cp, ind(V("SGX"), V("KL16")), idw)
    bits("SS", act, kids(0, 512), ind(V("OX", 0, 528), V("KL16")))
    lin("KIDD", kids(512, 768), kids(0, 256))
    quant("qu", "su", 0, 128, V("ut"))
    quant("qv", "sv", 0, 128, V("vt"))
    act(V("sup"), ind(V("su"), V("UL")), f=AF.Copy)
    u_ = V("UL")
    op("v", lambda: g.vector.tensor_copy(T.qup[:, 0:128].bitcast(dt.uint32), T.qu[:, 0:128].bitcast(dt.uint32).indirect(u_[0])), [V("qu")[1], u_[1]], [V("qup")[1]], cost=IFIX + 128 * GAT)
    nb, na, eb, ea = V("WBS", 64, 80), V("WBS", 80, 96), V("WBS", 32, 48), V("WBS", 48, 64)
    ts(V("MM"), V("ki"), 256.0, A.is_ge)
    ts(V("WBS", 64, 96), V("ki"), 256.0, A.is_lt)
    tt(V("KP"), V("ki"), V("MM"), A.mult)
    tt(V("WBS", 32, 64), V("KP"), V("IW"), A.max)
    tt(V("YW", 0, 16), nb, ea, A.mult)
    tt(V("YW", 16, 32), na, eb, A.mult)
    tt(V("WBS", 0, 32), V("KP"), V("YW"), A.add)
    cp(V("UN", 32, 64), V("WBS", 32, 64))
    cp(V("UN", 0, 32), V("WBS", 0, 32))
    act(V("W5", 512, 768), ind(idw, V("UN", 48, 64)))
    act(V("W5", 1024, 1280), ind(idw, V("UN", 32, 48)))
    act(V("W5", 0, 512), ind(idw, V("UN", 0, 32)))

    def state(r, turns, *how):
        quant("qx", "sx", 256, 512, V("xt", 1024, 2048))
        mm(V("pp", 0, 256), "qup", "sup", 0, "qx", "sx", 256, 512)
        quant("qx", "sx", 0, 256, V("xt", 0, 1024))
        ts(turns, V("pp", 0, 255), 0.0, *how)
        for j, (lo, hi) in enumerate([(256, 512), (0, 256)] if r in HALVES else [(0, 512)]):
            for b in range(4):
                p = V("pd", 512 * ((4 * j + b) % 6), 512 * ((4 * j + b) % 6) + hi - lo)
                mm(p, "qe", "se", 128 * b, "qx", "sx", lo, hi)
                act(V("xt", 4 * lo + b, 4 * hi, 4), p, f=AF.Copy)

    state(0, V("NFX", 0, 255), A.is_le, 256.0, A.mult)
    wrap("SOR", 0, V("NFX"), "CPJ")
    listed(V("LB"), "SOR", 0, 256)
    for a in (256, 0):
        wrap("SOG", a, V("SGX", 16 + a, 272 + a))
        listed(V("S0L", a // 16, a // 16 + 16), "SOG", a, 256, 256)
    act(V("VV", 256, 512), ind(V("W5", 768, 1280), V("LB")))
    cp(V("VV", 0, 256), ind(V("W5", 512, 1024), V("LB")))
    act(V("WB", BASE[0] + 256, BASE[0] + 512), ind(V("W5", 0, 512), V("LB")))
    cp(V("WB", BASE[0], BASE[0] + 256), ind(V("VV"), V("S0L", 16, 32)))
    for a in (256, 0):
        wrap("SOH", a, V("WB", BASE[0] + a, BASE[0] + a + 256))
        listed(V("LS0", 1 + a // 16, 17 + a // 16), "SOH", a, 256, 256 + BASE[0])
    lin("TW0", tw(TW0), V("NFX"), -1.0 / 256, 1.0)
    lin("TW0", tw(NF0), V("NFX"), 1.0 / 256)
    bits("SS", act, lw(LG, 512), ind(tw(TW0, 512), V("S0L")))
    bits("SS", act, lw(PARN, 512), ind(V("IDM"), V("S0L")))
    listed(V("SI"), "SOG", 0, 512, 256)
    ts(V("SJ"), V("SI"), 255, A.bitwise_and)
    wrap("SO4", 0, lw(PARN), "CP4")
    by_fours(V("P4L"), "SO4", 0, 256, c4u)
    wrap("SOC", 0, lw(LG, 512), apart=True)
    lin("L256", V("L256"), ends("SOC", 0, 512), 256.0, ch(256))
    tt(V("EV", 0, 16), V("SJ", 0, 16), V("L256", 0, 16), A.add)
    tt(V("EV", 16, 48), V("SJ"), V("L256"), A.subtract)
    tt(V("EV", 48, 64), iow, V("L256", 16, 32), A.subtract)
    ts(V("EVL"), V("EV"), 256.0, A.add)
    tt(V("DQ", 0, 16), ends("SOR", 0, 256), iow, A.subtract)
    tt(V("DQ", 16, 32), nb, na, A.subtract)
    ts(V("DQ", 32, 48), V("DQ", 0, 16), ch(1), A.add, 1.0 / 256, A.mult)
    tt(V("DQ", 0, 16), V("DQ", 32, 48), V("DQ", 16, 32), A.mult)
    tt(V("DQ", 48, 64), na, V("DQ", 0, 16), A.add)
    tt(V("DQ", 64, 80), nb, V("DQ", 0, 16), A.subtract)
    cp(V("UN", 64, 96), V("DQ", 48, 80))
    bits("SS", act, V("DE"), ind(V("IDL"), V("UN", 64, 96)), scale=0.5, bias=EPS / 2)
    cp(V("PARL"), V("SJ"))

    def ahead(r, slot, parent):
        m = 2 * HS[r]
        act(V("AJ", 0, 2 * m, 2), ind(kids(256, 768), slot))
        act(V("AJ", 1, 2 * m, 2), V("AJ", 0, 2 * m, 2), bias=512.0)
        act(V("TJ", 0, m), ind(V("SGX", 272, 528), parent))
        if r == 0:
            top = ind(lw(PARN + 256), parent)
            lin("CL", V("CL"), lw(LG), LEFT)
            counted(V("PAY"), V("IDL"), V("CL"))
        else:
            wrap("SOM", 0, V("TJ", 0, m))
            listed(V("TLJ", 0, m // 16), "SOM", 0, m, 256)
            top = ind(V("IDM"), V("TLJ", 0, m // 16))
        act(V("BJ", 1, 2 * m, 2), top, bias=512.0)
    ahead(0, V("S0L", 0, 16), V("PARL", 0, 16))

    def folds(r):
        n = 8 * HS[r]
        w = n // PARTS[r]
        for a in range(0, n, w):
            if r == 0:
                tt(V("fc", a, a + w), ind(V("xt", 1024, 2048), V("P4L", a // 16, (a + w) // 16)), V("xt", a, a + w), A.add)
                continue
            if r not in PAIRED:
                act(V("fg", a, a + w), ind(V("xt", 0, 1024), V("P4L", a // 16, (a + w) // 16)))
                tt(V("fc", a, a + w), ind(V("xt", 1024, 2048), V("P4L", (n + a) // 16, (n + a + w) // 16)), V("fg", a, a + w), A.add)
                continue
            for j in range(2):
                act(V("fg", 2 * a + j, 2 * (a + w), 2), ind(V("xt", 1024 * j, 1024 * j + 1024), V("P4L", (j * n + a) // 16, (j * n + a + w) // 16)))
            scan(V("fc", 2 * a, 2 * (a + w)), V("ALT", 0, 2 * w), V("fg", 2 * a, 2 * (a + w)), 0.0, A.mult, A.add)
    folds(0)
    for k in range(8):
        c, o, so = CH[k], OUT[k], "SOH" if k % 2 else "SOT"
        nc, ls = 32 + c, "LS%d" % k if k < 4 else "ORDW"
        win = V("WB", 0 if k < 4 else BASE[k], BASE[k] + 512)
        cuts = [a for e, a in LANES[k == 7]] + [nc]
        for (e, a), b in zip(LANES[k == 7], cuts[1:]):
            (cp if e == "v" else act)(V("WB", o + 16 * a, o + 16 * b), ind(win, V(ls, a, b)))
        for a, b in zip(cuts, cuts[1:]) if k < 7 else [(0, 8)]:
            wrap(so, 16 * a, V("WB", o + 16 * a, o + 16 * b))
            if k < 3:
                if a == 0:
                    ts(V("LS%d" % (k + 1), 0, 1), V(so, 15, 16), col(cW1 + k), A.add, 256.0, A.add)
                    a = 1
                listed(V("LS%d" % (k + 1), a, b), so, 16 * a, 16 * (b - a), 256 + BASE[k + 1])
            else:
                at = c if k > 3 else 0
                listed(V("ORDW", at + a, at + b), so, 16 * a, 16 * (b - a), 256)

    def shared(out, a, win, lst, b, n, bias=0.0):
        u = SHARE[out]
        act(V(out, a + 16 * u, a + n), ind(win, V(lst, b + u, b + n // 16)), bias=bias)
        ts(V(out, a, a + 16 * u), ind(win, V(lst, b, b + u)), bias, A.add)
    shared("OC", 0, V("WB", BASE[8], BASE[8] + 512), "ORDW", 0, 256)
    wrap("SOU", 0, V("OC"))
    listed(V("ORDW", 16, 32), "SOU", 0, 256, 256)
    for a, b in zip(TOUR, TOUR[1:]):
        if a == 256:
            shared("DD", 272, V("DE"), "ORDW", 16, 256)
        else:
            act(V("DD", 16 + a, 16 + b), ind(V("DE"), V("ORDW", a // 16, b // 16)))
        scan(V("SX", 16 + a, 16 + b), V("DD", 15 + a, 15 + b), V("DD", 16 + a, 16 + b), V("SX", 15 + a, 16 + a) if a else -EPS / 2, A.add, A.add)
        cp(ind(sxr(), V("ORDW", a // 16, b // 16)), V("SX", 16 + a, 16 + b))
    ordw = V("ORDW", 0, 32)
    shared("FLDE", 0, sxr(-256), "EVL", 0, 256, -0.5)
    wrap("SOB", 0, V("FLDE"))
    listed(V("NL0"), "SOB", 0, 256)
    cp(ind(V("BN0"), V("NL0")), V("PAY"))

    def send(r):
        h, u = HS[r], FOLD_V[r]
        wrap("SO5", 0, V("BN%d" % r, 1, 2 * h, 2), "CP4")
        two = r in PAIRED
        ts(V("FL", 0, h // 4), ends("SO5", 0, h, 4), 8.0 if two else 4.0, A.mult, col(c8t if two else c4t), A.add)
        fc = V("fc", 0, 16 * h if two else 8 * h)
        act(V("ft", 16 * u, 4 * h), ind(fc, V("FL", u, h // 4)), scale=0.5)
        if u:
            ts(V("ft", 0, 16 * u), ind(fc, V("FL", 0, u)), 0.5, A.mult)
        quant("qf", "sf", 128 * r, 128 * r + 128, V("ft"))
        peer = T.cores[rank ^ STEP[r]]
        rid, pid, _ = topo.addr(peer)
        eng = topo.engines(core, peer)[:8]
        mask = sum(1 << e for e in eng)
        a, lo, arr = 128 * r, LOFF[r], "arr%d" % r
        op("g", lambda: g.remote_dma(T.lq[:, lo:lo + h].bitcast(dt.uint8), T.qf[:, a:a + h].bitcast(dt.uint8), T.sem[arr], T.sem.snt, pid, rid, mask),
           [V("qf", a, a + h)[1]], [[(arr, 0, 1, True, 1)]], sem="snt", inc=len(eng), mark=False, cost=0.2, lat=FLIGHT[r])
        op("g", lambda: g.remote_dma(T.ls[:, lo:lo + h], T.sf[:, a:a + h], T.sem[arr], T.sem.snt, pid, rid, mask),
           [V("sf", a, a + h)[1]], [[(arr, 1, 2, True, 1)]], sem="snt", inc=len(eng), mark=False, cost=0.2, lat=FLIGHT[r])
        op("a", None, [[(arr, 0, 2, False, 1)]], [V("lq", lo, lo + h)[1], V("ls", lo, lo + h)[1]], sem=arr, inc=2 * len(topo.engines(peer, core)[:8]), cost=0.0, lat=-WAKE)

    def book(r):
        h, bn = HS[r], "BN%d" % r
        c = h // 16
        wrap("SOA", 0, V(bn, 1, 2 * h, 2))
        ts(V("JX", 0, c), ends("SOA", 0, h), 2.0, A.mult, col(cX), A.add)
        listed(V("JL", 0, c), "SOA", 0, h)
        ts(V("JX", 8, 8 + c), ends("SOA", 0, h), 2.0, A.mult, col(cY), A.add)
        odd, both, left = V("JL", 0, c), V("JX", 0, c), V("JX", 8, 8 + c)
        act(V("G1", h, 2 * h), ind(V("AJ", 0, 4 * h), both))
        act(V("G1", 2 * h, 3 * h), ind(V("BJ", 0, 4 * h), both))
        if r == 0:
            lin("GN", V("G1", 0, h), ind(lw(PARN), odd), 1.0, 256.0)
        else:
            lin("GN", V("G1", 0, h), ind(V("LP%d" % r, 2 * h, 4 * h), odd))
        other = V("G1", 3 * h, 4 * h)
        lin("GO", other, ind(V("AJ", 0, 4 * h), left), 1.0, -512.0)
        wrap("SOB", 0, V("G1", 0, 3 * h))
        listed(V("UL3", 0, 3 * c), "SOB", 0, 3 * h)
        cp(ind(V("RESW", 256, 512), V("UL3", 0, c)), V("KV", 0, h))
        wrap("SOF", 0, other, "CP4")
        by_fours(V("L5", 0, h // 4), "SOF", 0, h, c4t)
        lin("PBO", V("PB", 0, 2 * h, 2), other)
        act(V("GL", 0, h), ind(res, V("UL3", 2 * c, 3 * c)), bias=-511.0, f=AF.Relu)
        act(V("PB", 1, 2 * h, 2), ind(res, V("UL3", c, 2 * c)), f=AF.Relu)
        wrap("SON", 0, V("GL", 0, h), "CP4")
        by_fours(V("L5", h // 4, h // 2), "SON", 0, h, c4t)
        wrap("SOI", 0, V("PB", 0, 2 * h), "CP8")
        by_fours(V("L5", h // 2, 3 * h // 4), "SOI", 0, 2 * h, c4t, 8)
        act(V("G1", 4 * h, 5 * h), ind(V("BJ", 0, 4 * h), left))
        act(V("GT", 0, h), ind(V("TJ", 0, 2 * h), odd))
        lin("GT", V("GT", 129, 129 + h), V("GT", 0, h))
        if r < 2:
            wrap("SOA", h, V(bn, 0, 2 * h, 2))
            listed(V("JL", c, 2 * c), "SOA", h, h)
            act(V("LP%d" % (r + 1), 0, h), ind(V("LP1", 0, 128) if r else V("IDL"), V("JL", c, 2 * c)))
        n = 5 * h
        if r == 1:
            act(V("G1", 5 * h, 6 * h), V("LP2", 0, h))
            n = 6 * h
        wrap("SOL", 0, V("G1", 3 * h, n))
        listed(V("RL", 0, n // 16 - 3 * c), "SOL", 0, n - 3 * h)

    def relink(r):
        h = HS[r]
        c = h // 16
        for j in range(2):
            act(V("PA", j, 4 * h, 4), ind(res, V("RL", j * c, j * c + c)), bias=-383.0, f=AF.Relu)
        wrap("SOD", 0, V("PA", 0, 4 * h), "CP64")
        listed(V("STL", 0, c), "SOD", 0, 4 * h, run=64)
        act(V("SEL", 0, h), ind(V("GT"), V("STL", 0, c)))
        wrap("SOS", 0, V("SEL", 0, h))
        listed(V("STL", 8, 8 + c), "SOS", 0, h, 256)
        bits("SC", cp, ind(kids(0, 512), V("STL", 8, 8 + c)), V("G1", 3 * h, 4 * h))
        if r < 2:
            bits("SC", cp, ind(sr, V("RL", 0, c)), V("SEL", 0, h))
            lin("KIDD", kids(512, 768), kids(0, 256))

    def leaves(r):
        m = HS[r - 1]
        c = m // 16
        lt, lp = "LT%d" % r, "LP%d" % r
        if r == 1:
            lid, at, slot = V("JL", 8, 16), 8, V("BL", 0, 8)
            for j, t in enumerate((POSL, PARN)):
                act(V(lt, j * m, j * m + m), ind(lw(t), lid))
        else:
            lid, at, slot = V("RL", 8, 12), 56, V("BL", 64, 68)
            for j in range(2):
                act(V(lt, j * m, j * m + m), ind(V("LT1", 128 - 128 * j, 256 - 128 * j), V("JL", 4, 8)))
        wrap("SOE", 0, V(lt))
        listed(V("BL", at, at + 2 * c), "SOE", 0, 2 * m, 256)
        act(V("LN", 0, m), ind(sr, lid))
        wrap("SOE", 256, V("LN", 0, m))
        listed(slot, "SOE", 256, m, 256)
        act(V(lp, m, 2 * m), ind(V("IDM"), slot), bias=256.0)
        wrap("SO6", 0, V(lp), "CP4")
        by_fours(V("P4L", 0, m // 2), "SO6", 0, 2 * m, c4t)
        wrap("SOO", 0, V(lp, m, 2 * m))
        listed(V("NLJ", 0, c), "SOO", 0, m)
        ahead(r, slot, V("NLJ", 0, c))

    def update(r):
        h = HS[r]
        lo = LOFF[r] + h - 128
        for b in range(4):
            mm(V("pd", 512 * b, 512 * b + 128), "qw", "sw", 128 * b, "lq", "ls", lo, lo + 128)
            o, p = V("hz", 4 + b, 4 + 4 * h, 4), V("pd", 512 * b + 128 - h, 512 * b + 128)
            if b >= 4 - RELU_V:
                ts(o, p, 0.0, A.max, 0.03125, A.mult)
            else:
                act(o, p, scale=0.03125, f=AF.Relu)
        bits("U%d" % r, tt, V("vv", 1, 8 * h, 2), ind(xw, V("L5", 0, h // 4)), V("hz", 4, 4 + 4 * h), A.add)
        bits("U%d" % r, act, V("vv", 0, 8 * h, 2), ind(V("hz", 0, 4 + 4 * h), V("L5", h // 4, h // 2)))
        w = 2 * PIECE["U%d" % r]
        for a in range(0, 8 * h, w):
            scan(V("uu", a, a + w), V("ALT", 0, w), V("vv", a, a + w), 0.0, A.mult, A.add)
        cp(ind(V("xt"), V("L5", h // 2, 3 * h // 4)), V("uu", 1, 8 * h, 2))

    def number(r):
        m = HS[r - 1]
        c = m // 16
        t, bv, ev, lf, par, pos = (TW1, "BV1", m, 0, V("BL", 16, 24), V("BL", 8, 16)) if r == 1 else (TW2, "BVS", 0, 512, V("BL", 56, 60), V("BL", 60, 64))
        state(r, tw(t, 255), A.is_gt)
        folds(r)
        bits("PR", tt, V("PROD", 0, 512), ind(tw(t), V("BL", 24, 56)), V(bv, ev, ev + 512), A.mult)
        prog[-1][2].append(("order", r, r + 1, True, 1))
        for a in (0, 128):
            tt(tw(FLIP[r] + a, 128), tw(FLIP[r - 1] + a, 128), tw(t + a, 128), A.not_equal)
            prog[-1][2].append(("order", r, r + 1, False, 1))
        lin("NF", tw(FLIP[r] + 256), tw(FLIP[r]), -1.0, 1.0)
        act(V("CL", 0, m), ind(tw(FLIP[r], 512), V("BL", 0, 8) if r == 1 else V("BL", 64, 68)), scale=LEFT)
        tt(V("PROD", 512, 512 + m), ind(tw(t), par), V(bv, lf, lf + m), A.mult)
        w = PIECE["PR"]
        for a in range(0, 512, w):
            scan(V("SS", a, a + w), V("one", 0, w), V("PROD", a, a + w), V("SS", a - 1, a) if a else 0.0, A.mult, A.add)
        counted(V("PAY", 0, m), V("IDL", 0, m), V("CL", 0, m))
        tt(V("NUM", 0, m), ind(V("SS"), pos), V("PROD", 512, 512 + m), A.add)
        wrap("SOQ", 0, V("NUM", 0, m), "CPJ")
        listed(V("NL", 0, c), "SOQ", 0, m)
        cp(ind(V("BN%d" % r), V("NL", 0, c)), V("PAY", 0, m))

    send(0)
    book(0)
    lin("AL", V("AL", 0, 256), sxr(0, 256), 0.5, 128.375)
    lin("AL", V("AL", 256, 512), sxr(256), 0.5, 128.125)
    lin("RH", V("RH"), sxr(256), 1.0, 512.0)
    bits("DX", tt, V("DX"), sxr(256), V("RH"), A.subtract)
    act(lw(POSL), ind(V("DX"), V("PARL", 0, 16)), scale=1 / EPS, bias=512 / EPS - 256)
    lin("PARD", lw(PARN + 512), lw(PARN + 256))
    bits("SS", act, V("PE"), ind(lw(PARN + 256, 512), ordw))
    wrap("SOG", 0, V("PE"), apart=True)
    listed(V("BL", 24, 56), "SOG", 0, 512, 256)
    bits("SS", act, V("AI"), ind(V("AL"), V("EVL", 32, 64)))
    act(lw(AFL), ind(V("AL"), V("EVL", 16, 32)))
    bits("TG", tt, V("DT", 256, 512), ind(V("AL"), V("EVL", 32, 48)), V("AI", 256, 512), A.subtract)
    lin("NEG", V("DT", 0, 256), V("DT", 256, 512), -1.0)
    bits("SS", act, V("BV1", 128, 640), ind(V("DT"), ordw))
    act(lw(ALM + 128, 128), ind(lw(LG), V("JL", 8, 16)))
    counted(lw(ALM, 128), V("WB", 384, 512), lw(ALM + 128, 128))
    tt(V("BV1", 0, 128), ind(lw(AFL), V("JL", 8, 16)), lw(ALM, 128), A.subtract)
    act(lw(JTL, 128), ind(lw(AFL), V("JL", 8, 16)))
    update(0)
    relink(0)
    leaves(1)

    number(1)
    send(1)
    book(1)
    wrap("SOP", 0, V("AI"), apart=True)
    listed(V("AB2"), "SOP", 0, 512, -128)
    lin("SG1", tw(SG1), tw(TW1), -2.0, 1.0)
    stay = V("JL", 4, 8)
    for j, t in enumerate((JTL, ALM + 128)):
        act(V("LU", 64 * j, 64 * j + 64), ind(lw(t, 128), stay))
    wrap("SOR", 0, V("LU", 0, 64))
    listed(V("LM", 0, 4), "SOR", 0, 64, -128)
    cp(ind(V("ALV"), stay), V("one", 0, 64))
    scan(V("CNT", 1, 129), V("one", 0, 128), V("ALV"), 0.0, A.mult, A.add)
    cn = V("CNT", 0, 129)
    act(V("MR"), ind(cn, V("AB2", 16, 32)))
    tt(V("BLJ"), ind(cn, stay), V("LU", 64, 128), A.add)
    bits("TG", tt, V("DT", 0, 256), ind(cn, V("AB2", 0, 16)), V("MR"), A.subtract)
    bits("TG", tt, V("DT2", 256, 512), ind(tw(SG1), V("PARL", 16, 32)), V("DT", 0, 256), A.mult)
    tt(V("BV2", 512, 576), ind(cn, V("LM", 0, 4)), V("BLJ"), A.subtract)
    lin("NEG", V("DT2", 0, 256), V("DT2", 256, 512), -1.0)
    bits("SS", act, V("BVS", 0, 512), ind(V("DT2"), ordw))
    update(1)
    relink(1)
    leaves(2)
    tt(V("BVS", 512, 576), ind(tw(SG1), V("BL", 56, 60)), V("BV2", 512, 576), A.mult)

    number(2)
    send(2)
    book(2)
    update(2)

    w = PIECE["OUT"]
    for j, a in enumerate(range(0, 512, w)):
        quant("qx", "sx", a, a + w, V("xt", 4 * a, 4 * (a + w)))
        mm(V("pd", 512 * j, 512 * j + w), "qv", "sv", 0, "qx", "sx", a, a + w)
        if (a + w) % 256 == 0:
            dma("y", T.oc[:, 4 * (a + w) - 1024:4 * (a + w)], T.qx[:, a + w - 256:a + w].bitcast(dt.uint8), "outa", [V("qx", a + w - 256, a + w)[1]], [], 2.5)
        if a + w > 512 - w * YB_V:
            cp(V("yb", a, a + w), V("pd", 512 * j, 512 * j + w))
        else:
            act(V("yb", a, a + w), V("pd", 512 * j, 512 * j + w), f=AF.Copy)
        dma("s" if j % 2 else "y", T.y[:, a:a + w], T.yb[:, a:a + w], "outb" if j % 2 else "outa", [V("yb", a, a + w)[1]], [], 2.1 + w / 640)
    for k in range(4):
        dma("y", T.osc[4 * k:4 * k + 4, :], T.sx[32 * k:32 * k + 4, :], "outa", [V("sx")[1]], [], 1.9)
    relink(2)
    ts(tw(SGR), V("RESW", 256, 512), 0.0, A.is_gt, 768.0, A.mult)
    wrap("SOK", 0, tw(FLIP[2]))
    wrap("SOK", 256, tw(SGR), "CPJ")
    lin("KW", V("KW", 0, 16), ends("SOK", 0, 256), 256.0, ch(256))
    tt(V("KW", 32, 48), ends("SOK", 256, 256), V("KW", 0, 16), A.subtract)
    tt(V("KW", 48, 64), ends("SOK", 256, 256), V("KW", 0, 16), A.add)
    ts(V("KLL", 0, 16), V("KW", 32, 48), ch(1), A.add, 256.0, A.add)
    ts(V("KLL", 16, 32), V("KW", 48, 64), ch(1), A.add)
    act(V("KID"), ind(V("KIDS"), V("KLL")))
    klo = PLACE["KID"][1]
    dma("y", T.kid[:], T.f32[0:128:16, klo:klo + 512], "outa", [V("KID")[1]], [], 1.9)

    for i in schedule(prog):
        issue(*prog[i][:6])
    for s in ("v", "p", "g", "s", "outa", "outb"):
        need("y", s, cnt[s])
    need("g", "snt", cnt["snt"])
